import numpy as np, ml_dtypes
CORES = [2,6,10,14,18,22,26,30]
N = 8
import mx_ref
BF = ml_dtypes.bfloat16
def gcols(t, e):
    v = np.concatenate([t.reshape(8, 16, -1, 4), np.zeros((8, 16, 1, 4), BF)], axis=2)
    return np.ascontiguousarray(np.stack([v[g][:, e[g]] for g in range(8)])).reshape(128, -1)
def tile(rs):
    return np.stack(rs, axis=2).reshape(128, -1).astype(BF)
def pick(q, e):
    c = np.concatenate([q[0].reshape(128, -1, 4), np.zeros((128, 1, 4), np.uint8)], axis=1); s = np.concatenate([q[1], np.ones((16, 1), np.uint8)], axis=1)
    return (np.ascontiguousarray(c[:, e].reshape(128, -1)), np.ascontiguousarray(s[:, e]))
def join(*qs):
    return (np.concatenate([q[0] for q in qs], axis=1), np.concatenate([q[1] for q in qs], axis=1))
def put(q, e, v):
    c, s = q[0].reshape(128, -1, 4).copy(), q[1].copy(); c[:, e] = v[0].reshape(128, -1, 4); s[:, e] = v[1]
    return (c.reshape(128, -1), s)
def pk(c, s):
    return (np.ascontiguousarray(c), mx_ref.live(s))
def emit(q):
    return q[0], q[1]
def packed(v, rng):
    q = [mx_ref.quantize(np.ascontiguousarray(v[r])) for r in range(N)]
    return np.stack([a for a, b in q]), np.stack([mx_ref.plane(b, rng) for a, b in q])
def values_of_codes():
    e, c = np.zeros((128, 128, 4), np.float32), np.zeros((128, 2, 4), np.uint8)
    e[np.arange(128), np.arange(128), 0] = 1
    c[:127, :, 0] = np.arange(256).reshape(2, 128).T[:127]
    return mx_ref.matmul(mx_ref.quantize(e.reshape(128, 512).astype(BF)), (c.reshape(128, 8), np.full((16, 2), 127, np.uint8))).T.reshape(-1).astype(np.float64)
CODE_VALUE, SCALE_VALUE = values_of_codes(), 2.0 ** (np.arange(256) - 127.0)
def decode(q):
    return (CODE_VALUE[q[0]].reshape(16, 8, -1, 4) * SCALE_VALUE[q[1]][:, None, :, None] + 0.0).reshape(128, -1).astype(np.float32)
def f(rng, *shape):
    return mx_ref.flush((rng.standard_normal(shape, dtype=np.float32) * np.exp2(rng.integers(-2, 3, shape[:-1] + (1,)))).astype(BF))
def wide(rng, *shape, cols=0):
    v = rng.standard_normal(shape, dtype=np.float32) * np.exp2(rng.integers(-12, 13, shape)).astype(np.float32)
    if cols: v *= np.repeat(np.exp2(rng.integers(-cols, cols + 1, shape[:-2] + (1, shape[-1] // 4))) * (rng.random(shape[:-2] + (1, shape[-1] // 4)) > 0.0625), 4, axis=-1).astype(np.float32)
    return mx_ref.flush(v.astype(BF))
C, S, K, W, M, R = 288, 48, 6, 2, 2, 3
def big(v):
    v = v.astype(np.float32)
    v[np.abs(v) < np.float32(2.0 ** -16)] = 0
    return v.astype(BF)
def numbers_of(rng):
    return {"x": big(f(rng, N, 128, 4 * C)), "u": np.array(f(rng, N, 128, 512)), "v": np.array(f(rng, N, 128, 512))}
def layers(rng):
    return big(f(rng, N, 128, 2048)).reshape(N, 8, 16, 4, 8, 16, 4)
def weights(rng, w):
    c, p = packed(np.ascontiguousarray(w).reshape(N, 128, 2048), rng)
    return {"wc": c, "ws": p}
def bare(u):
    u = u.reshape(N, 128, 128, 4)
    u[:, :, ::16] = 0
    u[:, :, 1::16] = 0
    return u
def setup_inputs(rng):
    return {**numbers_of(rng), **weights(rng, layers(rng))}
def setup_inputs_ties(rng):
    d = numbers_of(rng)
    o = rng.permutation(N)
    x = d["x"].reshape(N, 8, 16, C, 4)
    x[:, :, :2] = 0
    x[:, :, :2, :, 0] = rng.integers(0, 3, (N, 8, 2, C)).astype(np.float32).astype(BF)
    u = bare(d["u"])
    for r in range(N):
        for h in range(0, 128, 16):
            u[r, h, h, 0] = 0.0 if r == o[0] else -1.0 if r == o[1] else 1.0
            u[r, h + 1, h + 1, 0] = u[r, h, h, 0]
    w = layers(rng)
    w[:, :, :, :, :, :2] = 0
    return {"x": x.reshape(N, 128, 4 * C), "u": u.reshape(N, 128, 512), "v": d["v"], **weights(rng, w)}
def setup_inputs_near(rng):
    d = numbers_of(rng)
    x = d["x"].astype(np.float32).reshape(N, 8, 16, C, 4)
    x[:, :, 0] = 0
    x[:, :, 8:] = 0
    u = bare(d["u"])
    s = rng.integers(0, 16, (N, 8, 2, C))
    s = ((s[..., None] >> np.arange(4)) & 1) * np.exp2(np.arange(4) - 23.0)
    h = rng.permutation(8)
    for i in range(8):
        g, k, p = h[i], i // 2, 16 * h[i]
        a = 1.0 if k == 0 else 2.0 ** -30
        if k == 2: x[:, g, 8:10, :, :i - 3] = (1.0 + 0.125 * rng.integers(0, 8, (N, 2, C, i - 3))) * 2.0 ** -30
        else: x[:, g, 8:10] = s[:, g]
        if k < 2:
            x[:, g, 0, :, 0] = 1.0 - 2.0 * (i % 2)
            x[:, g, 11, :, 0] = 2.0 ** -10
        if k == 3:
            for r in range(N): x[r, g, 0, rng.permutation(C)[:2], 0] = np.array([2.0 ** 29, -2.0 ** 29])
        for j in range(2):
            u[:, p + 8 + j, p + j] = a
            if i == 5:
                u[:, p + 8 + j, p + j, 0] = 1.125 * a
                u[:, p + 8 + j, p + j, 1] = -a
            if k < 2:
                u[:, p, p + j, 0] = a
                u[:, p + 11, p + j, 0] = a
            if k == 3: u[:, p, p + j, 0] = 1.0
    w = layers(rng)
    for i in [0, 8, 9, 10, 11, 12, 13, 14, 15]:
        w[:, :, i] = 0
        w[:, :, :, :, :, i] = 0
    return {"x": x.reshape(N, 128, 4 * C).astype(BF), "u": u.reshape(N, 128, 512), "v": d["v"], **weights(rng, w)}
def setup_inputs_huge(rng):
    d = numbers_of(rng)
    e = int(rng.integers(N))
    c = (np.argsort(rng.random((N, C)), axis=1) % 2 * 2.0 - 1.0).reshape(N, 1, 1, C, 1)
    c[e] = 1.0
    c[(e + 1) % N] = np.minimum(c[(e + 1) % N], 0.5)
    c[(e - 1) % N] = -1.0
    x = (1.0 - 0.0625 * rng.integers(0, 3, (N, 8, 16, C, 4))) * 2.0 ** 30 * c
    u = bare(d["u"])
    u[:, :, ::16] = (2.0 ** 30 * np.where(rng.random((N, 128, 8, 4)) < 0.25, 0.875, 1.0)).astype(np.float32).astype(BF)
    u[:, :, 1::16] = (2.0 ** 30 * np.where(rng.random((N, 128, 8, 4)) < 0.5, 0.25, 1.0)).astype(np.float32).astype(BF)
    w = np.zeros((N, 128, 4, 128, 4), np.float32)
    i = np.arange(128)
    for b in range(4): w[:, i, b, i, b] = -1
    return {"x": x.astype(np.float32).reshape(N, 128, 4 * C).astype(BF), "u": u.reshape(N, 128, 512), "v": d["v"], **weights(rng, w.astype(BF))}
def setup_inputs_held(rng):
    d = numbers_of(rng)
    x = d["x"].astype(np.float32).reshape(N, 8, 16, C, 4)
    t = (N, 8, 8, C, 4)
    x[:, :, :2] = 0
    x[:, :, 8:] = (1.0 + (2 * rng.integers(0, 64, t) + 1) * 2.0 ** -7) * np.exp2(-1.0 * rng.integers(8, 15, t)) * rng.choice([-1.0, 1.0], t)
    x[:, :, 8, :, 0] = 1.96875 * rng.choice([-1.0, 1.0], (N, 8, C))
    n = np.argsort(rng.random((N, 8, C)), axis=2)
    m = C - 1 - n
    x[:, :, 0, :, :3] = np.stack([m & 7, m & 56, m & 448], axis=-1)
    turn, at = rng.integers(0, 4, (8, S)), rng.integers(0, 2, (8, S))
    g = np.arange(8)[:, None]
    for r in range(N):
        k = n[r] // K
        x[r, :, 1, :, 0] = np.where(n[r] % K == at[g, k], np.array([8.0, 0.0, 2.0, 3.0])[(r + turn[g, k]) % 4], 0.0)
    u = bare(d["u"])
    for h in range(0, 128, 16):
        u[:, h, h, :3] = 1.0
        u[:, h + 1, h + 1, 0] = 1.0
    w = layers(rng)
    w[:, :, 0] = 0
    w[:, :, :, :, :, :2] = 0
    w[:, :, :, :, :, 8:] = 0
    return {"x": x.reshape(N, 128, 4 * C).astype(BF), "u": u.reshape(N, 128, 512), "v": d["v"], **weights(rng, w)}
def setup_inputs_spread(rng):
    d = setup_inputs(rng)
    d["x"] = big(wide(rng, N, 128, 4 * C, cols=6))
    return d
def check_inputs(d):
    b = []
    for k in ("x", "u", "v"):
        a = np.abs(d[k].astype(np.float32))
        if not (np.isfinite(a).all() and ((a == 0) | (a >= 2.0 ** -30) & (a <= 2.0 ** 30)).all()): b.append("a value of " + k)
    none, least, most = [emit(mx_ref.quantize(np.full((128, 16), k, np.float32).astype(BF)))[1][0, 0] for k in (0.0, 2.0 ** -30, 2.0 ** 30)]
    for r in range(N):
        if ((d["wc"][r] == 0x7F) | (d["wc"][r] == 0xFF)).any(): b.append("wc: a code that is no number")
        s = mx_ref.live(d["ws"][r])
        if ((s != none) & ((s < least) | (s > most))).any(): b.append("ws: a scale out of range")
    return b
def reference(x, u, v, wc, ws):
    qu = [mx_ref.quantize(u[r]) for r in range(N)]
    lay = [pk(wc[r], ws[r]) for r in range(N)]
    now = [x[r] for r in range(N)]
    held = np.full((N, 8, S, K), -1)
    cursor = np.zeros((N, 8, S), np.int64)
    kept = [np.zeros((128, 0), BF) for r in range(N)]
    item = np.arange(K)
    for t in range(R):
        score = [mx_ref.matmul(qu[r], mx_ref.quantize(now[r])) for r in range(N)]
        if t == 0: order = np.stack([np.argsort(-(score[r][::16] + np.float32(0.0)), axis=1, kind="stable") for r in range(N)])
        made = []
        for r in range(N):
            e = (r - 1) % N
            k = np.argsort(held[r] >= 0, axis=2, kind="stable")[:, :, :W]
            n = (K * np.arange(S)[:, None] + k).reshape(8, S * W)
            q = mx_ref.quantize(gcols(now[e], np.take_along_axis(order[e], n, axis=1)))
            kept[r] = np.concatenate([kept[r], decode(q).astype(BF)], axis=1)
            theirs = mx_ref.matmul(qu[r], q)[1::16]
            own = np.take_along_axis(score[r][1::16], np.take_along_axis(order[r], n, axis=1), axis=1)
            np.put_along_axis(held[r], k, np.where(theirs < own, -1, S * W * t + np.arange(S * W)).reshape(8, S, W), axis=2)
            lead = np.argmin(np.concatenate([held[r], np.full((8, S, 1), -1)], axis=2) >= 0, axis=2)
            end = np.minimum(cursor[r] + M, lead)
            goes = (item >= cursor[r][:, :, None]) & (item < end[:, :, None])
            cursor[r] = end
            where = np.zeros((8, C), np.int64)
            np.put_along_axis(where, order[r], np.where(goes, C + held[r], order[r].reshape(8, S, K)).reshape(8, C), axis=1)
            other = gcols(np.concatenate([now[r], kept[r]], axis=1), where)
            z = ((now[r].astype(np.float32) + other.astype(np.float32)) * np.float32(0.5)).astype(BF)
            qz = mx_ref.quantize(z)
            made.append(tile([mx_ref.matmul(pick(lay[r], np.arange(128 * b, 128 * b + 128)), qz) * np.float32(0.03125) + z[:, b::4].astype(np.float32) for b in range(4)]))
        now = made
    y, sk = np.zeros((N, 128, C), np.float32), np.zeros((N, 8, C), np.float32)
    oc, osc = np.zeros((N, 128, 4 * C), np.uint8), np.zeros((N, 16, C), np.uint8)
    for r in range(N):
        q = mx_ref.quantize(now[r])
        y[r] = mx_ref.matmul(mx_ref.quantize(v[r]), q)
        sk[r] = held[r].reshape(8, C)
        oc[r], osc[r] = emit(q)
    return {"y": y, "sk": sk, "oc": oc, "osc": osc}

@@ -1,0 +1,554 @@
+from concourse.mybir import dt, AluOpType as A, ActivationFunctionType as F
+
+C = 288
+BIG = 1.0e29
+K = 1024.0
+Q4, U8, BF, F32, U16, I32 = "float8_e4m3fn_x4", "uint8", "bfloat16", "float32", "uint16", "int32"
+
+
+def _sb(n, d):
+    return ("sbuf", [128, n], d)
+
+
+SCRATCH = {
+    "ub": _sb(512, BF), "vb": _sb(512, BF), "uq": _sb(128, Q4), "us": _sb(128, U8), "upq": _sb(256, Q4), "ups": _sb(256, U8),
+    "vq": _sb(128, Q4), "vs": _sb(128, U8), "wq": _sb(512, Q4), "wsc": _sb(512, U8),
+    "zw0": _sb(3200, BF), "zw1": _sb(3200, BF), "zw2": _sb(3200, BF), "xf": _sb(1152, BF),
+    "x32": _sb(1152, BF), "z32": _sb(1152, BF), "lq": _sb(576, Q4), "ls": _sb(576, U8),
+    "xq": _sb(C, Q4), "xs": _sb(C, U8), "zq": _sb(C, Q4), "zs": _sb(C, U8), "fq": _sb(C, Q4), "fs": _sb(C, U8),
+    "tt": _sb(512, BF), "tq": _sb(384, Q4), "ts": _sb(384, U8),
+    "zero": _sb(512, BF), "et": _sb(2048, BF), "eq": _sb(512, Q4), "es": _sb(512, U8),
+    "ot": _sb(512, BF), "oq": _sb(128, Q4), "osq": _sb(128, U8),
+    "bt": _sb(3840, BF), "bq": _sb(960, Q4), "bs": _sb(960, U8), "junk": _sb(2448, BF),
+    "pi": _sb(4, I32), "pb": _sb(4, I32), "col": _sb(16, F32), "upi": _sb(16, I32), "upl": _sb(16, U16),
+    "r16": _sb(C, F32), "e16": _sb(C, F32), "m16": _sb(C, F32), "d16": _sb(C, F32), "h0": _sb(C, BF),
+    "r4": _sb(96, F32), "e4": _sb(120, F32), "m4": _sb(96, F32), "d4": _sb(72, F32),
+    "mm": _sb(C, F32), "hh": _sb(C, F32), "rs": _sb(18, F32), "rc": _sb(18, F32), "ra": _sb(18, F32), "cx": _sb(C, F32),
+    "plu": _sb(18, U16), "ij": _sb(C, F32), "orep": _sb(C, F32), "ow": _sb(C, F32),
+    "ox": _sb(C, F32), "o16": _sb(18, U16), "lf": _sb(18, F32), "lu": _sb(18, U16),
+    "tl": _sb(72, U16), "jl": _sb(72, F32), "lb": _sb(72, U16), "jx": _sb(72, F32), "l16": _sb(18, U16),
+    "tg": _sb(72, F32), "xl": _sb(72, U16), "sl": _sb(72, U16), "sr": _sb(12, F32), "zo": _sb(24, F32), "zl": _sb(72, U16),
+    "s1": _sb(C, F32), "b4": _sb(1152, F32), "bm": _sb(96, F32), "ref": _sb(96, F32), "sc": _sb(128, F32), "dsc": _sb(96, F32),
+    "th": _sb(80, F32), "fl": _sb(240, BF), "fa": _sb(96, BF), "xc": _sb(384, BF), "dh": _sb(1152, BF), "val": _sb(384, BF),
+    "tu": _sb(192, F32), "su": _sb(384, F32), "t2": _sb(192, F32), "s2": _sb(192, F32), "tb": _sb(48, F32), "sb": _sb(48, F32),
+    "e2": _sb(16, F32), "tb1": _sb(12, F32), "tmp": _sb(24, F32), "ta": _sb(96, F32), "tm": _sb(96, F32), "tp": _sb(96, F32),
+    "tf": _sb(96, F32), "t1": _sb(48, F32), "ss": _sb(144, F32),
+    "arr": _sb(C, F32), "okr": _sb(96, F32), "okv": _sb(96, F32), "held": _sb(C, F32), "skb": _sb(C, F32), "yb": _sb(C, F32),
+    "ps": ("psum", [128, 4096], F32),
+}
+POOL = {"v": 40, "a": 30, "p": 16, "g": 20}
+NDMA = 24
+SEMAPHORES = (["%s%d" % (q, k) for q in POOL for k in range(POOL[q])] + ["d%d" % k for k in range(NDMA)]
+              + ["ta0", "ta1", "ta2", "fa0", "fa1", "left"])
+
+
+def R(name, a, b, s=1):
+    return (name, a, b, s)
+
+
+def bank(k, a=0, b=C):
+    return ("ps", 512 * k + a, 512 * k + b, 1)
+
+
+def bits(r):
+    if r[0] == "ps":
+        return 1 << (r[1] // 512)
+    m = 0
+    for c in range(r[1], r[2], r[3]):
+        m |= 1 << c
+    return m
+
+
+def emit(g, T, ops):
+    queue = {"v": g.vector, "a": g.scalar, "p": g.tensor, "g": g, "s": g.sync}
+    known_q = {q: 0 for q in queue}
+    before, done = {q: 0 for q in queue}, []
+    known, waits, wanted, seen = [], [], set(), {q: set() for q in queue}
+    for n, o in enumerate(ops):
+        deps = []
+        for k in range(n):
+            e = ops[k]
+            hit = False
+            for name, (rd, wr) in o["use"].items():
+                if name not in e["use"]:
+                    continue
+                erd, ewr = e["use"][name]
+                if name == "ps" and e["q"] != o["q"]:
+                    hit = hit or bool((rd | wr) & (erd | ewr))
+                elif name == "ps" and o["q"] == "p":
+                    hit = hit or (bool(wr & ewr) and not o["acc"])
+                else:
+                    hit = hit or bool(wr & (erd | ewr)) or bool(rd & ewr)
+            if hit:
+                deps.append(k)
+        have, mine = known_q[o["q"]], []
+        for k in reversed(deps):
+            if not have >> k & 1:
+                mine.append(k)
+                have |= known[k] | 1 << k
+                if not ops[k]["dma"]:
+                    have |= done[k]
+        known_q[o["q"]] = have
+        known.append(have)
+        done.append(before[o["q"]])
+        if not o["dma"]:
+            before[o["q"]] |= 1 << n | have
+        waits.append(mine)
+        wanted.update(mine)
+    sem, count, turn, ndma = {}, {}, {q: 0 for q in POOL}, 0
+    for n, o in enumerate(ops):
+        if o["dma"]:
+            sem[n] = ("d%d" % ndma, 16, 16)
+            ndma += 1
+        elif n in wanted:
+            name = "%s%d" % (o["q"], turn[o["q"]] % POOL[o["q"]])
+            turn[o["q"]] += 1
+            count[name] = count.get(name, 0) + 1
+            sem[n] = (name, count[name], 1)
+    for n, o in enumerate(ops):
+        q = queue[o["q"]]
+        for name, val in o["ext"]:
+            if name not in seen[o["q"]]:
+                seen[o["q"]].add(name)
+                q.wait_ge(T.sem[name], val)
+        for k in waits[n]:
+            q.wait_ge(T.sem[sem[k][0]], sem[k][1])
+        ins = o["fn"](q)
+        if n in sem:
+            ins.then_inc(T.sem[sem[n][0]], sem[n][2])
+    for n, o in enumerate(ops):
+        if o["dma"] and n not in wanted:
+            queue[o["q"]].wait_ge(T.sem[sem[n][0]], 16)
+
+
+def rank_program(g, core, T, topo):
+    rank = T.rank_of(core)
+    if rank is None:
+        return
+    n_ranks = len(T.cores)
+    nxt, prv = T.cores[(rank + 1) % n_ranks], T.cores[(rank - 1) % n_ranks]
+    common = set(topo.engines(T.cores[0], T.cores[1]))
+    for k in range(n_ranks):
+        common &= set(topo.engines(T.cores[k], T.cores[(k + 1) % n_ranks])) & set(topo.engines(T.cores[(k + 1) % n_ranks], T.cores[k]))
+    n_eng = len(common)
+    mask = sum(1 << e for e in common)
+    ops = []
+
+    def ap(r):
+        if len(r) == 2:
+            return ap(r[0]).indirect(ap(r[1]))
+        if r[3] == 1:
+            return T[r[0]][:, r[1]:r[2]]
+        return T[r[0]][:, r[1]:r[2]:r[3]]
+
+    def val(x):
+        return ap(x) if isinstance(x, tuple) else x
+
+    def op(q, fn, reads, writes, ext=(), dma=False, acc=False):
+        use = {}
+        for k, group in enumerate((reads, writes)):
+            for r in group:
+                if not isinstance(r, tuple):
+                    continue
+                parts = [(r, k)] if len(r) == 4 else [(r[0], k), (r[1], 0)]
+                for p, side in parts:
+                    u = use.setdefault(p[0], [0, 0])
+                    u[side] |= bits(p)
+        ops.append({"q": q, "fn": fn, "use": use, "ext": ext, "dma": dma, "acc": acc})
+
+    def tt(o, a, b, f, ext=()):
+        op("v", lambda q: q.tensor_tensor(ap(o), ap(a), ap(b), f), [a, b], [o], ext)
+
+    def ts(o, a, s1, f1, s2=None, f2=None):
+        if f2 is None:
+            op("v", lambda q: q.tensor_scalar(ap(o), ap(a), val(s1), None, f1), [a, s1], [o])
+        else:
+            op("v", lambda q: q.tensor_scalar(ap(o), ap(a), val(s1), val(s2), f1, f2), [a, s1, s2], [o])
+
+    def cp(o, a):
+        op("v", lambda q: q.tensor_copy(ap(o), ap(a)), [a], [o])
+
+    def fill(o, x):
+        op("v", lambda q: q.memset(ap(o), x), [], [o])
+
+    def scan(o, d0, d1, init, f0, f1, ext=()):
+        op("v", lambda q: q.tensor_tensor_scan(ap(o), ap(d0), ap(d1), init, f0, f1), [d0, d1], [o], ext)
+
+    def horner(o, flags, table, ext=()):
+        scan(o, flags, table, 0.0, A.mult, A.add, ext)
+
+    def pick_own(o, src, d):
+        scan(o, src, d, -K, A.max, A.add)
+
+    def quant(oq, osc, a):
+        op("v", lambda q: q.quantize_mx(ap(oq), ap(osc), ap(a)), [a], [oq, osc])
+
+    def act(o, a, scale=1.0, bias=None, accum=None):
+        if accum is not None:
+            op("a", lambda q: q.activation(ap(o), ap(a), F.Copy, accum_out=ap(accum)), [a], [o, accum])
+        elif bias is not None:
+            op("a", lambda q: q.activation(ap(o), ap(a), F.Identity, bias=val(bias), scale=scale), [a, bias], [o])
+        elif scale == 1.0:
+            op("a", lambda q: q.activation(ap(o), ap(a), F.Copy), [a], [o])
+        else:
+            op("a", lambda q: q.activation(ap(o), ap(a), F.Copy, scale=scale), [a], [o])
+
+    def mm(o, wq, wsc, xq, xsc, start=True, stop=True, ext=()):
+        op("p", lambda q: q.matmul_mx(ap(o), ap(wq), ap(wsc), ap(xq), ap(xsc), start, stop), [wq, wsc, xq, xsc], [o], ext, acc=not start)
+
+    def iota(o, pattern, base, cm=0):
+        if SCRATCH[o[0]][2] == I32:
+            op("g", lambda q: q.iota(ap(o), pattern, base, cm), [], [o])
+        else:
+            op("g", lambda q: q.iota(ap(o), pattern, base, cm, allow_small_or_imprecise_dtypes=True), [], [o])
+
+    def const(o, x):
+        iota(o, [[0, len(range(o[1], o[2], o[3]))]], x)
+
+    def sel(o, a, pattern, f, fill_with, base, cm):
+        op("g", lambda q: q.affine_select(ap(o), ap(a), pattern, f, fill_with, base, cm), [a], [o])
+
+    def dma(queue, o, a, reads, writes):
+        op(queue, lambda q: q.dma_start(o(), a()), reads, writes, dma=True)
+
+    def send(to, o, a, sem, codes=False):
+        rid, pid, _ = topo.addr(to)
+        if codes:
+            op("g", lambda q: q.remote_dma(ap(o).bitcast(dt.uint8), ap(a).bitcast(dt.uint8), T.sem[sem], T.sem.left, pid, rid, mask), [a], [])
+        else:
+            op("g", lambda q: q.remote_dma(ap(o), ap(a), T.sem[sem], T.sem.left, pid, rid, mask), [a], [])
+
+    def col(k):
+        return R("col", k, k + 1)
+
+    zw = ["zw0", "zw1", "zw2", "xf"]
+
+    dma("a", lambda: T.ub[:], lambda: T.u[:], [], [R("ub", 0, 512)])
+    dma("s", lambda: T.zw0[:, 0:1152], lambda: T.x[:], [], [R("zw0", 0, 1152)])
+
+    iota(R("pi", 0, 1), [[0, 1]], 0, 1)
+    iota(R("upi", 0, 16), [[1, 2], [16, 8]], 0)
+    iota(R("r16", 0, C), [[0, 18], [1, 16]], 0)
+    iota(R("rc", 0, 18), [[16, 18]], -303)
+    fill(R("zero", 0, 512), 0.0)
+    for b in range(4):
+        dma("s", lambda b=b: T.et[:, 512 * b:512 * b + 512], lambda: T.zero[:], [R("zero", 0, 512), R("zw0", 0, 1)],
+            [R("et", 512 * b, 512 * b + 512)])
+    dma("s", lambda: T.wq[:].bitcast(dt.uint8), lambda: T.wc[:], [], [R("wq", 0, 512)])
+    dma("s", lambda: T.wsc[:], lambda: T.ws[:], [], [R("wsc", 0, 512)])
+    dma("s", lambda: T.vb[:], lambda: T.v[:], [], [R("vb", 0, 512)])
+    fill(R("h0", 0, C), BIG)
+    ts(R("pb", 0, 1), R("pi", 0, 1), 15, A.bitwise_and)
+    ts(R("pb", 1, 2), R("pi", 0, 1), 2, A.arith_shift_right, 3, A.bitwise_and)
+    ts(R("pb", 2, 3), R("pi", 0, 1), 3, A.bitwise_and)
+    cp(R("upl", 0, 16), R("upi", 0, 16))
+    fill(R("h0", 0, C, 16), -BIG)
+    cp(R("col", 0, 3), R("pb", 0, 3))
+    tiles, at = [], 0
+    for blocks in ([None, 17, 16, 15], [14, 13, 12, 11], [10, 9, 8, 7], [6, 5, 4, 3], [2, 1, 0]):
+        w = max(128, 16 * max(c for c in blocks if c is not None) + 16)
+        low = 16 * blocks[-1] + 16 if len(blocks) == 4 else 0
+        tiles.append((at, w, blocks))
+        fill(R("bt", 4 * (at + low), 4 * (at + w)), 1.0 if len(tiles) == 2 else 0.0)
+        at += w
+    ts(R("e16", 0, C), R("r16", 0, C), col(0), A.is_equal, 0.5, A.subtract)
+    sel(R("ot", 0, 512), R("zero", 0, 512), [[-16, 8], [0, 64]], A.is_ge, 1.0, -16, 1)
+    sel(R("ot", 0, 512), R("ot", 0, 512), [[-16, 8], [0, 64]], A.is_ge, 0.0, 0, 1)
+    iota(R("r4", 0, 96), [[0, 24], [1, 4]], 0)
+    iota(R("ij", 0, C), [[1, C]], 0)
+    act(R("m16", 0, C), R("e16", 0, C), scale=2 * BIG)
+    quant(R("uq", 0, 128), R("us", 0, 128), R("ub", 0, 512))
+
+    def pick_u(k):
+        op("v", lambda q: q.tensor_copy(T.upq[:, 128 * k:128 * k + 128].bitcast(dt.uint32),
+                                        T.uq[:, 0:128].bitcast(dt.uint32).indirect(T.upl[:, 8 * k:8 * k + 8])),
+           [R("uq", 0, 128), R("upl", 0, 16)], [R("upq", 128 * k, 128 * k + 128)])
+        act(R("ups", 128 * k, 128 * k + 128), (R("us", 0, 128), R("upl", 8 * k, 8 * k + 8)))
+
+    pick_u(0)
+    u0, u1 = (R("upq", 0, 128), R("ups", 0, 128)), (R("upq", 128, 256), R("ups", 128, 256))
+
+    quant(R("lq", 0, C), R("ls", 0, C), R("zw0", 0, 1152))
+    mm(bank(0), u0[0], u0[1], R("lq", 0, C), R("ls", 0, C))
+    mm(bank(3), u0[0], u0[1], R("lq", 0, C), R("ls", 0, C))
+    pick_u(1)
+    mm(bank(1), u1[0], u1[1], R("lq", 0, C), R("ls", 0, C))
+    act(R("col", 3, 6), R("col", 0, 3), scale=-K, bias=-3 * K)
+    act(R("d16", 0, C), R("e16", 0, C), scale=18 * K, bias=8 * K)
+    act(R("rs", 0, 1), R("zero", 0, 1))
+    act(R("d16", 15, C, 16), R("d16", 15, C, 16), bias=col(3))
+    act(col(6), col(2), bias=4 * K)
+    act(col(7), R("d16", 15, 16))
+    act(R("ra", 0, 18), R("rc", 0, 18), bias=R("d16", 15, 16))
+    tt(R("mm", 0, C), bank(0), R("m16", 0, C), A.min)
+    scan(R("hh", 0, C), R("h0", 0, C), R("mm", 0, C), -BIG, A.min, A.max)
+    quant(R("oq", 0, 128), R("osq", 0, 128), R("ot", 0, 512))
+
+    def slot(n, t, w):
+        return R("bt", 4 * tiles[n][0] + t, 4 * (tiles[n][0] + w), 4)
+
+    def own_score(c):
+        return R("hh", 16 * c + 15, 16 * c + 16)
+
+    def row_sum(n, t):
+        c = tiles[n][2][t]
+        if c:
+            act(R("junk", 8 * c * (c - 1), 8 * c * (c + 1)), slot(n, t, 16 * c), accum=R("rs", c, c + 1))
+
+    def compare(n, t):
+        c = tiles[n][2][t]
+        ts(slot(n, t, 16 * c + 16), bank(0, 0, 16 * c + 16), own_score(c), A.is_ge)
+        row_sum(n, t)
+
+    def column_sums(n):
+        at, w = tiles[n][:2]
+        quant(R("bq", at, at + w), R("bs", at, at + w), R("bt", 4 * at, 4 * (at + w)))
+        mm(bank(2, 0, w), R("oq", 0, 128), R("osq", 0, 128), R("bq", at, at + w), R("bs", at, at + w), n == 0, n == 4)
+
+    for t, c in enumerate(tiles[1][2]):
+        act(slot(1, t, 16 * c + 16), bank(3, 0, 16 * c + 16), scale=-1.0, bias=own_score(c))
+    for t in range(1, 4):
+        compare(0, t)
+    tt(slot(0, 0, C), bank(0), R("hh", 0, C), A.not_equal)
+    whole = R("bt", 4 * tiles[1][0], 4 * tiles[2][0])
+    ts(whole, whole, 0.0, A.is_le)
+    for t in range(4):
+        row_sum(1, t)
+    column_sums(0)
+    column_sums(1)
+    for n in range(2, 5):
+        for t in range(len(tiles[n][2])):
+            compare(n, t)
+            if t == 0 and n > 2:
+                column_sums(n - 1)
+    ts(R("e4", 0, 96), R("r4", 0, 96), col(1), A.is_equal, 0.5, A.subtract)
+    column_sums(4)
+    ts(R("e4", 96, 120), R("r4", 0, 24), col(2), A.is_equal, 0.5, A.subtract)
+    const(R("dsc", 0, 96), 1)
+    const(R("th", 0, 32), 1)
+    const(R("dsc", 0, 96, 8), 0)
+    const(R("dsc", 4, 96, 8), 2)
+    iota(R("th", 32, 80), [[0, 12], [-1, 4]], 4)
+    iota(R("lf", 0, 2), [[64, 2]], 3)
+    iota(R("lf", 2, 6), [[32, 4]], 7)
+    iota(R("lf", 6, 12), [[0, 2], [4, 3]], 0)
+    iota(R("lf", 12, 18), [[16, 6]], 0)
+    iota(R("sr", 0, 12), [[32, 12]], 0)
+    for b in range(4):
+        sel(R("et", 512 * b + b, 512 * b + 512, 4), R("zero", 0, 128), [[-1, 128]], A.not_equal, 0.5, 0, 1)
+    act(R("d4", 0, 48), R("e4", 0, 48), scale=6 * K, bias=2 * K)
+    act(R("tt", 384, 512), R("zero", 0, 128))
+    act(R("d4", 3, 48, 4), R("d4", 3, 48, 4), bias=col(4))
+    tt(R("d16", 15, C, 16), R("ra", 0, 18), R("rs", 0, 18), A.subtract)
+    pick_own(R("cx", 0, C), bank(2), R("d16", 0, C))
+    ts(R("plu", 0, 18), R("cx", 15, C, 16), -1.0, A.mult, -K, A.add)
+    cp((R("orep", 0, C), R("plu", 0, 18)), R("ij", 0, C))
+    for k in range(2):
+        pick_own(R("ow", 48 * k, 48 * k + 48), R("orep", k, C, 6), R("d4", 0, 48))
+    for k in range(2):
+        ts(R("tl", k, 24, 2), R("ow", 48 * k + 3, 48 * k + 48, 4), 4.0, A.mult, col(6), A.add)
+    act(R("s1", 0, C), bank(1))
+    act(R("d16", 15, C, 16), R("zero", 0, 18), bias=col(7))
+    act(R("m4", 0, 96), R("e4", 0, 96), scale=2 * BIG)
+    act(R("d4", 48, 72), R("e4", 96, 120), scale=6 * K, bias=2 * K)
+    act(col(8), col(2), scale=1.0 / 2048, bias=2.0)
+    act(col(9), col(0), scale=4.0)
+    act(col(10), col(1), scale=8.0)
+    act(col(11), col(2), scale=4.0, bias=col(1))
+    act(R("d4", 51, 72, 4), R("d4", 51, 72, 4), bias=col(5))
+    act(R("lf", 0, 2), R("lf", 0, 2), bias=col(9))
+    act(R("lf", 2, 5), R("lf", 2, 5), bias=col(10))
+    act(R("lf", 6, 12), R("lf", 6, 12), bias=col(1))
+    act(R("lf", 12, 18), R("lf", 12, 18), bias=col(11))
+
+    def ow(k, n=1):
+        return R("ow", 48 * k + 3, 48 * (k + n), 4)
+
+    def su(k, role, n=1):
+        a = 96 * k + 48 * role
+        return R("su", a + 3, a + 48 * n, 4)
+
+    def receipts_out(r, part):
+        if part == 0:
+            pick_own(R("jx", 24 * r, 24 * r + 24), R("jl", 24 * r, 24 * r + 24), R("d4", 48, 72))
+            tt(R("okr", 0, 96), bank(3, 32, 128), R("b4", 384 * r, 384 * r + 384, 4), A.is_ge)
+            ts(R("l16", 6 * r, 6 * r + 6), R("jx", 24 * r + 3, 24 * r + 24, 4), K, A.add)
+            tt(R("okv", 0, 96), (R("okr", 0, 96), R("lu", 12, 18)), R("arr", 96 * r, 96 * r + 96), A.mult)
+        else:
+            cp((R("held", 0, C), R("l16", 6 * r, 6 * r + 6)), R("okv", 0, 96))
+
+    for r in range(3):
+        z, o24 = zw[r], 24 * r
+        own = R("fl", 80 * (r - 1) + 32, 80 * (r - 1) + 80)
+        came = R("fa", 48 * (r - 1), 48 * r)
+        if r == 0:
+            cp(R("tt", 0, 224), (R(z, 0, 1152), R("tl", 0, 14)))
+            act(R("tt", 224, 384), (R(z, 0, 1152), R("tl", 14, 24)))
+        else:
+            ts(R("tt", 0, 224), (R("x32", 0, 1152), R("tl", o24, o24 + 14)), 2.0 ** -5, A.mult)
+            act(R("tt", 224, 384), (R("x32", 0, 1152), R("tl", o24 + 14, o24 + 24)), scale=2.0 ** -5)
+            act(R(z, 2, 1152, 4), R("x32", 2, 1152, 4), scale=2.0 ** -5)
+        quant(R("tq", 128 * r, 128 * r + 128), R("ts", 128 * r, 128 * r + 128), R("tt", 0, 512))
+        land = C + 96 * r
+        send(nxt, R("lq", land, land + 96), R("tq", 128 * r, 128 * r + 96), "ta%d" % r, codes=True)
+        send(nxt, R("ls", land, land + 96), R("ts", 128 * r, 128 * r + 96), "ta%d" % r)
+        e2 = R("e2", 0, 12)
+        name, step = (("ow", 48), ("su", 96), ("s2", 96))[r]
+        first = [R(name, step * k + 3, step * k + 48, 4) for k in range(2)]
+
+        def targets(second):
+            for k, src in enumerate((first[0], second)):
+                ts(R("tg", o24 + k, o24 + 24, 2), src, 1.0 / 512, A.mult, col(8), A.add)
+            if r:
+                ts(R("xl", o24, o24 + 24), R("tg", o24, o24 + 24), 2048.0, A.mult)
+                act(R("xc", 0, 384), (R("x32", 0, 1152), R("xl", o24, o24 + 24)), scale=2.0 ** -6)
+
+        if r:
+            ts(R(z, 3, 1152, 4), R("x32", 3, 1152, 4), 2.0 ** -5, A.mult)
+            horner(R(name, 0, 48), own, R("tu" if r == 1 else "t2", 0, 48))
+            quant(R("xq", 0, C), R("xs", 0, C), R(z, 0, 1152))
+            mm(bank(1), u1[0], u1[1], R("xq", 0, C), R("xs", 0, C))
+            act(R("s1", 0, C), bank(1))
+            horner(R(name, 96, 144), own, R("tu", 48, 96) if r == 1 else R("t2", 96, 144))
+        for k in range(2):
+            ts(R("lb", o24 + k, o24 + 24, 2), first[k], K, A.add)
+        if r == 0:
+            act(R("tu", 0, 192), R("zero", 0, 192))
+        act(R("b4", 384 * r, 384 * r + 384), (R("s1", 0, C), R("lb", o24, o24 + 24)))
+        if r == 0:
+            act(R("xc", 0, 384), R("tt", 0, 384), scale=0.5)
+            act(R("sc", 96, 128), R("zero", 0, 32))
+            act(R("sr", 0, 12), R("sr", 0, 12), bias=col(0))
+            quant(R("eq", 0, 512), R("es", 0, 512), R("et", 0, 2048))
+            targets(first[1])
+            cp(R("lu", 0, 18), R("lf", 0, 18))
+            for k in range(2, 6):
+                pick_own(R("ow", 48 * k, 48 * k + 48), R("orep", k, C, 6), R("d4", 0, 48))
+            tt(R("tu", 1, 48, 4), ow(0), ow(1), A.subtract)
+            tt(R("tu", 48, 192, 4), ow(1, 3), ow(2, 3), A.subtract)
+            cp(R("tu", 3, 192, 4), ow(2, 4))
+            tt(R("tu", 2, 192, 4), ow(1, 4), ow(2, 4), A.subtract)
+            iota(R("arr", 0, 96, 2), [[16, 6], [2, 4], [8, 2]], 1)
+            iota(R("arr", 1, 96, 2), [[16, 6], [2, 4], [8, 2]], 2)
+            const(R("t1", 0, 48, 4), 384)
+            const(R("t1", 1, 48, 4), -384)
+            const(R("t1", 2, 48, 4), 0)
+        elif r == 1:
+            tt(e2, R("fl", 34, 80, 4), R("fl", 33, 80, 4), A.subtract)
+            horner(R("ss", 0, 48), own, R("t1", 0, 48))
+            tt(R("tmp", 0, 12), e2, R("tu", 2, 48, 4), A.mult)
+            cp(R("sl", 25, 48, 2), R("ss", 3, 48, 4))
+            tt(R("tb1", 0, 12), R("tmp", 0, 12), su(1, 0), A.add)
+            ts(R("th", 1, 24, 2), e2, 1.0, A.add)
+            targets(R("tb1", 0, 12))
+            for k in range(2, 4):
+                horner(R("su", 96 * k, 96 * k + 48), own, R("tu", 48 * k, 48 * k + 48))
+                horner(R("su", 96 * k + 48, 96 * k + 96), came, R("tu", 48 * k, 48 * k + 48))
+            tt(R("t2", 1, 96, 4), su(0, 0, 2), su(1, 0, 2), A.subtract)
+            tt(R("t2", 96, 192, 4), su(1, 0, 2), su(2, 0, 2), A.subtract)
+            tt(R("t2", 2, 192, 4), su(1, 0, 4), su(2, 0, 4), A.subtract)
+        else:
+            tt(R("tmp", 12, 24), su(1, 0), su(3, 0), A.subtract)
+            tt(R("tb", 1, 48, 4), R("tb1", 0, 12), su(2, 0), A.subtract)
+            tt(R("tmp", 12, 24), R("tmp", 12, 24), e2, A.mult)
+            tt(R("tp", 0, 96), (R("e2", 0, 12), R("lu", 6, 12)), R("tm", 0, 96), A.mult)
+            tt(R("tb", 3, 48, 4), R("tmp", 12, 24), su(3, 0), A.add)
+            tt(R("tf", 0, 96), R("tp", 0, 96), R("ta", 0, 96), A.add)
+            tt(R("tb", 2, 48, 4), su(2, 0), R("tb", 3, 48, 4), A.subtract)
+            horner(R("ss", 48, 96), own, R("tf", 0, 48))
+            horner(R("sb", 0, 48), own, R("tb", 0, 48))
+            horner(R("ss", 96, 144), own, R("tf", 48, 96))
+            targets(R("sb", 3, 48, 4))
+            cp(R("th", 1, 24, 2), R("ss", 51, 96, 4))
+            cp(R("sl", 49, 72, 2), R("ss", 99, 144, 4))
+        if r:
+            receipts_out(r - 1, 1)
+        tt(R("bm", 0, 96), R("b4", 384 * r, 384 * r + 384, 4), R("m4", 0, 96), A.min)
+        if r == 0:
+            pick_own(R("ox", 0, C), R("orep", 0, C), R("d16", 0, C))
+            quant(R("vq", 0, 128), R("vs", 0, 128), R("vb", 0, 512))
+            ts(R("o16", 0, 18), R("ox", 15, C, 16), K, A.add)
+            ts(R("sl", 24, 48, 2), R("sr", 0, 12), 384.0, A.add)
+            ts(R("sl", 48, 72, 2), R("sr", 0, 12), 768.0, A.add)
+        arrived = (("ta%d" % r, 2 * n_eng),)
+        tq, tsc = R("lq", land - 32, land + 96), R("ls", land - 32, land + 96)
+        mm(bank(3, 0, 128), u1[0], u1[1], tq, tsc, ext=arrived)
+        for b in range(4):
+            mm(bank(4 + b, 0, 128), R("eq", 128 * b, 128 * b + 128), R("es", 128 * b, 128 * b + 128), tq, tsc, ext=arrived)
+            if r:
+                act(R("dh", 384 * r + b, 384 * r + 384, 4), bank(4 + b, 32, 128))
+        tt(R("ref", 0, 96), bank(3, 32, 128), R("bm", 0, 96), A.is_lt)
+        horner(R("sc", 0, 96), R("dsc", 0, 96), R("ref", 0, 96))
+        if r < 2:
+            tt(R("fl", 80 * r, 80 * r + 80), (R("sc", 0, 128), R("lu", 0, 5)), R("th", 0, 80), A.is_ge)
+            send(prv, R("fa", 48 * r, 48 * r + 48), R("fl", 80 * r + 32, 80 * r + 80), "fa%d" % r)
+        else:
+            tt(R("fl", 160, 184), R("sc", 3, 96, 4), R("th", 0, 24), A.is_ge)
+        if r == 0:
+            for b in range(2):
+                tt(R("val", b, 384, 4), bank(4 + b, 32, 128), R("xc", b, 384, 4), A.add)
+        tt(R("zo", 0, 24), R("fl", 80 * r, 80 * r + 24), R("tg", o24, o24 + 24), A.add)
+        if r == 0:
+            for b in range(2, 4):
+                tt(R("val", b, 384, 4), bank(4 + b, 32, 128), R("xc", b, 384, 4), A.add)
+        ts(R("zl", o24, o24 + 24), R("zo", 0, 24), 2048.0, A.mult)
+        if r == 0:
+            for b in range(4):
+                act(R("dh", b, 384, 4), bank(4 + b, 32, 128))
+            for k, x in enumerate((-1, 1, 0, 1)):
+                const(R("ta", k, 48, 4), x)
+            const(R("tm", 48, 96), -384)
+            for k, x in enumerate((1, 0, -3, 3)):
+                const(R("tm", k, 48, 4), x)
+            const(R("tm", 50, 96, 4), 384)
+        else:
+            tt(R("val", 0, 384), (R("dh", 0, 384 * r + 384), R("sl", o24, o24 + 24)), R("xc", 0, 384), A.add)
+        for k in range(2):
+            act(R("jl", o24 + k, o24 + 24, 2), first[k], bias=K)
+        if r == 0:
+            act(R("held", 0, C), R("zero", 0, C))
+            act(R("t2", 0, 192), R("zero", 0, 192))
+            act(R("tb", 0, 48, 4), R("zero", 0, 12))
+            act(R("t1", 3, 48, 4), R("sr", 0, 12), bias=400.0)
+            act(R("arr", 96, 192), R("arr", 0, 96), bias=96.0)
+            act(R("arr", 192, 288), R("arr", 0, 96), bias=192.0)
+        if r == 1:
+            act(R("t2", 3, 192, 4), su(2, 0, 4))
+            act(R("ta", 48, 96), R("t1", 0, 48))
+            act(R("ta", 51, 96, 4), R("sr", 0, 12), bias=784.0)
+        cp((R(z, 0, 3200), R("zl", o24, o24 + 24)), R("val", 0, 384))
+        quant(R("zq", 0, C), R("zs", 0, C), R(z, 0, 1152))
+        for b in range(4):
+            act(R("z32", C * b, C * b + C), R(z, b, 1152, 4), scale=32.0)
+            mm(bank(4 + b), R("wq", 128 * b, 128 * b + 128), R("wsc", 128 * b, 128 * b + 128), R("zq", 0, C), R("zs", 0, C))
+        receipts_out(r, 0)
+        for b in range(4):
+            tt(R("x32", b, 1152, 4), bank(4 + b), R("z32", C * b, C * b + C), A.add)
+            if b < 2 or (b == 2 and r == 2):
+                act(R(zw[r + 1], b, 1152, 4), R("x32", b, 1152, 4), scale=2.0 ** -5)
+            if r < 2 and b == 2:
+                got, back = R("fa", 48 * r, 48 * r + 48), (("fa%d" % r, n_eng),)
+                for k in range(2):
+                    if r == 0:
+                        horner(R("su", 96 * k + 48, 96 * k + 96), got, R("tu", 48 * k, 48 * k + 48), back)
+                    else:
+                        horner(R("s2", 96 * k + 48, 96 * k + 96), got, R("t2", 96 * k + 48, 96 * k + 96), back)
+                for k in range(2):
+                    ts(R("tl", o24 + 24 + k, o24 + 48, 2), R("su" if r == 0 else "s2", 96 * k + 51, 96 * k + 96, 4), 4.0, A.mult, col(6), A.add)
+
+    ts(R("xf", 3, 1152, 4), R("x32", 3, 1152, 4), 2.0 ** -5, A.mult)
+    for h in range(2):
+        a, b = 144 * h, 144 * h + 144
+        quant(R("fq", a, b), R("fs", a, b), R("xf", 4 * a, 4 * b))
+        mm(bank(h, 0, 144), R("vq", 0, 128), R("vs", 0, 128), R("fq", a, b), R("fs", a, b))
+        act(R("yb", a, b), bank(h, 0, 144))
+    dma("a", lambda: T.y[:], lambda: T.yb[:], [R("yb", 0, C)], [])
+    dma("s", lambda: T.oc[:], lambda: T.fq[:].bitcast(dt.uint8), [R("fq", 0, C)], [])
+    for k in range(4):
+        dma("s" if k < 3 else "a", lambda k=k: T.osc[4 * k:4 * k + 4, :], lambda k=k: T.fs[32 * k:32 * k + 4, :], [R("fs", 0, C)], [])
+    receipts_out(2, 1)
+    ts(R("skb", 0, C), (R("held", 0, C), R("o16", 0, 18)), -1.0, A.add)
+    dma("a", lambda: T.sk[:], lambda: T.skb[0:128:16, :], [R("skb", 0, C)], [])
+
+    emit(g, T, ops)
+    g.wait_ge(T.sem.left, 8 * n_eng)

@@ -1,7 +1,9 @@
 from concourse.mybir import dt, AluOpType as A, ActivationFunctionType as F
 
 C = 288
+H = 144
 BIG = 1.0e29
+TINY = 2.0 ** -100
 K = 1024.0
 Q4, U8, BF, F32, U16, I32 = "float8_e4m3fn_x4", "uint8", "bfloat16", "float32", "uint16", "int32"
 
@@ -17,29 +19,30 @@ SCRATCH = {
     "x32": _sb(1152, BF), "z32": _sb(1152, BF), "lq": _sb(576, Q4), "ls": _sb(576, U8),
     "xq": _sb(C, Q4), "xs": _sb(C, U8), "zq": _sb(C, Q4), "zs": _sb(C, U8), "fq": _sb(C, Q4), "fs": _sb(C, U8),
     "tt": _sb(512, BF), "tq": _sb(384, Q4), "ts": _sb(384, U8),
-    "zero": _sb(512, BF), "et": _sb(2048, BF), "eq": _sb(512, Q4), "es": _sb(512, U8),
-    "ot": _sb(512, BF), "oq": _sb(128, Q4), "osq": _sb(128, U8),
+    "zero": _sb(512, BF), "et": _sb(516, BF), "eq": _sb(512, Q4), "es": _sb(512, U8),
+    "og": _sb(128, BF), "ot": _sb(512, BF), "oq": _sb(128, Q4), "osq": _sb(128, U8),
     "bt": _sb(3840, BF), "bq": _sb(960, Q4), "bs": _sb(960, U8), "junk": _sb(2448, BF),
-    "pi": _sb(4, I32), "pb": _sb(4, I32), "col": _sb(16, F32), "upi": _sb(16, I32), "upl": _sb(16, U16),
-    "r16": _sb(C, F32), "e16": _sb(C, F32), "m16": _sb(C, F32), "d16": _sb(C, F32), "h0": _sb(C, BF),
-    "r4": _sb(96, F32), "e4": _sb(120, F32), "m4": _sb(96, F32), "d4": _sb(72, F32),
+    "pi": _sb(4, I32), "pb": _sb(4, I32), "col": _sb(16, F32), "upi": _sb(16, I32), "upl": _sb(26, U16),
+    "ucq": _sb(16, Q4), "ucs": _sb(16, U8), "unq": _sb(16, Q4), "uns": _sb(16, U8), "upn": _sb(128, Q4), "usn": _sb(128, U8),
+    "hb": _sb(96, F32), "bo": _sb(16, F32), "bn": _sb(16, F32), "rf": _sb(6, F32), "ms": _sb(6, F32), "d6": _sb(6, F32),
+    "r16": _sb(C, F32), "e16": _sb(C, F32), "m16": _sb(C, F32), "d16": _sb(C, F32), "h0": _sb(C, BF), "d1": _sb(48, F32),
     "mm": _sb(C, F32), "hh": _sb(C, F32), "rs": _sb(18, F32), "rc": _sb(18, F32), "ra": _sb(18, F32), "cx": _sb(C, F32),
     "plu": _sb(18, U16), "ij": _sb(C, F32), "orep": _sb(C, F32), "ow": _sb(C, F32),
-    "ox": _sb(C, F32), "o16": _sb(18, U16), "lf": _sb(18, F32), "lu": _sb(18, U16),
-    "tl": _sb(72, U16), "jl": _sb(72, F32), "lb": _sb(72, U16), "jx": _sb(72, F32), "l16": _sb(18, U16),
-    "tg": _sb(72, F32), "xl": _sb(72, U16), "sl": _sb(72, U16), "sr": _sb(12, F32), "zo": _sb(24, F32), "zl": _sb(72, U16),
-    "s1": _sb(C, F32), "b4": _sb(1152, F32), "bm": _sb(96, F32), "ref": _sb(96, F32), "sc": _sb(128, F32), "dsc": _sb(96, F32),
-    "th": _sb(80, F32), "fl": _sb(240, BF), "fa": _sb(96, BF), "xc": _sb(384, BF), "dh": _sb(1152, BF), "val": _sb(384, BF),
-    "tu": _sb(192, F32), "su": _sb(384, F32), "t2": _sb(192, F32), "s2": _sb(192, F32), "tb": _sb(48, F32), "sb": _sb(48, F32),
-    "e2": _sb(16, F32), "tb1": _sb(12, F32), "tmp": _sb(24, F32), "ta": _sb(96, F32), "tm": _sb(96, F32), "tp": _sb(96, F32),
-    "tf": _sb(96, F32), "t1": _sb(48, F32), "ss": _sb(144, F32),
-    "arr": _sb(C, F32), "okr": _sb(96, F32), "okv": _sb(96, F32), "held": _sb(C, F32), "skb": _sb(C, F32), "yb": _sb(C, F32),
+    "lf": _sb(544, F32), "lx": _sb(544, F32), "lu": _sb(34, U16),
+    "tl": _sb(18, U16), "wl": _sb(12, U16), "xl": _sb(24, U16), "sl": _sb(6, U16),
+    "bc": _sb(72, F32), "tg": _sb(32, F32), "zo": _sb(24, F32), "zl": _sb(24, U16),
+    "s1": _sb(C, F32), "bm": _sb(96, F32), "ref": _sb(96, F32), "sc": _sb(96, F32), "dsc": _sb(96, F32),
+    "th": _sb(56, F32), "fl": _sb(144, BF), "fa": _sb(32, BF), "xc": _sb(384, BF), "dh": _sb(576, BF), "val": _sb(384, BF),
+    "tu": _sb(48, F32), "tv": _sb(24, F32), "tc": _sb(24, F32), "kt": _sb(72, F32), "t2": _sb(60, F32),
+    "ta": _sb(24, F32), "tm": _sb(32, F32), "tp": _sb(32, F32), "tf": _sb(24, F32),
+    "qs": _sb(72, F32), "sq": _sb(48, F32), "cs": _sb(36, F32), "kw": _sb(100, F32),
+    "oh": _sb(160, F32), "ne": _sb(160, F32), "st": _sb(150, F32), "so": _sb(150, F32), "skb": _sb(18, F32), "yb": _sb(C, F32),
     "ps": ("psum", [128, 4096], F32),
 }
 POOL = {"v": 40, "a": 30, "p": 16, "g": 20}
-NDMA = 24
+NDMA = 30
 SEMAPHORES = (["%s%d" % (q, k) for q in POOL for k in range(POOL[q])] + ["d%d" % k for k in range(NDMA)]
-              + ["ta0", "ta1", "ta2", "fa0", "fa1", "left"])
+              + ["ta0", "ta1", "ta2", "fa0", "fa1", "uc", "left"])
 
 
 def R(name, a, b, s=1):
@@ -130,8 +133,8 @@ def rank_program(g, core, T, topo):
     common = set(topo.engines(T.cores[0], T.cores[1]))
     for k in range(n_ranks):
         common &= set(topo.engines(T.cores[k], T.cores[(k + 1) % n_ranks])) & set(topo.engines(T.cores[(k + 1) % n_ranks], T.cores[k]))
-    n_eng = len(common)
-    mask = sum(1 << e for e in common)
+    common = sorted(common)
+    use = {name: common for name in ("ta0", "ta1", "ta2", "fa0", "fa1", "uc")}
     ops = []
 
     def ap(r):
@@ -177,21 +180,32 @@ def rank_program(g, core, T, topo):
     def horner(o, flags, table, ext=()):
         scan(o, flags, table, 0.0, A.mult, A.add, ext)
 
-    def pick_own(o, src, d):
-        scan(o, src, d, -K, A.max, A.add)
+    def pick_own(o, src, d, k=K):
+        scan(o, src, d, -k, A.max, A.add)
+
+    def columns(o, a):
+        ts(o, a, 1.0, A.add, 512.0, A.mult)
 
     def quant(oq, osc, a):
         op("v", lambda q: q.quantize_mx(ap(oq), ap(osc), ap(a)), [a], [oq, osc])
 
-    def act(o, a, scale=1.0, bias=None, accum=None):
-        if accum is not None:
-            op("a", lambda q: q.activation(ap(o), ap(a), F.Copy, accum_out=ap(accum)), [a], [o, accum])
-        elif bias is not None:
-            op("a", lambda q: q.activation(ap(o), ap(a), F.Identity, bias=val(bias), scale=scale), [a, bias], [o])
-        elif scale == 1.0:
-            op("a", lambda q: q.activation(ap(o), ap(a), F.Copy), [a], [o])
-        else:
-            op("a", lambda q: q.activation(ap(o), ap(a), F.Copy, scale=scale), [a], [o])
+    def act(o, a, scale=1.0, bias=None, accum=None, f=None):
+        kw = {}
+        if scale != 1.0:
+            kw["scale"] = scale
+        if f is None:
+            f = F.Copy if bias is None else F.Identity
+
+        def call(q):
+            if bias is not None:
+                kw["bias"] = val(bias)
+            if accum is not None:
+                kw["accum_out"] = ap(accum)
+            return q.activation(ap(o), ap(a), f, **kw)
+        op("a", call, [a, bias], [o, accum])
+
+    def zeros(o):
+        act(o, R("zero", 0, len(range(o[1], o[2], o[3]))))
 
     def mm(o, wq, wsc, xq, xsc, start=True, stop=True, ext=()):
         op("p", lambda q: q.matmul_mx(ap(o), ap(wq), ap(wsc), ap(xq), ap(xsc), start, stop), [wq, wsc, xq, xsc], [o], ext, acc=not start)
@@ -205,6 +219,9 @@ def rank_program(g, core, T, topo):
     def const(o, x):
         iota(o, [[0, len(range(o[1], o[2], o[3]))]], x)
 
+    def pair(name, y, x0, x1):
+        iota(R(name, y, 24, 4), [[x1 - x0, 2], [0, 3]], x0)
+
     def sel(o, a, pattern, f, fill_with, base, cm):
         op("g", lambda q: q.affine_select(ap(o), ap(a), pattern, f, fill_with, base, cm), [a], [o])
 
@@ -213,6 +230,7 @@ def rank_program(g, core, T, topo):
 
     def send(to, o, a, sem, codes=False):
         rid, pid, _ = topo.addr(to)
+        mask = sum(1 << e for e in use[sem])
         if codes:
             op("g", lambda q: q.remote_dma(ap(o).bitcast(dt.uint8), ap(a).bitcast(dt.uint8), T.sem[sem], T.sem.left, pid, rid, mask), [a], [])
         else:
@@ -221,7 +239,16 @@ def rank_program(g, core, T, topo):
     def col(k):
         return R("col", k, k + 1)
 
-    zw = ["zw0", "zw1", "zw2", "xf"]
+    def plane(name, b, a=0, e=C):
+        return R(name, C * b + a, C * b + e)
+
+    def entry(name, y, k, n=1):
+        return R(name, 12 * k + y, 12 * (k + n), 4)
+
+    def ow(k, n=1):
+        return R("ow", 48 * k + 15, 48 * (k + n), 16)
+
+    zw = ["zw0", "zw1", "zw2"]
 
     dma("a", lambda: T.ub[:], lambda: T.u[:], [], [R("ub", 0, 512)])
     dma("s", lambda: T.zw0[:, 0:1152], lambda: T.x[:], [], [R("zw0", 0, 1152)])
@@ -229,326 +256,441 @@ def rank_program(g, core, T, topo):
     iota(R("pi", 0, 1), [[0, 1]], 0, 1)
     iota(R("upi", 0, 16), [[1, 2], [16, 8]], 0)
     iota(R("r16", 0, C), [[0, 18], [1, 16]], 0)
-    iota(R("rc", 0, 18), [[16, 18]], -303)
+    iota(R("og", 0, 128), [[1, 8], [0, 16]], 0)
+    iota(R("rc", 0, 18), [[32, 18]], -574)
+    const(R("rc", 16, 18), -318)
+    iota(R("ij", 0, C), [[1, C]], 0)
     fill(R("zero", 0, 512), 0.0)
-    for b in range(4):
-        dma("s", lambda b=b: T.et[:, 512 * b:512 * b + 512], lambda: T.zero[:], [R("zero", 0, 512), R("zw0", 0, 1)],
-            [R("et", 512 * b, 512 * b + 512)])
-    dma("s", lambda: T.wq[:].bitcast(dt.uint8), lambda: T.wc[:], [], [R("wq", 0, 512)])
+    dma("s", lambda: T.wq[:].bitcast(dt.uint8), lambda: T.wc[:], [R("zw0", 0, 1)], [R("wq", 0, 512)])
     dma("s", lambda: T.wsc[:], lambda: T.ws[:], [], [R("wsc", 0, 512)])
     dma("s", lambda: T.vb[:], lambda: T.v[:], [], [R("vb", 0, 512)])
     fill(R("h0", 0, C), BIG)
     ts(R("pb", 0, 1), R("pi", 0, 1), 15, A.bitwise_and)
-    ts(R("pb", 1, 2), R("pi", 0, 1), 2, A.arith_shift_right, 3, A.bitwise_and)
-    ts(R("pb", 2, 3), R("pi", 0, 1), 3, A.bitwise_and)
+    ts(R("pb", 1, 2), R("pi", 0, 1), 4, A.arith_shift_right)
+    ts(R("pb", 2, 3), R("pi", 0, 1), 14, A.bitwise_and)
     cp(R("upl", 0, 16), R("upi", 0, 16))
     fill(R("h0", 0, C, 16), -BIG)
-    cp(R("col", 0, 3), R("pb", 0, 3))
+    cp(R("col", 0, 2), R("pb", 0, 2))
+    ts(R("upl", 24, 25), R("pb", 2, 3), 8.0, A.mult, 1.0, A.add)
+    ts(R("upl", 16, 24), R("upi", 0, 8), 0.125, A.mult)
     tiles, at = [], 0
     for blocks in ([None, 17, 16, 15], [14, 13, 12, 11], [10, 9, 8, 7], [6, 5, 4, 3], [2, 1, 0]):
         w = max(128, 16 * max(c for c in blocks if c is not None) + 16)
         low = 16 * blocks[-1] + 16 if len(blocks) == 4 else 0
         tiles.append((at, w, blocks))
-        fill(R("bt", 4 * (at + low), 4 * (at + w)), 1.0 if len(tiles) == 2 else 0.0)
+        if len(tiles) < 4:
+            zeros(R("bt", 4 * (at + low), 4 * (at + w)))
+        else:
+            fill(R("bt", 4 * (at + low), 4 * (at + w)), 0.0)
         at += w
+    zeros(R("tt", 384, 512))
+    zeros(R("et", 0, 512))
+    zeros(R("et", 512, 516))
     ts(R("e16", 0, C), R("r16", 0, C), col(0), A.is_equal, 0.5, A.subtract)
-    sel(R("ot", 0, 512), R("zero", 0, 512), [[-16, 8], [0, 64]], A.is_ge, 1.0, -16, 1)
-    sel(R("ot", 0, 512), R("ot", 0, 512), [[-16, 8], [0, 64]], A.is_ge, 0.0, 0, 1)
-    iota(R("r4", 0, 96), [[0, 24], [1, 4]], 0)
-    iota(R("ij", 0, C), [[1, C]], 0)
+    for t in range(4):
+        ts(R("ot", t, 512, 4), R("og", 0, 128), col(1), A.is_equal, 1.0 if t else 2.0, A.mult)
     act(R("m16", 0, C), R("e16", 0, C), scale=2 * BIG)
+    quant(R("oq", 0, 128), R("osq", 0, 128), R("ot", 0, 512))
     quant(R("uq", 0, 128), R("us", 0, 128), R("ub", 0, 512))
 
+    def pick(oq, osc, q_, sc_, by, ext=()):
+        op("v", lambda q: q.tensor_copy(ap(oq).bitcast(dt.uint32), ap(q_).bitcast(dt.uint32).indirect(ap(by))), [q_, by], [oq], ext)
+        op("a", lambda q: q.activation(ap(osc), ap((sc_, by)), F.Copy), [sc_, by], [osc], ext)
+
     def pick_u(k):
-        op("v", lambda q: q.tensor_copy(T.upq[:, 128 * k:128 * k + 128].bitcast(dt.uint32),
-                                        T.uq[:, 0:128].bitcast(dt.uint32).indirect(T.upl[:, 8 * k:8 * k + 8])),
-           [R("uq", 0, 128), R("upl", 0, 16)], [R("upq", 128 * k, 128 * k + 128)])
-        act(R("ups", 128 * k, 128 * k + 128), (R("us", 0, 128), R("upl", 8 * k, 8 * k + 8)))
+        pick(R("upq", 128 * k, 128 * k + 128), R("ups", 128 * k, 128 * k + 128), R("uq", 0, 128), R("us", 0, 128), R("upl", 8 * k, 8 * k + 8))
 
     pick_u(0)
+    pick(R("ucq", 0, 16), R("ucs", 0, 16), R("uq", 0, 128), R("us", 0, 128), R("upl", 24, 25))
+    send(prv, R("unq", 0, 16), R("ucq", 0, 16), "uc", codes=True)
+    send(prv, R("uns", 0, 16), R("ucs", 0, 16), "uc")
+    pick_u(1)
+    act(col(2), col(0), scale=-K, bias=-3 * K)
+    act(R("d16", 0, C), R("e16", 0, C), scale=18 * K, bias=8 * K)
+    zeros(R("rs", 0, 1))
+    act(R("d16", 15, C, 16), R("d16", 15, C, 16), bias=col(2))
+    act(col(4), R("d16", 15, 16))
+    act(R("ra", 0, 18), R("rc", 0, 18), bias=R("d16", 15, 16))
+    act(col(3), col(0), scale=-1.0, bias=-3.0)
     u0, u1 = (R("upq", 0, 128), R("ups", 0, 128)), (R("upq", 128, 256), R("ups", 128, 256))
 
-    quant(R("lq", 0, C), R("ls", 0, C), R("zw0", 0, 1152))
+    low = C - 128
+    quant(R("lq", low, C), R("ls", low, C), R("zw0", 4 * low, 4 * C))
+    mm(bank(4, 0, 128), u0[0], u0[1], R("lq", low, C), R("ls", low, C))
+    quant(R("lq", 0, low), R("ls", 0, low), R("zw0", 0, 4 * low))
     mm(bank(0), u0[0], u0[1], R("lq", 0, C), R("ls", 0, C))
     mm(bank(3), u0[0], u0[1], R("lq", 0, C), R("ls", 0, C))
-    pick_u(1)
-    mm(bank(1), u1[0], u1[1], R("lq", 0, C), R("ls", 0, C))
-    act(R("col", 3, 6), R("col", 0, 3), scale=-K, bias=-3 * K)
-    act(R("d16", 0, C), R("e16", 0, C), scale=18 * K, bias=8 * K)
-    act(R("rs", 0, 1), R("zero", 0, 1))
-    act(R("d16", 15, C, 16), R("d16", 15, C, 16), bias=col(3))
-    act(col(6), col(2), bias=4 * K)
-    act(col(7), R("d16", 15, 16))
-    act(R("ra", 0, 18), R("rc", 0, 18), bias=R("d16", 15, 16))
-    tt(R("mm", 0, C), bank(0), R("m16", 0, C), A.min)
-    scan(R("hh", 0, C), R("h0", 0, C), R("mm", 0, C), -BIG, A.min, A.max)
-    quant(R("oq", 0, 128), R("osq", 0, 128), R("ot", 0, 512))
+    tt(R("mm", low, C), bank(4, 0, 128), R("m16", low, C), A.min)
+    scan(R("hh", low, C), R("h0", low, C), R("mm", low, C), -BIG, A.min, A.max)
 
-    def slot(n, t, w):
-        return R("bt", 4 * tiles[n][0] + t, 4 * (tiles[n][0] + w), 4)
+    def slot(n, t, w, low=0):
+        return R("bt", 4 * (tiles[n][0] + low) + t, 4 * (tiles[n][0] + w), 4)
 
     def own_score(c):
         return R("hh", 16 * c + 15, 16 * c + 16)
 
-    def row_sum(n, t):
-        c = tiles[n][2][t]
-        if c:
-            act(R("junk", 8 * c * (c - 1), 8 * c * (c + 1)), slot(n, t, 16 * c), accum=R("rs", c, c + 1))
-
     def compare(n, t):
         c = tiles[n][2][t]
-        ts(slot(n, t, 16 * c + 16), bank(0, 0, 16 * c + 16), own_score(c), A.is_ge)
-        row_sum(n, t)
+        if t:
+            ts(slot(n, t, 16 * c + 16), bank(0, 0, 16 * c + 16), own_score(c), A.is_ge, 2.0, A.mult)
+        else:
+            ts(slot(n, t, 16 * c + 16), bank(0, 0, 16 * c + 16), own_score(c), A.is_ge)
+        if c:
+            act(R("junk", 8 * c * (c - 1), 8 * c * (c + 1)), slot(n, t, 16 * c), scale=1.0 if t else 2.0, accum=R("rs", c, c + 1))
 
     def column_sums(n):
         at, w = tiles[n][:2]
         quant(R("bq", at, at + w), R("bs", at, at + w), R("bt", 4 * at, 4 * (at + w)))
         mm(bank(2, 0, w), R("oq", 0, 128), R("osq", 0, 128), R("bq", at, at + w), R("bs", at, at + w), n == 0, n == 4)
 
-    for t, c in enumerate(tiles[1][2]):
-        act(slot(1, t, 16 * c + 16), bank(3, 0, 16 * c + 16), scale=-1.0, bias=own_score(c))
-    for t in range(1, 4):
-        compare(0, t)
+    for t in (1, 2):
+        c = tiles[0][2][t]
+        act(slot(0, t, 16 * c + 16), bank(3, 0, 16 * c + 16), scale=-1.0, bias=own_score(c))
+    for t in (1, 2):
+        c = tiles[0][2][t]
+        act(slot(0, t, 16 * c), slot(0, t, 16 * c), scale=-1.0, bias=TINY, accum=R("rs", c, c + 1), f=F.Sign)
+        act(slot(0, t, 16 * c + 16, 16 * c), slot(0, t, 16 * c + 16, 16 * c), scale=-1.0, bias=TINY, f=F.Sign)
+    tt(R("mm", 0, low), bank(0, 0, low), R("m16", 0, low), A.min)
+    compare(0, 3)
+    scan(R("hh", 0, low), R("h0", 0, low), R("mm", 0, low), -BIG, A.min, A.max)
+    compare(1, 0)
     tt(slot(0, 0, C), bank(0), R("hh", 0, C), A.not_equal)
-    whole = R("bt", 4 * tiles[1][0], 4 * tiles[2][0])
-    ts(whole, whole, 0.0, A.is_le)
-    for t in range(4):
-        row_sum(1, t)
-    column_sums(0)
-    column_sums(1)
+    for t in range(1, 4):
+        compare(1, t)
     for n in range(2, 5):
         for t in range(len(tiles[n][2])):
             compare(n, t)
-            if t == 0 and n > 2:
-                column_sums(n - 1)
-    ts(R("e4", 0, 96), R("r4", 0, 96), col(1), A.is_equal, 0.5, A.subtract)
+            if t == 0:
+                column_sums(n - 2)
+    column_sums(3)
     column_sums(4)
-    ts(R("e4", 96, 120), R("r4", 0, 24), col(2), A.is_equal, 0.5, A.subtract)
-    const(R("dsc", 0, 96), 1)
-    const(R("th", 0, 32), 1)
-    const(R("dsc", 0, 96, 8), 0)
-    const(R("dsc", 4, 96, 8), 2)
-    iota(R("th", 32, 80), [[0, 12], [-1, 4]], 4)
-    iota(R("lf", 0, 2), [[64, 2]], 3)
-    iota(R("lf", 2, 6), [[32, 4]], 7)
-    iota(R("lf", 6, 12), [[0, 2], [4, 3]], 0)
-    iota(R("lf", 12, 18), [[16, 6]], 0)
-    iota(R("sr", 0, 12), [[32, 12]], 0)
-    for b in range(4):
-        sel(R("et", 512 * b + b, 512 * b + 512, 4), R("zero", 0, 128), [[-1, 128]], A.not_equal, 0.5, 0, 1)
-    act(R("d4", 0, 48), R("e4", 0, 48), scale=6 * K, bias=2 * K)
-    act(R("tt", 384, 512), R("zero", 0, 128))
-    act(R("d4", 3, 48, 4), R("d4", 3, 48, 4), bias=col(4))
+
+    def unpacker(b):
+        quant(R("eq", 128 * b, 128 * b + 128), R("es", 128 * b, 128 * b + 128), R("et", 3 - b, 515 - b))
+
+    sel(R("et", 3, 515, 4), R("zero", 0, 128), [[-1, 128]], A.not_equal, 0.5, 0, 1)
+    unpacker(0)
+    const(R("lf", 48, 544), 0)
+    iota(R("lf", 512, 536), [[0, 2], [2, 3], [0, 4]], 1)
+    iota(R("d6", 0, 6), [[0, 3], [2, 2]], 0)
+    iota(R("lf", 0, 24), [[0, 2], [32, 3], [0, 4]], 31)
+    iota(R("lf", 24, 48), [[0, 8], [32, 3]], 31)
+    iota(R("lf", 64, 88), [[0, 4], [48, 2], [16, 3]], 15)
+    iota(R("lf", 96, 120), [[48, 2], [0, 4], [4, 3]], 3)
+    iota(R("lf", 128, 152), [[12, 2], [0, 4], [4, 3]], 3)
+    iota(R("lf", 160, 184), [[0, 2], [4, 3], [0, 4]], 15)
+    iota(R("th", 0, 24), [[0, 6], [-1, 4]], 4)
+    iota(R("th", 24, 48), [[0, 4], [-1, 2], [0, 3]], 2)
+    iota(R("bc", 0, 36), [[1, 6], [0, 6]], 2048)
+    iota(R("bc", 36, 72), [[0, 3], [1, 4], [0, 3]], 2048)
+    for at, n in ((192, 5), (384, 3)):
+        iota(R("lf", at, at + 18 * n), [[4, 3], [0, 6], [12, n]], 3)
+        iota(R("lf", at + 16 * n + 16, at + 34 * n + 16), [[16, 3], [48, 6], [0, n]], 15)
+    for y, (x0, x1) in enumerate(((-1, 48), (1, -48), (0, 0))):
+        pair("tc", y, x0, x1)
+    const(entry("tc", 3, 0), 1)
+    iota(entry("tc", 3, 1), [[16, 3]], 48)
+    const(R("cs", 0, 12), 2)
+    act(R("ij", 0, C), R("ij", 0, C), scale=1.0 / 512)
+    act(R("d1", 0, 48), R("e16", 0, 48), scale=18.0, bias=8.0)
+    act(plane("x32", 0), R("zw0", 0, 1152, 4), scale=32.0)
+    act(R("d1", 15, 48, 16), R("d1", 15, 48, 16), bias=col(3))
+    for b in range(1, 4):
+        act(plane("x32", b), R("zw0", b, 1152, 4), scale=32.0)
     tt(R("d16", 15, C, 16), R("ra", 0, 18), R("rs", 0, 18), A.subtract)
+    unpacker(1)
     pick_own(R("cx", 0, C), bank(2), R("d16", 0, C))
-    ts(R("plu", 0, 18), R("cx", 15, C, 16), -1.0, A.mult, -K, A.add)
+    mm(bank(1), u1[0], u1[1], R("lq", 0, C), R("ls", 0, C))
+    ts(R("plu", 0, 18), R("cx", 15, C, 16), K, A.add, -0.5, A.mult)
     cp((R("orep", 0, C), R("plu", 0, 18)), R("ij", 0, C))
     for k in range(2):
-        pick_own(R("ow", 48 * k, 48 * k + 48), R("orep", k, C, 6), R("d4", 0, 48))
-    for k in range(2):
-        ts(R("tl", k, 24, 2), R("ow", 48 * k + 3, 48 * k + 48, 4), 4.0, A.mult, col(6), A.add)
+        pick_own(R("ow", 48 * k, 48 * k + 48), R("orep", k, C, 6), R("d1", 0, 48), 1.0)
+    columns(R("tl", 0, 6), ow(0, 2))
+    act(R("d16", 15, C, 16), R("zero", 0, 18), bias=col(4))
     act(R("s1", 0, C), bank(1))
-    act(R("d16", 15, C, 16), R("zero", 0, 18), bias=col(7))
-    act(R("m4", 0, 96), R("e4", 0, 96), scale=2 * BIG)
-    act(R("d4", 48, 72), R("e4", 96, 120), scale=6 * K, bias=2 * K)
-    act(col(8), col(2), scale=1.0 / 2048, bias=2.0)
-    act(col(9), col(0), scale=4.0)
-    act(col(10), col(1), scale=8.0)
-    act(col(11), col(2), scale=4.0, bias=col(1))
-    act(R("d4", 51, 72, 4), R("d4", 51, 72, 4), bias=col(5))
-    act(R("lf", 0, 2), R("lf", 0, 2), bias=col(9))
-    act(R("lf", 2, 5), R("lf", 2, 5), bias=col(10))
-    act(R("lf", 6, 12), R("lf", 6, 12), bias=col(1))
-    act(R("lf", 12, 18), R("lf", 12, 18), bias=col(11))
+    zeros(R("tu", 0, 48))
+    zeros(R("t2", 0, 60))
+    zeros(R("tv", 0, 12, 4))
+    zeros(R("kw", 0, 76))
 
-    def ow(k, n=1):
-        return R("ow", 48 * k + 3, 48 * (k + n), 4)
+    def take(q, r, b, c0=0, c1=6):
+        o, a = R("tt", 64 * c0 + b, 64 * c1, 4), (plane("x32", b), R("tl", 6 * r + c0, 6 * r + c1))
+        if q == "v":
+            ts(o, a, 2.0 ** -5, A.mult)
+        else:
+            act(o, a, scale=2.0 ** -5)
 
-    def su(k, role, n=1):
-        a = 96 * k + 48 * role
-        return R("su", a + 3, a + 48 * n, 4)
+    def flags(r):
+        return R("fl", 48 * r, 48 * r + 24)
 
-    def receipts_out(r, part):
+    def tables(name, k, part):
         if part == 0:
-            pick_own(R("jx", 24 * r, 24 * r + 24), R("jl", 24 * r, 24 * r + 24), R("d4", 48, 72))
-            tt(R("okr", 0, 96), bank(3, 32, 128), R("b4", 384 * r, 384 * r + 384, 4), A.is_ge)
-            ts(R("l16", 6 * r, 6 * r + 6), R("jx", 24 * r + 3, 24 * r + 24, 4), K, A.add)
-            tt(R("okv", 0, 96), (R("okr", 0, 96), R("lu", 12, 18)), R("arr", 96 * r, 96 * r + 96), A.mult)
+            tt(entry("t2", 2, k, 2), entry(name, 3, 1, 2), entry(name, 3, 2, 2), A.subtract)
+            tt(entry("t2", 1, k), entry(name, 3, 0), entry(name, 3, 1), A.subtract)
         else:
-            cp((R("held", 0, C), R("l16", 6 * r, 6 * r + 6)), R("okv", 0, 96))
+            act(entry("t2", 3, k, 2), entry(name, 3, 2, 2))
+            act(entry("t2", 0, k + 1), entry("t2", 2, k))
 
-    for r in range(3):
-        z, o24 = zw[r], 24 * r
-        own = R("fl", 80 * (r - 1) + 32, 80 * (r - 1) + 80)
-        came = R("fa", 48 * (r - 1), 48 * r)
+    def targets(r):
         if r == 0:
-            cp(R("tt", 0, 224), (R(z, 0, 1152), R("tl", 0, 14)))
-            act(R("tt", 224, 384), (R(z, 0, 1152), R("tl", 14, 24)))
+            tt(R("tg", 0, 32), (R("ow", 0, 96), R("lu", 4, 6)), R("bc", 0, 32), A.add)
         else:
-            ts(R("tt", 0, 224), (R("x32", 0, 1152), R("tl", o24, o24 + 14)), 2.0 ** -5, A.mult)
-            act(R("tt", 224, 384), (R("x32", 0, 1152), R("tl", o24 + 14, o24 + 24)), scale=2.0 ** -5)
-            act(R(z, 2, 1152, 4), R("x32", 2, 1152, 4), scale=2.0 ** -5)
+            tt(R("tg", 0, 32), (R("qs", 0, 64), R("lu", 6, 8)), R("bc", 36, 68), A.add)
+        ts(R("xl", 0, 24), R("tg", 0, 24), 2048.0, A.mult)
+        act(R("xc", 0, 384), (R(zw[r], 0, 1152), R("xl", 0, 24)), scale=0.5)
+
+    def bars(r):
+        scan(R("hb", 0, 96), R("h0", 0, 96), R("bm", 0, 96), -BIG, A.min, A.max)
+        sel(R("bo", 8 * r, 8 * r + 6), R("hb", 15, 96, 16), [[0, 6]], A.is_ge, 0.0, 0, 0)
+        send(prv, R("bn", 8 * r, 8 * r + 6), R("bo", 8 * r, 8 * r + 6), "fa%d" % r)
+
+    def refused(r, step):
+        if step == 0:
+            for i in range(2):
+                tt(R("rf", i, 6, 2), R("hh", 48 * i + 15, 48 * i + 48, 16), R("bn", 8 * r + 3 * i, 8 * r + 3 * i + 3), A.is_lt,
+                   (("fa%d" % r, len(use["fa%d" % r])),))
+        elif step == 1:
+            horner(R("ms", 0, 6), R("d6", 0, 6), R("rf", 0, 6))
+        elif step == 2:
+            tt(R("fa", 0, 32), (R("ms", 0, 6), R("lu", 32, 34)), R("th", 0, 32), A.is_ge)
+        elif step == 3:
+            horner(R("sq", 0, 24), R("fa", 0, 24), R("tu", 0, 24) if r == 0 else R("t2", 24, 48))
+        else:
+            columns(R("tl", 6 * r + 6, 6 * r + 12), entry("sq", 3, 0, 2))
+
+    def hold(r, b):
+        act(R("dh", H * b + 48 * r, H * b + 48 * r + 48), bank(4 + b, 80, 128))
+
+    def received(r):
+        at = (12, 36, 76)[r]
+        horner(R("kw", at, at + 24), flags(r), R("kt", 24 * r, 24 * r + 24))
+
+    def arrivals(k, part):
+        at, n = ((0, 5), (96, 3))[k]
+        if part == 0:
+            tt(R("ne", at, at + 16 * n + 16), (R("kw", 64 * k, 64 * k + 12 * n), R("lu", 12 + 12 * k, 13 + 12 * k + n)),
+               R("oh", at, at + 16 * n + 16), A.not_equal)
+        else:
+            horner(R("so", at, at + 18 * n), R("ne", at, at + 18 * n), R("st", at, at + 18 * n))
+
+    def aside(r, k):
+        if r == 0 and k == 0:
+            tt(entry("tv", 1, 1), ow(2), ow(4), A.subtract)
+        elif r == 0:
+            ts(R("lu", 12, 34), R("lx", 207, 544, 16), K, A.add)
+        elif r == 1:
+            tt(entry("t2", 2 - k, 4), entry("qs", 3, 2 + 2 * k), entry("qs", 3, 5 - 3 * k), A.subtract)
+
+    for b in range(4):
+        take("va"[b // 2], 0, b)
+    for r in range(3):
+        z = zw[r]
         quant(R("tq", 128 * r, 128 * r + 128), R("ts", 128 * r, 128 * r + 128), R("tt", 0, 512))
         land = C + 96 * r
         send(nxt, R("lq", land, land + 96), R("tq", 128 * r, 128 * r + 96), "ta%d" % r, codes=True)
         send(nxt, R("ls", land, land + 96), R("ts", 128 * r, 128 * r + 96), "ta%d" % r)
-        e2 = R("e2", 0, 12)
-        name, step = (("ow", 48), ("su", 96), ("s2", 96))[r]
-        first = [R(name, step * k + 3, step * k + 48, 4) for k in range(2)]
-
-        def targets(second):
-            for k, src in enumerate((first[0], second)):
-                ts(R("tg", o24 + k, o24 + 24, 2), src, 1.0 / 512, A.mult, col(8), A.add)
-            if r:
-                ts(R("xl", o24, o24 + 24), R("tg", o24, o24 + 24), 2048.0, A.mult)
-                act(R("xc", 0, 384), (R("x32", 0, 1152), R("xl", o24, o24 + 24)), scale=2.0 ** -6)
-
-        if r:
-            ts(R(z, 3, 1152, 4), R("x32", 3, 1152, 4), 2.0 ** -5, A.mult)
-            horner(R(name, 0, 48), own, R("tu" if r == 1 else "t2", 0, 48))
-            quant(R("xq", 0, C), R("xs", 0, C), R(z, 0, 1152))
-            mm(bank(1), u1[0], u1[1], R("xq", 0, C), R("xs", 0, C))
-            act(R("s1", 0, C), bank(1))
-            horner(R(name, 96, 144), own, R("tu", 48, 96) if r == 1 else R("t2", 96, 144))
-        for k in range(2):
-            ts(R("lb", o24 + k, o24 + 24, 2), first[k], K, A.add)
         if r == 0:
-            act(R("tu", 0, 192), R("zero", 0, 192))
-        act(R("b4", 384 * r, 384 * r + 384), (R("s1", 0, C), R("lb", o24, o24 + 24)))
-        if r == 0:
-            act(R("xc", 0, 384), R("tt", 0, 384), scale=0.5)
-            act(R("sc", 96, 128), R("zero", 0, 32))
-            act(R("sr", 0, 12), R("sr", 0, 12), bias=col(0))
-            quant(R("eq", 0, 512), R("es", 0, 512), R("et", 0, 2048))
-            targets(first[1])
-            cp(R("lu", 0, 18), R("lf", 0, 18))
+            window = R("tl", 0, 6)
+            act(R("bc", 0, 72), R("bc", 0, 72), scale=1.0 / 2048)
+            act(R("dsc", 0, 96, 2), R("zero", 0, 48), bias=1.0)
+            act(R("dsc", 1, 96, 2), R("e16", 0, 48), bias=1.5)
+            zeros(R("dsc", 0, 96, 32))
+            tt(R("bm", 0, 96), (R("s1", 0, C), window), R("m16", 0, 96), A.min)
+            pick_own(R("lx", 0, 192), R("lf", 0, 192), R("d16", 0, 192))
+            bars(0)
+            ts(R("lu", 0, 12), R("lx", 15, 192, 16), K, A.add)
+            unpacker(2)
+            targets(0)
+            unpacker(3)
             for k in range(2, 6):
-                pick_own(R("ow", 48 * k, 48 * k + 48), R("orep", k, C, 6), R("d4", 0, 48))
-            tt(R("tu", 1, 48, 4), ow(0), ow(1), A.subtract)
-            tt(R("tu", 48, 192, 4), ow(1, 3), ow(2, 3), A.subtract)
-            cp(R("tu", 3, 192, 4), ow(2, 4))
-            tt(R("tu", 2, 192, 4), ow(1, 4), ow(2, 4), A.subtract)
-            iota(R("arr", 0, 96, 2), [[16, 6], [2, 4], [8, 2]], 1)
-            iota(R("arr", 1, 96, 2), [[16, 6], [2, 4], [8, 2]], 2)
-            const(R("t1", 0, 48, 4), 384)
-            const(R("t1", 1, 48, 4), -384)
-            const(R("t1", 2, 48, 4), 0)
-        elif r == 1:
-            tt(e2, R("fl", 34, 80, 4), R("fl", 33, 80, 4), A.subtract)
-            horner(R("ss", 0, 48), own, R("t1", 0, 48))
-            tt(R("tmp", 0, 12), e2, R("tu", 2, 48, 4), A.mult)
-            cp(R("sl", 25, 48, 2), R("ss", 3, 48, 4))
-            tt(R("tb1", 0, 12), R("tmp", 0, 12), su(1, 0), A.add)
-            ts(R("th", 1, 24, 2), e2, 1.0, A.add)
-            targets(R("tb1", 0, 12))
-            for k in range(2, 4):
-                horner(R("su", 96 * k, 96 * k + 48), own, R("tu", 48 * k, 48 * k + 48))
-                horner(R("su", 96 * k + 48, 96 * k + 96), came, R("tu", 48 * k, 48 * k + 48))
-            tt(R("t2", 1, 96, 4), su(0, 0, 2), su(1, 0, 2), A.subtract)
-            tt(R("t2", 96, 192, 4), su(1, 0, 2), su(2, 0, 2), A.subtract)
-            tt(R("t2", 2, 192, 4), su(1, 0, 4), su(2, 0, 4), A.subtract)
+                pick_own(R("ow", 48 * k, 48 * k + 48), R("orep", k, C, 6), R("d1", 0, 48), 1.0)
+            pick(R("upn", 0, 128), R("usn", 0, 128), R("unq", 0, 16), R("uns", 0, 16), R("upl", 16, 24), (("uc", 2 * len(use["uc"])),))
         else:
-            tt(R("tmp", 12, 24), su(1, 0), su(3, 0), A.subtract)
-            tt(R("tb", 1, 48, 4), R("tb1", 0, 12), su(2, 0), A.subtract)
-            tt(R("tmp", 12, 24), R("tmp", 12, 24), e2, A.mult)
-            tt(R("tp", 0, 96), (R("e2", 0, 12), R("lu", 6, 12)), R("tm", 0, 96), A.mult)
-            tt(R("tb", 3, 48, 4), R("tmp", 12, 24), su(3, 0), A.add)
-            tt(R("tf", 0, 96), R("tp", 0, 96), R("ta", 0, 96), A.add)
-            tt(R("tb", 2, 48, 4), su(2, 0), R("tb", 3, 48, 4), A.subtract)
-            horner(R("ss", 48, 96), own, R("tf", 0, 48))
-            horner(R("sb", 0, 48), own, R("tb", 0, 48))
-            horner(R("ss", 96, 144), own, R("tf", 48, 96))
-            targets(R("sb", 3, 48, 4))
-            cp(R("th", 1, 24, 2), R("ss", 51, 96, 4))
-            cp(R("sl", 49, 72, 2), R("ss", 99, 144, 4))
-        if r:
-            receipts_out(r - 1, 1)
-        tt(R("bm", 0, 96), R("b4", 384 * r, 384 * r + 384, 4), R("m4", 0, 96), A.min)
+            window = R("wl", 6 * r - 6, 6 * r)
+            for b in (3, 2, 1):
+                ts(R(z, b, 1152, 4), plane("x32", b), 2.0 ** -5, A.mult)
+            act(R(z, 0, 1152, 4), plane("x32", 0), scale=2.0 ** -5)
+            act(R("th", 24, 56), (R("cs", 0, 24), R("lu", 8, 10)))
+            for h in range(2):
+                quant(R("xq", H * h, H * h + H), R("xs", H * h, H * h + H), R(z, 4 * H * h, 4 * H * h + 4 * H))
+                mm(bank(h, 0, H), u1[0], u1[1], R("xq", H * h, H * h + H), R("xs", H * h, H * h + H))
+                act(R("s1", H * h, H * h + H), bank(h, 0, H))
+            targets(r)
         if r == 0:
-            pick_own(R("ox", 0, C), R("orep", 0, C), R("d16", 0, C))
+            const(R("dh", 0, 576), 0)
+            act(entry("tu", 3, 0, 4), ow(2, 4))
+            tt(entry("tu", 2, 0, 4), ow(1, 4), ow(2, 4), A.subtract)
+            tt(entry("tu", 1, 0), ow(0), ow(1), A.subtract)
+            tt(entry("tu", 0, 1, 3), ow(1, 3), ow(2, 3), A.subtract)
+            for k in range(2):
+                act(entry("tv", 3, k), ow(3 + 2 * k))
+                act(entry("tv", 2, k), entry("tu", 2, 1 + 2 * k))
+            act(entry("tv", 1, 0), entry("tu", 2, 0))
+            act(entry("tv", 0, 1), entry("tu", 2, 1), scale=-1.0)
+            act(entry("tc", 3, 1), entry("tc", 3, 1), bias=col(0))
+            act(entry("ta", 3, 1), entry("tc", 3, 1), bias=96.0)
+            act(col(5), col(0), scale=2.0)
+            act(col(6), col(0), scale=-2.0)
+            pick_own(R("lx", 192, 384), R("lf", 192, 384), R("d16", 0, 192))
+            pick_own(R("lx", 384, 544), R("lf", 384, 544), R("d16", 0, 160))
+        else:
+            columns(window, entry("qs", 3, 0, 2))
+            for k in range(2):
+                ts(R("sl", 3 * k, 3 * k + 3), entry("cs", 3, 2), float(H * k), A.add)
+            if r == 1:
+                horner(R("qs", 24, 48), flags(0), R("tu", 24, 48))
+                horner(R("sq", 24, 48), R("fa", 0, 24), R("tu", 24, 48))
+                tt(R("tp", 0, 32), (R("cs", 0, 24), R("lu", 10, 12)), R("tm", 0, 32), A.mult)
+            else:
+                received(0)
+                received(1)
+            tt(R("bm", 0, 96), (R("s1", 0, C), window), R("m16", 0, 96), A.min)
+        if r < 2:
+            mm(bank(2, 0, 128), R("upn", 0, 128), R("usn", 0, 128), R("tq", 128 * r, 128 * r + 128), R("ts", 128 * r, 128 * r + 128))
+            tt(R("mm", 0, 96), bank(2, 0, 96), R("m16", 0, 96), A.min)
+            if r:
+                bars(1)
+            scan(R("hh", 0, 96), R("h0", 0, 96), R("mm", 0, 96), -BIG, A.min, A.max)
+        if r == 2:
+            act(R("st", 0, 90, 5), R("st", 0, 90, 5), bias=col(6))
+            act(R("st", 98, 150, 3), R("st", 98, 150, 3), bias=col(5))
+            arrivals(0, 0)
             quant(R("vq", 0, 128), R("vs", 0, 128), R("vb", 0, 512))
-            ts(R("o16", 0, 18), R("ox", 15, C, 16), K, A.add)
-            ts(R("sl", 24, 48, 2), R("sr", 0, 12), 384.0, A.add)
-            ts(R("sl", 48, 72, 2), R("sr", 0, 12), 768.0, A.add)
-        arrived = (("ta%d" % r, 2 * n_eng),)
+            arrivals(0, 1)
+        if r == 1:
+            tables("qs", 0, 0)
+            tables("sq", 2, 0)
+            tt(R("tf", 0, 24), R("tp", 0, 24), R("ta", 0, 24), A.add)
+        aside(r, 1)
+        arrived = (("ta%d" % r, 2 * len(use["ta%d" % r])),)
         tq, tsc = R("lq", land - 32, land + 96), R("ls", land - 32, land + 96)
         mm(bank(3, 0, 128), u1[0], u1[1], tq, tsc, ext=arrived)
         for b in range(4):
             mm(bank(4 + b, 0, 128), R("eq", 128 * b, 128 * b + 128), R("es", 128 * b, 128 * b + 128), tq, tsc, ext=arrived)
             if r:
-                act(R("dh", 384 * r + b, 384 * r + 384, 4), bank(4 + b, 32, 128))
-        tt(R("ref", 0, 96), bank(3, 32, 128), R("bm", 0, 96), A.is_lt)
+                hold(r, b)
+
+        def fresh(b):
+            n = 48 if r else 96
+            tt(R("val", n * b, n * b + n), bank(4 + b, 32, 32 + n), R("xc", n * b, n * b + n), A.add)
+
+        def second(k):
+            at = 192 + 96 * k
+            tt(R("val", at, at + 96), (R("dh", C * k, C * k + C), R("sl", 0, 6)), R("xc", at, at + 96), A.add)
+
+        for i in range(2):
+            tt(R("ref", i, 96, 2), bank(3, 32 + 48 * i, 80 + 48 * i), R("bm", 48 * i, 48 * i + 48), A.is_lt)
+        aside(r, 0)
         horner(R("sc", 0, 96), R("dsc", 0, 96), R("ref", 0, 96))
-        if r < 2:
-            tt(R("fl", 80 * r, 80 * r + 80), (R("sc", 0, 128), R("lu", 0, 5)), R("th", 0, 80), A.is_ge)
-            send(prv, R("fa", 48 * r, 48 * r + 48), R("fl", 80 * r + 32, 80 * r + 80), "fa%d" % r)
-        else:
-            tt(R("fl", 160, 184), R("sc", 3, 96, 4), R("th", 0, 24), A.is_ge)
-        if r == 0:
-            for b in range(2):
-                tt(R("val", b, 384, 4), bank(4 + b, 32, 128), R("xc", b, 384, 4), A.add)
-        tt(R("zo", 0, 24), R("fl", 80 * r, 80 * r + 24), R("tg", o24, o24 + 24), A.add)
-        if r == 0:
-            for b in range(2, 4):
-                tt(R("val", b, 384, 4), bank(4 + b, 32, 128), R("xc", b, 384, 4), A.add)
-        ts(R("zl", o24, o24 + 24), R("zo", 0, 24), 2048.0, A.mult)
+        fresh(0)
+        tt(R("fl", 48 * r, 48 * r + 48), (R("sc", 0, 96), R("lu", 0, 3)), R("th", 0, 48), A.is_ge)
+        fresh(1)
+        tt(R("zo", 0, 24), R("fl", 48 * r + 24, 48 * r + 48), R("tg", 0, 24), A.add)
+        if r:
+            second(0)
+        fresh(2)
+        ts(R("zl", 0, 24), R("zo", 0, 24), 2048.0, A.mult)
+        if r:
+            second(1)
+        fresh(3)
+        cp((R(z, 0, 3200), R("zl", 0, 24)), R("val", 0, 384))
         if r == 0:
             for b in range(4):
-                act(R("dh", b, 384, 4), bank(4 + b, 32, 128))
-            for k, x in enumerate((-1, 1, 0, 1)):
-                const(R("ta", k, 48, 4), x)
-            const(R("tm", 48, 96), -384)
-            for k, x in enumerate((1, 0, -3, 3)):
-                const(R("tm", k, 48, 4), x)
-            const(R("tm", 50, 96, 4), 384)
-        else:
-            tt(R("val", 0, 384), (R("dh", 0, 384 * r + 384), R("sl", o24, o24 + 24)), R("xc", 0, 384), A.add)
-        for k in range(2):
-            act(R("jl", o24 + k, o24 + 24, 2), first[k], bias=K)
-        if r == 0:
-            act(R("held", 0, C), R("zero", 0, C))
-            act(R("t2", 0, 192), R("zero", 0, 192))
-            act(R("tb", 0, 48, 4), R("zero", 0, 12))
-            act(R("t1", 3, 48, 4), R("sr", 0, 12), bias=400.0)
-            act(R("arr", 96, 192), R("arr", 0, 96), bias=96.0)
-            act(R("arr", 192, 288), R("arr", 0, 96), bias=192.0)
+                hold(0, b)
+            iota(R("kt", 0, 72, 2), [[0, 3], [8, 2], [0, 6]], 0)
+            iota(R("kt", 1, 72, 4), [[0, 3], [-16, 2], [0, 3]], 8)
+            for y, (m0, m1) in enumerate(((1, -48), (0, -48), (-3, 48), (3, -48))):
+                pair("tm", y, m0, m1)
+            for y, (a0, a1) in enumerate(((-2, 96), (1, 0), (3, -48))):
+                pair("ta", y, a0, a1)
+            const(entry("ta", 3, 0), -2)
+            const(R("tm", 24, 32), 0)
+            act(R("oh", 0, 96), (R("ow", 0, C), R("lu", 18, 24)))
+            act(R("oh", 96, 160), (R("ow", 0, C), R("lu", 28, 32)))
+            zeros(R("oh", 0, 90, 5))
+            zeros(R("oh", 96, 150, 3))
+        act(entry("kt", 3, 2 * r, 2), entry("qs", 3, 0, 2) if r else ow(0, 2))
         if r == 1:
-            act(R("t2", 3, 192, 4), su(2, 0, 4))
-            act(R("ta", 48, 96), R("t1", 0, 48))
-            act(R("ta", 51, 96, 4), R("sr", 0, 12), bias=784.0)
-        cp((R(z, 0, 3200), R("zl", o24, o24 + 24)), R("val", 0, 384))
-        quant(R("zq", 0, C), R("zs", 0, C), R(z, 0, 1152))
-        for b in range(4):
-            act(R("z32", C * b, C * b + C), R(z, b, 1152, 4), scale=32.0)
-            mm(bank(4 + b), R("wq", 128 * b, 128 * b + 128), R("wsc", 128 * b, 128 * b + 128), R("zq", 0, C), R("zs", 0, C))
-        receipts_out(r, 0)
-        for b in range(4):
-            tt(R("x32", b, 1152, 4), bank(4 + b), R("z32", C * b, C * b + C), A.add)
-            if b < 2 or (b == 2 and r == 2):
-                act(R(zw[r + 1], b, 1152, 4), R("x32", b, 1152, 4), scale=2.0 ** -5)
-            if r < 2 and b == 2:
-                got, back = R("fa", 48 * r, 48 * r + 48), (("fa%d" % r, n_eng),)
-                for k in range(2):
-                    if r == 0:
-                        horner(R("su", 96 * k + 48, 96 * k + 96), got, R("tu", 48 * k, 48 * k + 48), back)
-                    else:
-                        horner(R("s2", 96 * k + 48, 96 * k + 96), got, R("t2", 96 * k + 48, 96 * k + 96), back)
-                for k in range(2):
-                    ts(R("tl", o24 + 24 + k, o24 + 48, 2), R("su" if r == 0 else "s2", 96 * k + 51, 96 * k + 96, 4), 4.0, A.mult, col(6), A.add)
+            tables("qs", 0, 1)
+            tables("sq", 2, 1)
+            act(entry("t2", 3, 4), entry("qs", 3, 5))
+            const(R("st", 0, 150), -1)
+            for y in (2, 4):
+                const(R("st", y, 90, 5), -95)
+            iota(R("st", 0, 90, 5), [[-32, 3], [0, 6]], -1)
+            iota(R("st", 98, 150, 3), [[32, 3], [0, 6]], 193)
+        if r == 2:
+            act(R("st", 96, 150, 3), R("so", 4, 90, 5))
+        order = [(b, h) for b in range(4) for h in range(2)] if r < 2 else [(b, h) for h in range(2) for b in range(4)]
+        half = ((0, H), (H, C)) if r < 2 else ((0, C - 128), (C - 128, C))
+        for a, e in half:
+            quant(R("zq", a, e), R("zs", a, e), R(z, 4 * a, 4 * e))
+            if r == 2 and a == 0:
+                received(2)
+        for b, h in order:
+            a, e = half[h]
+            if r == 2:
+                act(plane("z32", b, a, e), R(z, 4 * a + b, 4 * e, 4), scale=32.0)
+            elif h == 0:
+                act(plane("z32", b), R(z, b, 1152, 4), scale=32.0)
+            mm(bank(4 - 4 * h + b, 0, e - a), R("wq", 128 * b, 128 * b + 128), R("wsc", 128 * b, 128 * b + 128), R("zq", a, e), R("zs", a, e))
+        if r < 2:
+            refused(r, 0)
+        else:
+            arrivals(1, 0)
 
-    ts(R("xf", 3, 1152, 4), R("x32", 3, 1152, 4), 2.0 ** -5, A.mult)
-    for h in range(2):
-        a, b = 144 * h, 144 * h + 144
-        quant(R("fq", a, b), R("fs", a, b), R("xf", 4 * a, 4 * b))
-        mm(bank(h, 0, 144), R("vq", 0, 128), R("vs", 0, 128), R("fq", a, b), R("fs", a, b))
-        act(R("yb", a, b), bank(h, 0, 144))
-    dma("a", lambda: T.y[:], lambda: T.yb[:], [R("yb", 0, C)], [])
-    dma("s", lambda: T.oc[:], lambda: T.fq[:].bitcast(dt.uint8), [R("fq", 0, C)], [])
+        def own_lists(k):
+            if k == 0:
+                horner(R("cs", 12, 36), flags(r), R("tf" if r else "tc", 0, 24))
+            elif k == 1:
+                horner(R("qs", 0, 24), flags(r), R("t2" if r else "tu", 0, 24))
+            elif r == 0:
+                horner(R("qs", 48, 72), flags(0), R("tv", 0, 24))
+            else:
+                horner(R("qs", 48, 60), R("fl", 48, 60), R("t2", 48, 60))
+
+        def outputs(h):
+            a, e = half[h]
+            quant(R("fq", a, e), R("fs", a, e), R("xf", 4 * a, 4 * e))
+            mm(bank(4 - 4 * h, 0, e - a), R("vq", 0, 128), R("vs", 0, 128), R("fq", a, e), R("fs", a, e))
+            dma("s", lambda: T.oc[:, 4 * a:4 * e], lambda: T.fq[:, a:e].bitcast(dt.uint8), [R("fq", a, e)], [])
+            act(R("yb", a, e), bank(4 - 4 * h, 0, e - a))
+            dma("a", lambda: T.y[:, a:e], lambda: T.yb[:, a:e], [R("yb", a, e)], [])
+
+        for n, (b, h) in enumerate(order):
+            a, e = half[h]
+            tt(plane("x32", b, a, e), bank(4 - 4 * h + b, 0, e - a), plane("z32", b, a, e), A.add)
+            if r == 2:
+                if h == 0:
+                    act(R("xf", b, 4 * e, 4), plane("x32", b, a, e), scale=2.0 ** -5)
+                if n == 0:
+                    arrivals(1, 1)
+                    sel(R("skb", 0, 18), R("so", 98, 150, 3), [[0, 18]], A.is_ge, 0.0, 0, 0)
+                    for c in range(3):
+                        dma("s", lambda c=c: T.sk[:, 96 * c:96 * c + 96], lambda c=c: T.skb[:, 6 * c:6 * c + 6], [R("skb", 0, 18)], [])
+                if n == 5:
+                    ts(R("xf", 4 * a, 4 * e, 4), plane("x32", 0, a, e), 2.0 ** -5, A.mult)
+                if n in (5, 6):
+                    act(R("xf", 4 * a + b, 4 * e, 4), plane("x32", b, a, e), scale=2.0 ** -5)
+                if n == 7:
+                    outputs(0)
+                    ts(R("xf", 4 * a + b, 4 * e, 4), plane("x32", b, a, e), 2.0 ** -5, A.mult)
+                    outputs(1)
+                continue
+            if n < 4:
+                refused(r, n + 1)
+            elif n < 7:
+                own_lists(n - 4)
+            if n == 3:
+                take("a", r + 1, 0)
+                take("a", r + 1, 1)
+            if n == 5:
+                take("a", r + 1, 2)
+            if n == 7:
+                take("v", r + 1, 3)
+
     for k in range(4):
-        dma("s" if k < 3 else "a", lambda k=k: T.osc[4 * k:4 * k + 4, :], lambda k=k: T.fs[32 * k:32 * k + 4, :], [R("fs", 0, C)], [])
-    receipts_out(2, 1)
-    ts(R("skb", 0, C), (R("held", 0, C), R("o16", 0, 18)), -1.0, A.add)
-    dma("a", lambda: T.sk[:], lambda: T.skb[0:128:16, :], [R("skb", 0, C)], [])
+        dma("s", lambda k=k: T.osc[4 * k:4 * k + 4, :], lambda k=k: T.fs[32 * k:32 * k + 4, :], [R("fs", 0, C)], [])
 
     emit(g, T, ops)
-    g.wait_ge(T.sem.left, 8 * n_eng)
+    g.wait_ge(T.sem.left, sum(len(e) * (1 if name[0] == "f" else 2) for name, e in use.items()))

@@ -1,7 +1,19 @@
-from concourse.mybir import dt, AluOpType as A, ActivationFunctionType as F
+from concourse.mybir import dt, AluOpType as A, ActivationFunctionType as F, AxisListType as AX
 
 C = 288
 H = 144
+LOW = 128
+SIGNS = (17, 16)
+EARLY = 1
+SHORT = (1, 2)
+BLEND = "f0 h0 r0 f1 h1 r1 v2 f2 r2 v3 f3 r3"
+LAST = ("qz0 rc qz1 az01 az02 az03 vz00 ne ad00 so ad01 ax00 ad02 ax01 ad03 ax02 vx03 vz10 vz11 qx0 vz12 vz13 "
+        "ad10 ad11 ay0 vx10 ad12 ax11 ad13 vx12 vx13 qx1 vy1")
+CUT = 160
+ZV = (0,)
+SPLIT = 2
+PLANES = 0
+PACK0 = 14
 BIG = 1.0e29
 TINY = 2.0 ** -100
 K = 1024.0
@@ -24,21 +36,27 @@ SCRATCH = {
     "bt": _sb(3840, BF), "bq": _sb(960, Q4), "bs": _sb(960, U8), "junk": _sb(2448, BF),
     "pi": _sb(4, I32), "pb": _sb(4, I32), "col": _sb(16, F32), "upi": _sb(16, I32), "upl": _sb(26, U16),
     "ucq": _sb(16, Q4), "ucs": _sb(16, U8), "unq": _sb(16, Q4), "uns": _sb(16, U8), "upn": _sb(128, Q4), "usn": _sb(128, U8),
-    "hb": _sb(96, F32), "bo": _sb(16, F32), "bn": _sb(16, F32), "rf": _sb(6, F32), "ms": _sb(6, F32), "d6": _sb(6, F32),
+    "hb": _sb(96, F32), "bo": _sb(16, F32), "bn": _sb(16, F32), "rf": _sb(6, F32), "tn": _sb(32, F32), "sf": _sb(16, F32), "sb": _sb(18, F32), "dk": _sb(160, F32), "ms": _sb(6, F32), "d6": _sb(6, F32),
     "r16": _sb(C, F32), "e16": _sb(C, F32), "m16": _sb(C, F32), "d16": _sb(C, F32), "h0": _sb(C, BF), "d1": _sb(48, F32),
     "mm": _sb(C, F32), "hh": _sb(C, F32), "rs": _sb(18, F32), "rc": _sb(18, F32), "ra": _sb(18, F32), "cx": _sb(C, F32),
     "plu": _sb(18, U16), "ij": _sb(C, F32), "orep": _sb(C, F32), "ow": _sb(C, F32),
-    "lf": _sb(544, F32), "lx": _sb(544, F32), "lu": _sb(34, U16),
-    "tl": _sb(18, U16), "wl": _sb(12, U16), "xl": _sb(24, U16), "sl": _sb(6, U16),
+    "lf": _sb(552, F32), "lx": _sb(544, F32), "lu": _sb(34, U16),
+    "tl": _sb(18, U16), "wl": _sb(12, U16), "xl": _sb(24, U16), "sl": _sb(12, U16),
     "bc": _sb(72, F32), "tg": _sb(32, F32), "zo": _sb(24, F32), "zl": _sb(24, U16),
     "s1": _sb(C, F32), "bm": _sb(96, F32), "ref": _sb(96, F32), "sc": _sb(96, F32), "dsc": _sb(96, F32),
     "th": _sb(56, F32), "fl": _sb(144, BF), "fa": _sb(32, BF), "xc": _sb(384, BF), "dh": _sb(576, BF), "val": _sb(384, BF),
     "tu": _sb(48, F32), "tv": _sb(24, F32), "tc": _sb(24, F32), "kt": _sb(72, F32), "t2": _sb(60, F32),
     "ta": _sb(24, F32), "tm": _sb(32, F32), "tp": _sb(32, F32), "tf": _sb(24, F32),
-    "qs": _sb(72, F32), "sq": _sb(48, F32), "cs": _sb(36, F32), "kw": _sb(100, F32),
+    "qs": _sb(72, F32), "sq": _sb(48, F32), "cs": _sb(48, F32), "kw": _sb(104, F32),
     "oh": _sb(160, F32), "ne": _sb(160, F32), "st": _sb(150, F32), "so": _sb(150, F32), "skb": _sb(18, F32), "yb": _sb(C, F32),
     "ps": ("psum", [128, 4096], F32),
 }
+CYCLE, PE, SCALAR, SCATTER, WAKE, LOCAL, REMOTE = 0.87, 1.15, 15.0, 2.5, 180.0, 900.0, 1100.0
+HOLD = {"local": 300.0, "remote": 300.0, "first": 2700.0}
+GRAIN, SLACK, LATE = 100.0, 20.0, 5000.0
+STORES = "ssaa"
+PASSES = 6
+WHOLE = True
 POOL = {"v": 40, "a": 30, "p": 16, "g": 20}
 NDMA = 30
 SEMAPHORES = (["%s%d" % (q, k) for q in POOL for k in range(POOL[q])] + ["d%d" % k for k in range(NDMA)]
@@ -62,42 +80,104 @@ def bits(r):
     return m
 
 
+def clash(o, e):
+    for name, (rd, wr) in o["use"].items():
+        if name in e["use"]:
+            erd, ewr = e["use"][name]
+            if name == "ps" and e["q"] != o["q"]:
+                if (rd | wr) & (erd | ewr):
+                    return True
+            elif name == "ps" and o["q"] == "p":
+                if wr & ewr and not o["acc"]:
+                    return True
+            elif wr & (erd | ewr) or rd & ewr:
+                return True
+    return False
+
+
+def arrange(ops):
+    n = len(ops)
+    pred, reach = [], []
+    for i, o in enumerate(ops):
+        mine, have = [], 0
+        for k in range(i - 1, -1, -1):
+            e = ops[k]
+            if e["sent"] and any(e["sent"] == name for name, _ in o["ext"]):
+                mine.append((k, e["lat"]))
+            elif o["acc"] and e["q"] == "p" and o["use"]["ps"][1] & e["use"]["ps"][1] and not have >> k & 1:
+                mine.append((k, 0.0))
+            elif not have >> k & 1 and clash(o, e):
+                mine.append((k, (e["lat"] if e["dma"] else 0.0) + WAKE))
+            else:
+                continue
+            have |= reach[k] | 1 << k
+        pred.append(mine)
+        reach.append(have)
+    rest = [o["cost"] + o["lat"] for o in ops]
+    for i in range(n - 1, -1, -1):
+        for k, gap in pred[i]:
+            rest[k] = max(rest[k], ops[k]["cost"] + gap + rest[i])
+    free, end, order, left = {}, {}, [], list(range(n))
+    while left:
+        soon = {}
+        for i in left:
+            t = free.get(ops[i]["q"], 0.0)
+            for k, gap in pred[i]:
+                t = max(t, (end[k] if k in end else soon[k] + ops[k]["cost"]) + gap)
+            soon[i] = t
+        bound = max(soon[i] + rest[i] for i in left)
+        ready = sorted((i for i in left if all(k in end for k, _ in pred[i])), key=lambda i: (soon[i] // GRAIN, -rest[i]))
+        best = None
+        for i in ready:
+            stop = soon[i] + ops[i]["cost"]
+            harm = max([stop + rest[u] - bound for u in left if u != i and ops[u]["q"] == ops[i]["q"] and soon[u] < stop and rest[u] > rest[i]] + [0.0])
+            if best is None or harm < best[0]:
+                best = (harm, i)
+            if harm <= SLACK:
+                break
+        i = best[1]
+        end[i] = free[ops[i]["q"]] = soon[i] + ops[i]["cost"]
+        order.append(i)
+        left.remove(i)
+    succ = [[] for _ in ops]
+    for i in range(n):
+        for k, gap in pred[i]:
+            succ[k].append((i, gap))
+
+    def place(turn, before, lead):
+        start, busy = {}, {}
+        for i in turn:
+            t, c = max([start[k] + ops[k]["cost"] + gap for k, gap in before[i]] + [lead[i]]), ops[i]["cost"]
+            for a, e in sorted(busy.setdefault(ops[i]["q"], [])):
+                if e > t and a < t + c:
+                    t = e
+            busy[ops[i]["q"]].append((t, t + c))
+            start[i] = t
+        return start
+
+    best = (max(end[i] + ops[i]["lat"] for i in range(n)), order)
+    for _ in range(PASSES):
+        back = place(sorted(range(n), key=lambda i: (-end[i], -i)), succ, [o["lat"] for o in ops])
+        turn = sorted(range(n), key=lambda i: (-back[i] - ops[i]["cost"], i))
+        start = place(turn, pred, [0.0] * n)
+        end = {i: start[i] + ops[i]["cost"] for i in range(n)}
+        span = max(end[i] + ops[i]["lat"] for i in range(n))
+        if span < best[0]:
+            best = (span, sorted(range(n), key=lambda i: (start[i], i)))
+    return best[1]
+
+
+PLAN = []
+
+
 def emit(g, T, ops):
     queue = {"v": g.vector, "a": g.scalar, "p": g.tensor, "g": g, "s": g.sync}
-    known_q = {q: 0 for q in queue}
-    before, done = {q: 0 for q in queue}, []
-    known, waits, wanted, seen = [], [], set(), {q: set() for q in queue}
-    for n, o in enumerate(ops):
-        deps = []
-        for k in range(n):
-            e = ops[k]
-            hit = False
-            for name, (rd, wr) in o["use"].items():
-                if name not in e["use"]:
-                    continue
-                erd, ewr = e["use"][name]
-                if name == "ps" and e["q"] != o["q"]:
-                    hit = hit or bool((rd | wr) & (erd | ewr))
-                elif name == "ps" and o["q"] == "p":
-                    hit = hit or (bool(wr & ewr) and not o["acc"])
-                else:
-                    hit = hit or bool(wr & (erd | ewr)) or bool(rd & ewr)
-            if hit:
-                deps.append(k)
-        have, mine = known_q[o["q"]], []
-        for k in reversed(deps):
-            if not have >> k & 1:
-                mine.append(k)
-                have |= known[k] | 1 << k
-                if not ops[k]["dma"]:
-                    have |= done[k]
-        known_q[o["q"]] = have
-        known.append(have)
-        done.append(before[o["q"]])
-        if not o["dma"]:
-            before[o["q"]] |= 1 << n | have
-        waits.append(mine)
-        wanted.update(mine)
+    if not PLAN:
+        PLAN.append(arrange(ops))
+        PLAN.append(waits_of([ops[i] for i in PLAN[0]]))
+    ops = [ops[i] for i in PLAN[0]]
+    waits = PLAN[1]
+    wanted, seen = {k for mine in waits for k in mine}, {q: set() for q in queue}
     sem, count, turn, ndma = {}, {}, {q: 0 for q in POOL}, 0
     for n, o in enumerate(ops):
         if o["dma"]:
@@ -124,6 +204,57 @@ def emit(g, T, ops):
             queue[o["q"]].wait_ge(T.sem[sem[n][0]], 16)
 
 
+def waits_of(ops):
+    known_q = {q: 0 for q in "vapgs"}
+    before, done = {q: 0 for q in "vapgs"}, []
+    known, waits = [], []
+    for n, o in enumerate(ops):
+        deps = [k for k in range(n) if clash(o, ops[k])]
+        have, mine = known_q[o["q"]], []
+        for k in reversed(deps):
+            if not have >> k & 1:
+                mine.append(k)
+                have |= known[k] | 1 << k
+                if not ops[k]["dma"]:
+                    have |= done[k]
+        known_q[o["q"]] = have
+        known.append(have)
+        done.append(before[o["q"]])
+        if not o["dma"]:
+            before[o["q"]] |= 1 << n | have
+        waits.append(mine)
+    return waits
+
+
+def size(r):
+    return 16 * (r[1][2] - r[1][1]) if len(r) == 2 else len(range(r[1], r[2], r[3]))
+
+
+def cost_of(q, kind, reads, writes):
+    if kind in HOLD:
+        return HOLD[kind]
+    out = writes[0]
+    n = size(out)
+    if kind == "quant":
+        return 12 + 0.9 * n
+    if q == "p":
+        return (n + 16) * PE
+    if q == "g":
+        return 150 + 2 * CYCLE * n
+    if len(out) == 2:
+        return 50 + SCATTER * CYCLE * n
+    if reads and len(reads[0]) == 2:
+        return 60 + 1.56 * CYCLE * n
+    if kind == "sum":
+        n = size(reads[0])
+    sides = [r[0] for r in [out] + list(reads) if isinstance(r, tuple) and size(r) == n]
+    if kind == "pair" and "ps" not in sides:
+        n *= 2
+    if q == "v" and kind == "" and all(SCRATCH[s][2] in (BF, U16) for s in sides):
+        n /= 2
+    return max(64, n) * CYCLE + (SCALAR if q == "a" else 0)
+
+
 def rank_program(g, core, T, topo):
     rank = T.rank_of(core)
     if rank is None:
@@ -147,7 +278,7 @@ def rank_program(g, core, T, topo):
     def val(x):
         return ap(x) if isinstance(x, tuple) else x
 
-    def op(q, fn, reads, writes, ext=(), dma=False, acc=False):
+    def op(q, fn, reads, writes, ext=(), dma=False, acc=False, kind="", lat=0.0, sent=None):
         use = {}
         for k, group in enumerate((reads, writes)):
             for r in group:
@@ -157,10 +288,11 @@ def rank_program(g, core, T, topo):
                 for p, side in parts:
                     u = use.setdefault(p[0], [0, 0])
                     u[side] |= bits(p)
-        ops.append({"q": q, "fn": fn, "use": use, "ext": ext, "dma": dma, "acc": acc})
+        ops.append({"q": q, "fn": fn, "use": use, "ext": ext, "dma": dma, "acc": acc, "lat": lat, "sent": sent,
+                    "cost": cost_of(q, kind, reads, writes)})
 
     def tt(o, a, b, f, ext=()):
-        op("v", lambda q: q.tensor_tensor(ap(o), ap(a), ap(b), f), [a, b], [o], ext)
+        op("v", lambda q: q.tensor_tensor(ap(o), ap(a), ap(b), f), [a, b], [o], ext, kind="pair")
 
     def ts(o, a, s1, f1, s2=None, f2=None):
         if f2 is None:
@@ -187,7 +319,7 @@ def rank_program(g, core, T, topo):
         ts(o, a, 1.0, A.add, 512.0, A.mult)
 
     def quant(oq, osc, a):
-        op("v", lambda q: q.quantize_mx(ap(oq), ap(osc), ap(a)), [a], [oq, osc])
+        op("v", lambda q: q.quantize_mx(ap(oq), ap(osc), ap(a)), [a], [oq, osc], kind="quant")
 
     def act(o, a, scale=1.0, bias=None, accum=None, f=None):
         kw = {}
@@ -225,16 +357,19 @@ def rank_program(g, core, T, topo):
     def sel(o, a, pattern, f, fill_with, base, cm):
         op("g", lambda q: q.affine_select(ap(o), ap(a), pattern, f, fill_with, base, cm), [a], [o])
 
-    def dma(queue, o, a, reads, writes):
-        op(queue, lambda q: q.dma_start(o(), a()), reads, writes, dma=True)
+    def dma(queue, o, a, reads, writes, row=512):
+        op(queue, lambda q: q.dma_start(o(), a()), reads, writes, dma=True, kind="local", lat=LOCAL + row / 3.0)
 
     def send(to, o, a, sem, codes=False):
         rid, pid, _ = topo.addr(to)
         mask = sum(1 << e for e in use[sem])
+        kind = "remote" if any(e["sent"] for e in ops) else "first"
+        lat = LATE if sem == "uc" else REMOTE
         if codes:
-            op("g", lambda q: q.remote_dma(ap(o).bitcast(dt.uint8), ap(a).bitcast(dt.uint8), T.sem[sem], T.sem.left, pid, rid, mask), [a], [])
+            op("g", lambda q: q.remote_dma(ap(o).bitcast(dt.uint8), ap(a).bitcast(dt.uint8), T.sem[sem], T.sem.left, pid, rid, mask), [a], [],
+               kind=kind, lat=lat, sent=sem)
         else:
-            op("g", lambda q: q.remote_dma(ap(o), ap(a), T.sem[sem], T.sem.left, pid, rid, mask), [a], [])
+            op("g", lambda q: q.remote_dma(ap(o), ap(a), T.sem[sem], T.sem.left, pid, rid, mask), [a], [], kind=kind, lat=lat, sent=sem)
 
     def col(k):
         return R("col", k, k + 1)
@@ -250,46 +385,60 @@ def rank_program(g, core, T, topo):
 
     zw = ["zw0", "zw1", "zw2"]
 
-    dma("a", lambda: T.ub[:], lambda: T.u[:], [], [R("ub", 0, 512)])
-    dma("s", lambda: T.zw0[:, 0:1152], lambda: T.x[:], [], [R("zw0", 0, 1152)])
+    dma("a", lambda: T.ub[:], lambda: T.u[:], [], [R("ub", 0, 512)], 1024)
+    dma("s", lambda: T.zw0[:, 0:4 * C], lambda: T.x[:], [], [R("zw0", 0, 4 * C)], 3300)
 
     iota(R("pi", 0, 1), [[0, 1]], 0, 1)
     iota(R("upi", 0, 16), [[1, 2], [16, 8]], 0)
-    iota(R("r16", 0, C), [[0, 18], [1, 16]], 0)
+    iota(R("r16", 0, 160), [[0, 10], [1, 16]], 0)
     iota(R("og", 0, 128), [[1, 8], [0, 16]], 0)
-    iota(R("rc", 0, 18), [[32, 18]], -574)
-    const(R("rc", 16, 18), -318)
-    iota(R("ij", 0, C), [[1, C]], 0)
     fill(R("zero", 0, 512), 0.0)
-    dma("s", lambda: T.wq[:].bitcast(dt.uint8), lambda: T.wc[:], [R("zw0", 0, 1)], [R("wq", 0, 512)])
+    fill(R("et", 0, 516), 0.0)
+    sel(R("et", 3, 515, 4), R("zero", 0, 128), [[-1, 128]], A.not_equal, 0.5, 0, 1)
+    rc = [16 * sum(k >= c for k in SIGNS) - 16 * c * (c in SIGNS) - 32 * (18 - c) - 30 for c in range(18)]
+    c = 0
+    while c < 18:
+        step, e = (0 if c in SIGNS else 32), c + 1
+        while e < 18 and (e in SIGNS) == (c in SIGNS):
+            e += 1
+        iota(R("rc", c, e), [[step, e - c]], rc[c])
+        c = e
+    iota(R("ij", 0, C), [[1, C]], 0)
+    dma("s", lambda: T.wq[:].bitcast(dt.uint8), lambda: T.wc[:], [R("zw0", 1151, 1152)], [R("wq", 0, 512)])
     dma("s", lambda: T.wsc[:], lambda: T.ws[:], [], [R("wsc", 0, 512)])
     dma("s", lambda: T.vb[:], lambda: T.v[:], [], [R("vb", 0, 512)])
-    fill(R("h0", 0, C), BIG)
+    fill(R("h0", 0, 160), BIG)
     ts(R("pb", 0, 1), R("pi", 0, 1), 15, A.bitwise_and)
     ts(R("pb", 1, 2), R("pi", 0, 1), 4, A.arith_shift_right)
     ts(R("pb", 2, 3), R("pi", 0, 1), 14, A.bitwise_and)
     cp(R("upl", 0, 16), R("upi", 0, 16))
-    fill(R("h0", 0, C, 16), -BIG)
+    fill(R("h0", 0, 160, 16), -BIG)
     cp(R("col", 0, 2), R("pb", 0, 2))
     ts(R("upl", 24, 25), R("pb", 2, 3), 8.0, A.mult, 1.0, A.add)
     ts(R("upl", 16, 24), R("upi", 0, 8), 0.125, A.mult)
     tiles, at = [], 0
-    for blocks in ([None, 17, 16, 15], [14, 13, 12, 11], [10, 9, 8, 7], [6, 5, 4, 3], [2, 1, 0]):
+    for blocks in ([None, 17, 16, 15], [14, 13, 12, 11], [10, 9, 8, 7], [6, 5, 4, 3], [0, 2, 1]):
         w = max(128, 16 * max(c for c in blocks if c is not None) + 16)
-        low = 16 * blocks[-1] + 16 if len(blocks) == 4 else 0
+        low = 16 * min(c for c in blocks if c is not None) + 16 if len(blocks) == 4 else 0
         tiles.append((at, w, blocks))
-        if len(tiles) < 4:
+        if len(tiles) < 5:
             zeros(R("bt", 4 * (at + low), 4 * (at + w)))
         else:
             fill(R("bt", 4 * (at + low), 4 * (at + w)), 0.0)
         at += w
-    zeros(R("tt", 384, 512))
-    zeros(R("et", 0, 512))
-    zeros(R("et", 512, 516))
-    ts(R("e16", 0, C), R("r16", 0, C), col(0), A.is_equal, 0.5, A.subtract)
+    ts(R("e16", 0, 160), R("r16", 0, 160), col(0), A.is_equal, 0.5, A.subtract)
+    act(R("m16", 0, 160), R("e16", 0, 160), scale=2 * BIG)
+    act(col(2), col(0), scale=-K, bias=-3 * K)
+    act(R("dk", 0, 160), R("e16", 0, 160), scale=18 * K, bias=8 * K)
+    fill(R("lf", 48, 128), 0.0)
+    fill(R("tt", 384, 512), 0.0)
+    fill(R("rs", 0, 1), 0.0)
     for t in range(4):
         ts(R("ot", t, 512, 4), R("og", 0, 128), col(1), A.is_equal, 1.0 if t else 2.0, A.mult)
-    act(R("m16", 0, C), R("e16", 0, C), scale=2 * BIG)
+
+    def unpacker(b):
+        quant(R("eq", 128 * b, 128 * b + 128), R("es", 128 * b, 128 * b + 128), R("et", 3 - b, 515 - b))
+
     quant(R("oq", 0, 128), R("osq", 0, 128), R("ot", 0, 512))
     quant(R("uq", 0, 128), R("us", 0, 128), R("ub", 0, 512))
 
@@ -301,27 +450,7 @@ def rank_program(g, core, T, topo):
         pick(R("upq", 128 * k, 128 * k + 128), R("ups", 128 * k, 128 * k + 128), R("uq", 0, 128), R("us", 0, 128), R("upl", 8 * k, 8 * k + 8))
 
     pick_u(0)
-    pick(R("ucq", 0, 16), R("ucs", 0, 16), R("uq", 0, 128), R("us", 0, 128), R("upl", 24, 25))
-    send(prv, R("unq", 0, 16), R("ucq", 0, 16), "uc", codes=True)
-    send(prv, R("uns", 0, 16), R("ucs", 0, 16), "uc")
-    pick_u(1)
-    act(col(2), col(0), scale=-K, bias=-3 * K)
-    act(R("d16", 0, C), R("e16", 0, C), scale=18 * K, bias=8 * K)
-    zeros(R("rs", 0, 1))
-    act(R("d16", 15, C, 16), R("d16", 15, C, 16), bias=col(2))
-    act(col(4), R("d16", 15, 16))
-    act(R("ra", 0, 18), R("rc", 0, 18), bias=R("d16", 15, 16))
-    act(col(3), col(0), scale=-1.0, bias=-3.0)
     u0, u1 = (R("upq", 0, 128), R("ups", 0, 128)), (R("upq", 128, 256), R("ups", 128, 256))
-
-    low = C - 128
-    quant(R("lq", low, C), R("ls", low, C), R("zw0", 4 * low, 4 * C))
-    mm(bank(4, 0, 128), u0[0], u0[1], R("lq", low, C), R("ls", low, C))
-    quant(R("lq", 0, low), R("ls", 0, low), R("zw0", 0, 4 * low))
-    mm(bank(0), u0[0], u0[1], R("lq", 0, C), R("ls", 0, C))
-    mm(bank(3), u0[0], u0[1], R("lq", 0, C), R("ls", 0, C))
-    tt(R("mm", low, C), bank(4, 0, 128), R("m16", low, C), A.min)
-    scan(R("hh", low, C), R("h0", low, C), R("mm", low, C), -BIG, A.min, A.max)
 
     def slot(n, t, w, low=0):
         return R("bt", 4 * (tiles[n][0] + low) + t, 4 * (tiles[n][0] + w), 4)
@@ -329,89 +458,112 @@ def rank_program(g, core, T, topo):
     def own_score(c):
         return R("hh", 16 * c + 15, 16 * c + 16)
 
-    def compare(n, t):
-        c = tiles[n][2][t]
+    where = {c: (n, t) for n in range(5) for t, c in enumerate(tiles[n][2])}
+
+    def compare(c):
+        (n, t), scores = where[c], bank(0, 0, 16 * c + 16)
         if t:
-            ts(slot(n, t, 16 * c + 16), bank(0, 0, 16 * c + 16), own_score(c), A.is_ge, 2.0, A.mult)
+            ts(slot(n, t, 16 * c + 16), scores, own_score(c), A.is_ge, 2.0, A.mult)
         else:
-            ts(slot(n, t, 16 * c + 16), bank(0, 0, 16 * c + 16), own_score(c), A.is_ge)
-        if c:
+            ts(slot(n, t, 16 * c + 16), scores, own_score(c), A.is_ge)
+
+    def row_sum(c):
+        n, t = where[c]
+        if c not in SHORT:
             act(R("junk", 8 * c * (c - 1), 8 * c * (c + 1)), slot(n, t, 16 * c), scale=1.0 if t else 2.0, accum=R("rs", c, c + 1))
+
+    def short_sum(c):
+        row = slot(*where[c], 16 * c)
+        op("v", lambda q: q.tensor_reduce(ap(R("rs", c, c + 1)), ap(row), AX.X, A.add), [row], [R("rs", c, c + 1)], kind="sum")
+
+    def pack(n):
+        at, w = tiles[n][:2]
+        quant(R("bq", at, at + w), R("bs", at, at + w), R("bt", 4 * at, 4 * (at + w)))
 
     def column_sums(n):
         at, w = tiles[n][:2]
-        quant(R("bq", at, at + w), R("bs", at, at + w), R("bt", 4 * at, 4 * (at + w)))
         mm(bank(2, 0, w), R("oq", 0, 128), R("osq", 0, 128), R("bq", at, at + w), R("bs", at, at + w), n == 0, n == 4)
 
-    for t in (1, 2):
-        c = tiles[0][2][t]
-        act(slot(0, t, 16 * c + 16), bank(3, 0, 16 * c + 16), scale=-1.0, bias=own_score(c))
-    for t in (1, 2):
-        c = tiles[0][2][t]
-        act(slot(0, t, 16 * c), slot(0, t, 16 * c), scale=-1.0, bias=TINY, accum=R("rs", c, c + 1), f=F.Sign)
-        act(slot(0, t, 16 * c + 16, 16 * c), slot(0, t, 16 * c + 16, 16 * c), scale=-1.0, bias=TINY, f=F.Sign)
+    def signs(blocks, k):
+        for c in blocks:
+            act(slot(*where[c], 16 * c + 16), bank(k, 0, 16 * c + 16), scale=-1.0, bias=own_score(c))
+        for c in blocks:
+            n, t = where[c]
+            act(slot(n, t, 16 * c), slot(n, t, 16 * c), scale=-1.0, bias=TINY, accum=R("rs", c, c + 1), f=F.Sign)
+            act(slot(n, t, 16 * c + 16, 16 * c), slot(n, t, 16 * c + 16, 16 * c), scale=-1.0, bias=TINY, f=F.Sign)
+
+    pick(R("ucq", 0, 16), R("ucs", 0, 16), R("uq", 0, 128), R("us", 0, 128), R("upl", 24, 25))
+    send(prv, R("unq", 0, 16), R("ucq", 0, 16), "uc", codes=True)
+    send(prv, R("uns", 0, 16), R("ucs", 0, 16), "uc")
+    pick_u(1)
+    act(R("dk", 15, 160, 16), R("dk", 15, 160, 16), bias=col(2))
+    act(R("d16", 0, 160), R("dk", 0, 160))
+    act(R("d16", 160, C), R("dk", 0, C - 160))
+    act(R("ra", 0, 18), R("rc", 0, 18), bias=R("dk", 15, 16))
+    low = C - 128
+    quant(R("lq", low, C), R("ls", low, C), R("zw0", 4 * low, 4 * C))
+    mm(bank(4, 0, 128), u0[0], u0[1], R("lq", low, C), R("ls", low, C))
+    quant(R("lq", 0, low), R("ls", 0, low), R("zw0", 0, 4 * low))
+    mm(bank(0), u0[0], u0[1], R("lq", 0, C), R("ls", 0, C))
+    mm(bank(3), u0[0], u0[1], R("lq", 0, C), R("ls", 0, C))
+    tt(R("mm", low, C), bank(4, 0, 128), R("m16", 0, 128), A.min)
+    scan(R("hh", low, C), R("h0", 0, 128), R("mm", low, C), -BIG, A.min, A.max)
+    signs(SIGNS, 3)
     tt(R("mm", 0, low), bank(0, 0, low), R("m16", 0, low), A.min)
-    compare(0, 3)
-    scan(R("hh", 0, low), R("h0", 0, low), R("mm", 0, low), -BIG, A.min, A.max)
-    compare(1, 0)
-    tt(slot(0, 0, C), bank(0), R("hh", 0, C), A.not_equal)
-    for t in range(1, 4):
-        compare(1, t)
-    for n in range(2, 5):
-        for t in range(len(tiles[n][2])):
-            compare(n, t)
-            if t == 0:
-                column_sums(n - 2)
-    column_sums(3)
-    column_sums(4)
-
-    def unpacker(b):
-        quant(R("eq", 128 * b, 128 * b + 128), R("es", 128 * b, 128 * b + 128), R("et", 3 - b, 515 - b))
-
-    sel(R("et", 3, 515, 4), R("zero", 0, 128), [[-1, 128]], A.not_equal, 0.5, 0, 1)
-    unpacker(0)
-    const(R("lf", 48, 544), 0)
-    iota(R("lf", 512, 536), [[0, 2], [2, 3], [0, 4]], 1)
-    iota(R("d6", 0, 6), [[0, 3], [2, 2]], 0)
+    for c in range(17, -1, -1):
+        if c not in SIGNS:
+            compare(c)
+            if c:
+                row_sum(c)
+        if c == 15:
+            scan(R("hh", 0, low), R("h0", 0, low), R("mm", 0, low), -BIG, A.min, A.max)
+        if c == 14:
+            tt(slot(0, 0, C), bank(0), R("hh", 0, C), A.not_equal)
+        if c in (10, 6, 2):
+            pack((10 - c) // 4)
+            column_sums((10 - c) // 4)
+    for n in (3, 4):
+        pack(n)
+        column_sums(n)
+    mm(bank(1), u1[0], u1[1], R("lq", 0, C), R("ls", 0, C))
+    for c in SHORT:
+        short_sum(c)
+    act(R("ij", 0, C), R("ij", 0, C), scale=1.0 / 512)
     iota(R("lf", 0, 24), [[0, 2], [32, 3], [0, 4]], 31)
     iota(R("lf", 24, 48), [[0, 8], [32, 3]], 31)
     iota(R("lf", 64, 88), [[0, 4], [48, 2], [16, 3]], 15)
-    iota(R("lf", 96, 120), [[48, 2], [0, 4], [4, 3]], 3)
-    iota(R("lf", 128, 152), [[12, 2], [0, 4], [4, 3]], 3)
-    iota(R("lf", 160, 184), [[0, 2], [4, 3], [0, 4]], 15)
+    for at in (96, 108):
+        iota(R("lf", at, at + 12), [[1, 3], [0, 2], [3, 2]], 0)
+    iota(R("bc", 0, 36), [[1, 6], [0, 6]], 2048)
     iota(R("th", 0, 24), [[0, 6], [-1, 4]], 4)
     iota(R("th", 24, 48), [[0, 4], [-1, 2], [0, 3]], 2)
-    iota(R("bc", 0, 36), [[1, 6], [0, 6]], 2048)
-    iota(R("bc", 36, 72), [[0, 3], [1, 4], [0, 3]], 2048)
-    for at, n in ((192, 5), (384, 3)):
-        iota(R("lf", at, at + 18 * n), [[4, 3], [0, 6], [12, n]], 3)
-        iota(R("lf", at + 16 * n + 16, at + 34 * n + 16), [[16, 3], [48, 6], [0, n]], 15)
-    for y, (x0, x1) in enumerate(((-1, 48), (1, -48), (0, 0))):
-        pair("tc", y, x0, x1)
-    const(entry("tc", 3, 0), 1)
-    iota(entry("tc", 3, 1), [[16, 3]], 48)
-    const(R("cs", 0, 12), 2)
-    act(R("ij", 0, C), R("ij", 0, C), scale=1.0 / 512)
-    act(R("d1", 0, 48), R("e16", 0, 48), scale=18.0, bias=8.0)
-    act(plane("x32", 0), R("zw0", 0, 1152, 4), scale=32.0)
-    act(R("d1", 15, 48, 16), R("d1", 15, 48, 16), bias=col(3))
-    for b in range(1, 4):
+    const(R("lf", 128, 224), 3)
+    iota(R("lf", 128, 152), [[48, 2], [0, 4], [4, 3]], 3)
+    iota(R("lf", 160, 184), [[12, 2], [0, 4], [4, 3]], 3)
+    iota(R("lf", 192, 216), [[0, 2], [4, 3], [0, 4]], 15)
+    for at, n in ((224, 5), (416, 3)):
+        iota(R("lf", at, at + 24 * n), [[4, 4], [0, 6], [12, n]], 3)
+        iota(R("lf", at + 16 * n + 16, at + 40 * n + 16), [[16, 4], [48, 6], [0, n]], 15)
+    act(R("d1", 0, 48), R("dk", 0, 48), scale=1.0 / K)
+    for b in range(PLANES, 4):
         act(plane("x32", b), R("zw0", b, 1152, 4), scale=32.0)
+    act(R("s1", 0, C), bank(1))
     tt(R("d16", 15, C, 16), R("ra", 0, 18), R("rs", 0, 18), A.subtract)
-    unpacker(1)
+    fill(R("dsc", 0, 96), 1.0)
     pick_own(R("cx", 0, C), bank(2), R("d16", 0, C))
-    mm(bank(1), u1[0], u1[1], R("lq", 0, C), R("ls", 0, C))
+    ts(R("dsc", 1, 96, 2), R("e16", 0, 48), 1.5, A.add)
     ts(R("plu", 0, 18), R("cx", 15, C, 16), K, A.add, -0.5, A.mult)
+    fill(R("dsc", 0, 96, 32), 0.0)
     cp((R("orep", 0, C), R("plu", 0, 18)), R("ij", 0, C))
+    fill(R("tu", 0, 48), 0.0)
     for k in range(2):
         pick_own(R("ow", 48 * k, 48 * k + 48), R("orep", k, C, 6), R("d1", 0, 48), 1.0)
+    pick_own(R("ow", 96, 144), R("orep", 2, C, 6), R("d1", 0, 48), 1.0)
     columns(R("tl", 0, 6), ow(0, 2))
-    act(R("d16", 15, C, 16), R("zero", 0, 18), bias=col(4))
-    act(R("s1", 0, C), bank(1))
-    zeros(R("tu", 0, 48))
-    zeros(R("t2", 0, 60))
-    zeros(R("tv", 0, 12, 4))
-    zeros(R("kw", 0, 76))
+    pick_own(R("ow", 144, 192), R("orep", 3, C, 6), R("d1", 0, 48), 1.0)
+
+    def copy(o, a):
+        sel(o, a, [[0, len(range(o[1], o[2], o[3]))]], A.is_ge, 0.0, 0, 0)
 
     def take(q, r, b, c0=0, c1=6):
         o, a = R("tt", 64 * c0 + b, 64 * c1, 4), (plane("x32", b), R("tl", 6 * r + c0, 6 * r + c1))
@@ -428,35 +580,50 @@ def rank_program(g, core, T, topo):
             tt(entry("t2", 2, k, 2), entry(name, 3, 1, 2), entry(name, 3, 2, 2), A.subtract)
             tt(entry("t2", 1, k), entry(name, 3, 0), entry(name, 3, 1), A.subtract)
         else:
-            act(entry("t2", 3, k, 2), entry(name, 3, 2, 2))
-            act(entry("t2", 0, k + 1), entry("t2", 2, k))
+            copy(entry("t2", 3, k, 2), entry(name, 3, 2, 2))
+            copy(entry("t2", 0, k + 1), entry("t2", 2, k))
 
     def targets(r):
         if r == 0:
             tt(R("tg", 0, 32), (R("ow", 0, 96), R("lu", 4, 6)), R("bc", 0, 32), A.add)
         else:
-            tt(R("tg", 0, 32), (R("qs", 0, 64), R("lu", 6, 8)), R("bc", 36, 68), A.add)
-        ts(R("xl", 0, 24), R("tg", 0, 24), 2048.0, A.mult)
-        act(R("xc", 0, 384), (R(zw[r], 0, 1152), R("xl", 0, 24)), scale=0.5)
+            tt(R("tg", 0, 32), (R("qs", 0, 64), R("lu", 8, 10)), R("bc", 36, 68), A.add)
+            ts(R("xl", 0, 24), R("tg", 0, 24), 2048.0, A.mult)
+            act(R("xc", 0, 384), (R(zw[r], 0, 1152), R("xl", 0, 24)), scale=0.5)
 
     def bars(r):
         scan(R("hb", 0, 96), R("h0", 0, 96), R("bm", 0, 96), -BIG, A.min, A.max)
-        sel(R("bo", 8 * r, 8 * r + 6), R("hb", 15, 96, 16), [[0, 6]], A.is_ge, 0.0, 0, 0)
+        copy(R("bo", 8 * r, 8 * r + 6), R("hb", 15, 96, 16))
         send(prv, R("bn", 8 * r, 8 * r + 6), R("bo", 8 * r, 8 * r + 6), "fa%d" % r)
 
     def refused(r, step):
         if step == 0:
-            for i in range(2):
-                tt(R("rf", i, 6, 2), R("hh", 48 * i + 15, 48 * i + 48, 16), R("bn", 8 * r + 3 * i, 8 * r + 3 * i + 3), A.is_lt,
-                   (("fa%d" % r, len(use["fa%d" % r])),))
+            tt(R("rf", 0, 6), R("hh", 15, 96, 16), R("bn", 8 * r, 8 * r + 6), A.is_lt, (("fa%d" % r, len(use["fa%d" % r])),))
         elif step == 1:
-            horner(R("ms", 0, 6), R("d6", 0, 6), R("rf", 0, 6))
+            tt(R("rf", 3, 6), R("rf", 0, 3), R("rf", 3, 6), A.add)
         elif step == 2:
-            tt(R("fa", 0, 32), (R("ms", 0, 6), R("lu", 32, 34)), R("th", 0, 32), A.is_ge)
+            tt(R("fa", 0, 32), (R("rf", 0, 6), R("lu", 6, 8)), R("tn", 0, 32), A.is_ge)
         elif step == 3:
             horner(R("sq", 0, 24), R("fa", 0, 24), R("tu", 0, 24) if r == 0 else R("t2", 24, 48))
         else:
             columns(R("tl", 6 * r + 6, 6 * r + 12), entry("sq", 3, 0, 2))
+
+    def score_sent(r, step):
+        if step == 0:
+            mm(bank(2, 0, 128), R("upn", 0, 128), R("usn", 0, 128), R("tq", 128 * r, 128 * r + 128), R("ts", 128 * r, 128 * r + 128))
+            tt(R("mm", 0, 96), bank(2, 0, 96), R("m16", 0, 96), A.min)
+        else:
+            scan(R("hh", 0, 96), R("h0", 0, 96), R("mm", 0, 96), -BIG, A.min, A.max)
+
+    def own_lists(r, k):
+        if k == 0:
+            horner(R("cs", 12, 36), flags(r), R("tf" if r else "tc", 0, 24))
+        elif k == 1:
+            horner(R("qs", 0, 24), flags(r), R("t2" if r else "tu", 0, 24))
+        elif r == 0:
+            horner(R("qs", 48, 72), flags(0), R("tv", 0, 24))
+        else:
+            horner(R("qs", 48, 60), R("fl", 48, 60), R("t2", 48, 60))
 
     def hold(r, b):
         act(R("dh", H * b + 48 * r, H * b + 48 * r + 48), bank(4 + b, 80, 128))
@@ -468,21 +635,22 @@ def rank_program(g, core, T, topo):
     def arrivals(k, part):
         at, n = ((0, 5), (96, 3))[k]
         if part == 0:
-            tt(R("ne", at, at + 16 * n + 16), (R("kw", 64 * k, 64 * k + 12 * n), R("lu", 12 + 12 * k, 13 + 12 * k + n)),
+            tt(R("ne", at, at + 16 * n + 16), (R("kw", 64 * k, 64 * k + 12 * n + 4), R("lu", 14 + 12 * k, 15 + 12 * k + n)),
                R("oh", at, at + 16 * n + 16), A.not_equal)
         else:
             horner(R("so", at, at + 18 * n), R("ne", at, at + 18 * n), R("st", at, at + 18 * n))
 
-    def aside(r, k):
-        if r == 0 and k == 0:
-            tt(entry("tv", 1, 1), ow(2), ow(4), A.subtract)
-        elif r == 0:
-            ts(R("lu", 12, 34), R("lx", 207, 544, 16), K, A.add)
-        elif r == 1:
-            tt(entry("t2", 2 - k, 4), entry("qs", 3, 2 + 2 * k), entry("qs", 3, 5 - 3 * k), A.subtract)
+    def lists(a, e):
+        for at in range(16 * a, 16 * e, 160):
+            n = min(160, 16 * e - at)
+            pick_own(R("lx", at, at + n), R("lf", at, at + n), R("dk", 0, n))
+
+    def offsets(a, e):
+        ts(R("lu", a, e), R("lx", 16 * a + 15, 16 * e, 16), K, A.add)
 
     for b in range(4):
         take("va"[b // 2], 0, b)
+    pick_own(R("ow", 192, 240), R("orep", 4, C, 6), R("d1", 0, 48), 1.0)
     for r in range(3):
         z = zw[r]
         quant(R("tq", 128 * r, 128 * r + 128), R("ts", 128 * r, 128 * r + 128), R("tt", 0, 512))
@@ -491,206 +659,225 @@ def rank_program(g, core, T, topo):
         send(nxt, R("ls", land, land + 96), R("ts", 128 * r, 128 * r + 96), "ta%d" % r)
         if r == 0:
             window = R("tl", 0, 6)
-            act(R("bc", 0, 72), R("bc", 0, 72), scale=1.0 / 2048)
-            act(R("dsc", 0, 96, 2), R("zero", 0, 48), bias=1.0)
-            act(R("dsc", 1, 96, 2), R("e16", 0, 48), bias=1.5)
-            zeros(R("dsc", 0, 96, 32))
+            act(R("bc", 0, 36), R("bc", 0, 36), scale=1.0 / 2048)
+            act(R("xc", 0, 384), R("tt", 0, 384), scale=0.5)
             tt(R("bm", 0, 96), (R("s1", 0, C), window), R("m16", 0, 96), A.min)
-            pick_own(R("lx", 0, 192), R("lf", 0, 192), R("d16", 0, 192))
+            lists(0, 8)
             bars(0)
-            ts(R("lu", 0, 12), R("lx", 15, 192, 16), K, A.add)
-            unpacker(2)
-            targets(0)
-            unpacker(3)
-            for k in range(2, 6):
-                pick_own(R("ow", 48 * k, 48 * k + 48), R("orep", k, C, 6), R("d1", 0, 48), 1.0)
+            offsets(0, 8)
             pick(R("upn", 0, 128), R("usn", 0, 128), R("unq", 0, 16), R("uns", 0, 16), R("upl", 16, 24), (("uc", 2 * len(use["uc"])),))
+            targets(0)
+            for b in range(4):
+                unpacker(b)
+            pick_own(R("ow", 240, C), R("orep", 5, C, 6), R("d1", 0, 48), 1.0)
+            iota(R("tn", 0, 32), [[0, 8], [-1, 2], [0, 2]], 2)
+            score_sent(0, 0)
+            tt(entry("tu", 2, 0, 4), ow(1, 4), ow(2, 4), A.subtract)
+            score_sent(0, 1)
+            tt(entry("tu", 1, 0), ow(0), ow(1), A.subtract)
+            tt(entry("tu", 0, 1, 3), ow(1, 3), ow(2, 3), A.subtract)
+            tt(entry("tv", 1, 1), ow(2), ow(4), A.subtract)
+            lists(8, 34)
+            offsets(8, 34)
+            act(entry("tu", 3, 0, 4), ow(2, 4))
+            act(col(5), col(0), scale=2.0)
+            act(col(6), col(0), scale=-2.0)
+            zeros(R("kw", 0, 104))
+            zeros(R("t2", 0, 60))
+            for y, (x0, x1) in enumerate(((-1, 48), (1, -48), (0, 0))):
+                pair("tc", y, x0, x1)
+            const(entry("tc", 3, 0), 1)
+            iota(entry("tc", 3, 1), [[16, 3]], 48)
+            const(R("cs", 0, 48), 2)
+            iota(R("bc", 36, 72), [[0, 3], [1, 4], [0, 3]], 2048)
+            iota(R("sb", 0, 18), [[H, 6], [0, 3]], 0)
+            const(R("tv", 0, 12, 4), 0)
+            for k in range(2):
+                copy(entry("tv", 3, k), ow(3 + 2 * k))
+                copy(entry("tv", 2, k), entry("tu", 2, 1 + 2 * k))
+            copy(entry("tv", 1, 0), entry("tu", 2, 0))
         else:
             window = R("wl", 6 * r - 6, 6 * r)
             for b in (3, 2, 1):
                 ts(R(z, b, 1152, 4), plane("x32", b), 2.0 ** -5, A.mult)
             act(R(z, 0, 1152, 4), plane("x32", 0), scale=2.0 ** -5)
-            act(R("th", 24, 56), (R("cs", 0, 24), R("lu", 8, 10)))
+            own_lists(r - 1, 1)
             for h in range(2):
                 quant(R("xq", H * h, H * h + H), R("xs", H * h, H * h + H), R(z, 4 * H * h, 4 * H * h + 4 * H))
                 mm(bank(h, 0, H), u1[0], u1[1], R("xq", H * h, H * h + H), R("xs", H * h, H * h + H))
                 act(R("s1", H * h, H * h + H), bank(h, 0, H))
-            targets(r)
-        if r == 0:
-            const(R("dh", 0, 576), 0)
-            act(entry("tu", 3, 0, 4), ow(2, 4))
-            tt(entry("tu", 2, 0, 4), ow(1, 4), ow(2, 4), A.subtract)
-            tt(entry("tu", 1, 0), ow(0), ow(1), A.subtract)
-            tt(entry("tu", 0, 1, 3), ow(1, 3), ow(2, 3), A.subtract)
-            for k in range(2):
-                act(entry("tv", 3, k), ow(3 + 2 * k))
-                act(entry("tv", 2, k), entry("tu", 2, 1 + 2 * k))
-            act(entry("tv", 1, 0), entry("tu", 2, 0))
-            act(entry("tv", 0, 1), entry("tu", 2, 1), scale=-1.0)
-            act(entry("tc", 3, 1), entry("tc", 3, 1), bias=col(0))
-            act(entry("ta", 3, 1), entry("tc", 3, 1), bias=96.0)
-            act(col(5), col(0), scale=2.0)
-            act(col(6), col(0), scale=-2.0)
-            pick_own(R("lx", 192, 384), R("lf", 192, 384), R("d16", 0, 192))
-            pick_own(R("lx", 384, 544), R("lf", 384, 544), R("d16", 0, 160))
-        else:
+            own_lists(r - 1, 2)
             columns(window, entry("qs", 3, 0, 2))
-            for k in range(2):
-                ts(R("sl", 3 * k, 3 * k + 3), entry("cs", 3, 2), float(H * k), A.add)
+            own_lists(r - 1, 0)
+            targets(r)
+            tt(R("bm", 0, 96), (R("s1", 0, C), window), R("m16", 0, 96), A.min)
+            if r < 2:
+                score_sent(r, 0)
+                bars(r)
+                score_sent(r, 1)
+            act(R("th", 24, 56), (R("cs", 0, 24), R("lu", 10, 12)))
+            tt(R("sf", 0, 16), (R("cs", 24, 48), R("lu", 10, 11)), R("sb", 0, 16), A.add)
             if r == 1:
                 horner(R("qs", 24, 48), flags(0), R("tu", 24, 48))
                 horner(R("sq", 24, 48), R("fa", 0, 24), R("tu", 24, 48))
-                tt(R("tp", 0, 32), (R("cs", 0, 24), R("lu", 10, 12)), R("tm", 0, 32), A.mult)
             else:
                 received(0)
                 received(1)
-            tt(R("bm", 0, 96), (R("s1", 0, C), window), R("m16", 0, 96), A.min)
-        if r < 2:
-            mm(bank(2, 0, 128), R("upn", 0, 128), R("usn", 0, 128), R("tq", 128 * r, 128 * r + 128), R("ts", 128 * r, 128 * r + 128))
-            tt(R("mm", 0, 96), bank(2, 0, 96), R("m16", 0, 96), A.min)
-            if r:
-                bars(1)
-            scan(R("hh", 0, 96), R("h0", 0, 96), R("mm", 0, 96), -BIG, A.min, A.max)
+            cp(R("sl", 0, 12), R("sf", 0, 12))
+        if r == 1:
+            tables("sq", 2, 0)
+            tables("sq", 2, 1)
+            tables("qs", 0, 0)
+            tt(R("tp", 0, 32), (R("cs", 0, 24), R("lu", 12, 14)), R("tm", 0, 32), A.mult)
+            for k in range(2):
+                tt(entry("t2", 2 - k, 4), entry("qs", 3, 2 + 2 * k), entry("qs", 3, 5 - 3 * k), A.subtract)
+            tt(R("tf", 0, 24), R("tp", 0, 24), R("ta", 0, 24), A.add)
         if r == 2:
             act(R("st", 0, 90, 5), R("st", 0, 90, 5), bias=col(6))
             act(R("st", 98, 150, 3), R("st", 98, 150, 3), bias=col(5))
             arrivals(0, 0)
             quant(R("vq", 0, 128), R("vs", 0, 128), R("vb", 0, 512))
             arrivals(0, 1)
-        if r == 1:
-            tables("qs", 0, 0)
-            tables("sq", 2, 0)
-            tt(R("tf", 0, 24), R("tp", 0, 24), R("ta", 0, 24), A.add)
-        aside(r, 1)
         arrived = (("ta%d" % r, 2 * len(use["ta%d" % r])),)
         tq, tsc = R("lq", land - 32, land + 96), R("ls", land - 32, land + 96)
         mm(bank(3, 0, 128), u1[0], u1[1], tq, tsc, ext=arrived)
         for b in range(4):
             mm(bank(4 + b, 0, 128), R("eq", 128 * b, 128 * b + 128), R("es", 128 * b, 128 * b + 128), tq, tsc, ext=arrived)
-            if r:
-                hold(r, b)
 
         def fresh(b):
             n = 48 if r else 96
-            tt(R("val", n * b, n * b + n), bank(4 + b, 32, 32 + n), R("xc", n * b, n * b + n), A.add)
+            tt(R("val", n * b, n * b + n), bank(4 + b, 32, 32 + n), R("xc", n * b, n * b + n) if r else R("xc", b, 384, 4), A.add)
 
-        def second(k):
-            at = 192 + 96 * k
-            tt(R("val", at, at + 96), (R("dh", C * k, C * k + C), R("sl", 0, 6)), R("xc", at, at + 96), A.add)
-
+        receipts = [lambda: horner(R("sc", 0, 96), R("dsc", 0, 96), R("ref", 0, 96)),
+                    lambda: tt(R("fl", 48 * r, 48 * r + 48), (R("sc", 0, 96), R("lu", 0, 3)), R("th", 0, 48), A.is_ge),
+                    lambda: tt(R("zo", 0, 24), R("fl", 48 * r + 24, 48 * r + 48), R("tg", 0, 24), A.add),
+                    lambda: ts(R("zl", 0, 24), R("zo", 0, 24), 2048.0, A.mult)]
         for i in range(2):
             tt(R("ref", i, 96, 2), bank(3, 32 + 48 * i, 80 + 48 * i), R("bm", 48 * i, 48 * i + 48), A.is_lt)
-        aside(r, 0)
-        horner(R("sc", 0, 96), R("dsc", 0, 96), R("ref", 0, 96))
-        fresh(0)
-        tt(R("fl", 48 * r, 48 * r + 48), (R("sc", 0, 96), R("lu", 0, 3)), R("th", 0, 48), A.is_ge)
-        fresh(1)
-        tt(R("zo", 0, 24), R("fl", 48 * r + 24, 48 * r + 48), R("tg", 0, 24), A.add)
+        for step in (BLEND if r else "f0 r0 f1 r1 f2 r2 f3 r3").split():
+            k = int(step[1])
+            if step[0] == "f":
+                fresh(k)
+            elif step[0] == "h":
+                hold(r, k)
+            elif step[0] == "v":
+                cp(R("dh", H * k + 48 * r, H * k + 48 * r + 48), bank(4 + k, 80, 128))
+            else:
+                receipts[k]()
         if r:
-            second(0)
-        fresh(2)
-        ts(R("zl", 0, 24), R("zo", 0, 24), 2048.0, A.mult)
-        if r:
-            second(1)
-        fresh(3)
+            tt(R("val", 192, 384), (R("dh", 0, 576), R("sl", 0, 12)), R("xc", 192, 384), A.add)
+        if r == 0:
+            refused(0, 0)
         cp((R(z, 0, 3200), R("zl", 0, 24)), R("val", 0, 384))
         if r == 0:
             for b in range(4):
                 hold(0, b)
-            iota(R("kt", 0, 72, 2), [[0, 3], [8, 2], [0, 6]], 0)
-            iota(R("kt", 1, 72, 4), [[0, 3], [-16, 2], [0, 3]], 8)
+            act(R("bc", 36, 72), R("bc", 36, 72), scale=1.0 / 2048)
+            act(entry("tc", 3, 1), entry("tc", 3, 1), bias=col(0))
+            act(entry("ta", 3, 1), entry("tc", 3, 1), bias=96.0)
+            act(entry("tv", 0, 1), entry("tu", 2, 1), scale=-1.0)
             for y, (m0, m1) in enumerate(((1, -48), (0, -48), (-3, 48), (3, -48))):
                 pair("tm", y, m0, m1)
+            const(R("tm", 24, 32), 0)
             for y, (a0, a1) in enumerate(((-2, 96), (1, 0), (3, -48))):
                 pair("ta", y, a0, a1)
             const(entry("ta", 3, 0), -2)
-            const(R("tm", 24, 32), 0)
-            act(R("oh", 0, 96), (R("ow", 0, C), R("lu", 18, 24)))
-            act(R("oh", 96, 160), (R("ow", 0, C), R("lu", 28, 32)))
-            zeros(R("oh", 0, 90, 5))
-            zeros(R("oh", 96, 150, 3))
-        act(entry("kt", 3, 2 * r, 2), entry("qs", 3, 0, 2) if r else ow(0, 2))
+        if r == 1:
+            iota(R("kt", 0, 72, 2), [[0, 3], [8, 2], [0, 6]], 0)
+            iota(R("kt", 1, 72, 4), [[0, 3], [-16, 2], [0, 3]], 8)
+            copy(entry("kt", 3, 0, 2), ow(0, 2))
+        if r:
+            copy(entry("kt", 3, 2 * r, 2), entry("qs", 3, 0, 2))
         if r == 1:
             tables("qs", 0, 1)
-            tables("sq", 2, 1)
-            act(entry("t2", 3, 4), entry("qs", 3, 5))
+            copy(entry("t2", 3, 4), entry("qs", 3, 5))
+            act(R("oh", 0, 96), (R("ow", 0, C), R("lu", 20, 26)))
+            act(R("oh", 96, 160), (R("ow", 0, C), R("lu", 30, 34)))
+            const(R("oh", 0, 90, 5), 0)
+            const(R("oh", 96, 150, 3), 0)
             const(R("st", 0, 150), -1)
             for y in (2, 4):
                 const(R("st", y, 90, 5), -95)
             iota(R("st", 0, 90, 5), [[-32, 3], [0, 6]], -1)
             iota(R("st", 98, 150, 3), [[32, 3], [0, 6]], 193)
         if r == 2:
-            act(R("st", 96, 150, 3), R("so", 4, 90, 5))
-        order = [(b, h) for b in range(4) for h in range(2)] if r < 2 else [(b, h) for h in range(2) for b in range(4)]
-        half = ((0, H), (H, C)) if r < 2 else ((0, C - 128), (C - 128, C))
-        for a, e in half:
-            quant(R("zq", a, e), R("zs", a, e), R(z, 4 * a, 4 * e))
-            if r == 2 and a == 0:
-                received(2)
-        for b, h in order:
+            copy(R("st", 96, 150, 3), R("so", 4, 90, 5))
+        half = ((0, H), (H, C)) if r < 2 else ((0, CUT), (CUT, C))
+
+        def product(b, h):
             a, e = half[h]
-            if r == 2:
-                act(plane("z32", b, a, e), R(z, 4 * a + b, 4 * e, 4), scale=32.0)
-            elif h == 0:
-                act(plane("z32", b), R(z, b, 1152, 4), scale=32.0)
             mm(bank(4 - 4 * h + b, 0, e - a), R("wq", 128 * b, 128 * b + 128), R("wsc", 128 * b, 128 * b + 128), R("zq", a, e), R("zs", a, e))
-        if r < 2:
-            refused(r, 0)
-        else:
-            arrivals(1, 0)
 
-        def own_lists(k):
-            if k == 0:
-                horner(R("cs", 12, 36), flags(r), R("tf" if r else "tc", 0, 24))
-            elif k == 1:
-                horner(R("qs", 0, 24), flags(r), R("t2" if r else "tu", 0, 24))
-            elif r == 0:
-                horner(R("qs", 48, 72), flags(0), R("tv", 0, 24))
-            else:
-                horner(R("qs", 48, 60), R("fl", 48, 60), R("t2", 48, 60))
-
-        def outputs(h):
-            a, e = half[h]
-            quant(R("fq", a, e), R("fs", a, e), R("xf", 4 * a, 4 * e))
-            mm(bank(4 - 4 * h, 0, e - a), R("vq", 0, 128), R("vs", 0, 128), R("fq", a, e), R("fs", a, e))
-            dma("s", lambda: T.oc[:, 4 * a:4 * e], lambda: T.fq[:, a:e].bitcast(dt.uint8), [R("fq", a, e)], [])
-            act(R("yb", a, e), bank(4 - 4 * h, 0, e - a))
-            dma("a", lambda: T.y[:, a:e], lambda: T.yb[:, a:e], [R("yb", a, e)], [])
-
-        for n, (b, h) in enumerate(order):
+        def add(b, h):
             a, e = half[h]
             tt(plane("x32", b, a, e), bank(4 - 4 * h + b, 0, e - a), plane("z32", b, a, e), A.add)
-            if r == 2:
-                if h == 0:
-                    act(R("xf", b, 4 * e, 4), plane("x32", b, a, e), scale=2.0 ** -5)
-                if n == 0:
+
+        def scaled(q, o, a, x):
+            if q == "v":
+                ts(o, a, x, A.mult)
+            else:
+                act(o, a, scale=x)
+
+        if r == 2:
+            for step in LAST.split():
+                kind, h, b = step[:2], int(step[2:3] or 0), int(step[3:4] or 0)
+                a, e = half[h] if h < 2 else (0, C)
+                if kind == "qz":
+                    quant(R("zq", a, e), R("zs", a, e), R(z, 4 * a, 4 * e))
+                    for k in range(4):
+                        product(k, h)
+                elif kind == "rc":
+                    received(2)
+                elif kind == "ne":
+                    arrivals(1, 0)
+                elif kind == "so":
                     arrivals(1, 1)
-                    sel(R("skb", 0, 18), R("so", 98, 150, 3), [[0, 18]], A.is_ge, 0.0, 0, 0)
+                    copy(R("skb", 0, 18), R("so", 98, 150, 3))
                     for c in range(3):
                         dma("s", lambda c=c: T.sk[:, 96 * c:96 * c + 96], lambda c=c: T.skb[:, 6 * c:6 * c + 6], [R("skb", 0, 18)], [])
-                if n == 5:
-                    ts(R("xf", 4 * a, 4 * e, 4), plane("x32", 0, a, e), 2.0 ** -5, A.mult)
-                if n in (5, 6):
-                    act(R("xf", 4 * a + b, 4 * e, 4), plane("x32", b, a, e), scale=2.0 ** -5)
-                if n == 7:
-                    outputs(0)
-                    ts(R("xf", 4 * a + b, 4 * e, 4), plane("x32", b, a, e), 2.0 ** -5, A.mult)
-                    outputs(1)
-                continue
-            if n < 4:
-                refused(r, n + 1)
-            elif n < 7:
-                own_lists(n - 4)
-            if n == 3:
-                take("a", r + 1, 0)
-                take("a", r + 1, 1)
-            if n == 5:
-                take("a", r + 1, 2)
+                elif kind == "ad":
+                    add(b, h)
+                elif kind == "qx":
+                    quant(R("fq", a, e), R("fs", a, e), R("xf", 4 * a, 4 * e))
+                    mm(bank(4 - 4 * h, 0, e - a), R("vq", 0, 128), R("vs", 0, 128), R("fq", a, e), R("fs", a, e))
+                    a = 0 if WHOLE else a
+                    if h or not WHOLE:
+                        dma("s", lambda a=a, e=e: T.oc[:, 4 * a:4 * e], lambda a=a, e=e: T.fq[:, a:e].bitcast(dt.uint8), [R("fq", a, e)], [], 4 * (e - a))
+                elif kind[1] == "z":
+                    scaled(kind[0], plane("z32", b, a, e), R(z, 4 * a + b, 4 * e, 4), 32.0)
+                elif kind[1] == "x":
+                    scaled(kind[0], R("xf", 4 * a + b, 4 * e, 4), plane("x32", b, a, e), 2.0 ** -5)
+                else:
+                    scaled(kind[0], R("yb", a, e), bank(4 - 4 * h, 0, e - a), 1.0)
+                    a = 0 if WHOLE else a
+                    if h or not WHOLE:
+                        dma("a", lambda a=a, e=e: T.y[:, a:e], lambda a=a, e=e: T.yb[:, a:e], [R("yb", a, e)], [], 4 * (e - a))
+            break
+        order = [(b, h) for b in range(4) for h in range(2)]
+        steps = list(range(1 - r, 5))
+        for a, e in half:
+            refused(r, steps.pop(0))
+            quant(R("zq", a, e), R("zs", a, e), R(z, 4 * a, 4 * e))
+        for b, h in order:
+            if h == 0 and b not in ZV:
+                scaled("a", plane("z32", b), R(z, b, 1152, 4), 32.0)
+            product(b, h)
+        refused(r, steps.pop(0))
+        for n, (b, h) in enumerate(order):
+            if h == 0 and b in ZV:
+                scaled("v", plane("z32", b), R(z, b, 1152, 4), 32.0)
+            add(b, h)
+            if steps:
+                refused(r, steps.pop(0))
+            if n in (1, 3, 5):
+                take("a", r + 1, n // 2)
             if n == 7:
-                take("v", r + 1, 3)
+                take("v", r + 1, 3, SPLIT, 6)
+                if SPLIT:
+                    take("a", r + 1, 3, 0, SPLIT)
 
     for k in range(4):
-        dma("s", lambda k=k: T.osc[4 * k:4 * k + 4, :], lambda k=k: T.fs[32 * k:32 * k + 4, :], [R("fs", 0, C)], [])
+        dma(STORES[k], lambda k=k: T.osc[4 * k:4 * k + 4, :], lambda k=k: T.fs[32 * k:32 * k + 4, :], [R("fs", 0, C)], [])
 
     emit(g, T, ops)
     g.wait_ge(T.sem.left, sum(len(e) * (1 if name[0] == "f" else 2) for name, e in use.items()))

@@ -1,15 +1,21 @@
+from concourse.bass import DstId, RemoteDMATransfer
 from concourse.mybir import dt, AluOpType as A, ActivationFunctionType as F, AxisListType as AX
 
 C = 288
 H = 144
+SEG = 57
 LOW = 128
 SIGNS = (17, 16)
 EARLY = 1
-SHORT = (1, 2)
-BLEND = "f0 h0 r0 f1 h1 r1 v2 f2 r2 v3 f3 r3"
-LAST = ("qz0 rc qz1 az01 az02 az03 vz00 ne ad00 so ad01 ax00 ad02 ax01 ad03 ax02 vx03 vz10 vz11 qx0 vz12 vz13 "
+SHORT = (1, 2, 3)
+BLEND = "h0 h1 h2 h3 f0 f1 f2 f3"
+SECOND = ((0, 2), (2, 4))
+LAST = ("qz0 rc qz1 az01 az02 az03 vz00 ne ad00 so ad01 ax00 ad02 ax01 ad03 ax02 vx03 az10 az11 qx0 az12 az13 "
         "ad10 ad11 ay0 vx10 ad12 ax11 ad13 vx12 vx13 qx1 vy1")
 CUT = 160
+PARTS = True
+ROW2 = 2000
+CUTS = (144, 144, 144, 144)
 ZV = (0,)
 SPLIT = 2
 PLANES = 0
@@ -27,8 +33,8 @@ def _sb(n, d):
 SCRATCH = {
     "ub": _sb(512, BF), "vb": _sb(512, BF), "uq": _sb(128, Q4), "us": _sb(128, U8), "upq": _sb(256, Q4), "ups": _sb(256, U8),
     "vq": _sb(128, Q4), "vs": _sb(128, U8), "wq": _sb(512, Q4), "wsc": _sb(512, U8),
-    "zw0": _sb(3200, BF), "zw1": _sb(3200, BF), "zw2": _sb(3200, BF), "xf": _sb(1152, BF),
-    "x32": _sb(1152, BF), "z32": _sb(1152, BF), "lq": _sb(576, Q4), "ls": _sb(576, U8),
+    "zw0": _sb(5248, BF), "zw1": _sb(5248, BF), "zw2": _sb(5248, BF), "xf": _sb(1152, BF),
+    "x32": _sb(1152, BF), "z32": _sb(1152, BF), "lq": _sb(1248, Q4), "ls": _sb(1248, U8),
     "xq": _sb(C, Q4), "xs": _sb(C, U8), "zq": _sb(C, Q4), "zs": _sb(C, U8), "fq": _sb(C, Q4), "fs": _sb(C, U8),
     "tt": _sb(512, BF), "tq": _sb(384, Q4), "ts": _sb(384, U8),
     "zero": _sb(512, BF), "et": _sb(516, BF), "eq": _sb(512, Q4), "es": _sb(512, U8),
@@ -40,22 +46,33 @@ SCRATCH = {
     "r16": _sb(C, F32), "e16": _sb(C, F32), "m16": _sb(C, F32), "d16": _sb(C, F32), "h0": _sb(C, BF), "d1": _sb(48, F32),
     "mm": _sb(C, F32), "hh": _sb(C, F32), "rs": _sb(18, F32), "rc": _sb(18, F32), "ra": _sb(18, F32), "cx": _sb(C, F32),
     "plu": _sb(18, U16), "ij": _sb(C, F32), "orep": _sb(C, F32), "ow": _sb(C, F32),
-    "lf": _sb(552, F32), "lx": _sb(544, F32), "lu": _sb(34, U16),
-    "tl": _sb(18, U16), "wl": _sb(12, U16), "xl": _sb(24, U16), "sl": _sb(12, U16),
-    "bc": _sb(72, F32), "tg": _sb(32, F32), "zo": _sb(24, F32), "zl": _sb(24, U16),
+    "lf": _sb(584, F32), "lx": _sb(576, F32), "lu": _sb(36, U16),
+    "tl": _sb(18, U16), "wl": _sb(12, U16), "xl": _sb(24, U16), "sl": _sb(14, U16),
+    "bc": _sb(72, F32), "tg": _sb(32, F32), "zo": _sb(24, F32), "zl": _sb(32, U16),
     "s1": _sb(C, F32), "bm": _sb(96, F32), "ref": _sb(96, F32), "sc": _sb(96, F32), "dsc": _sb(96, F32),
     "th": _sb(56, F32), "fl": _sb(144, BF), "fa": _sb(32, BF), "xc": _sb(384, BF), "dh": _sb(576, BF), "val": _sb(384, BF),
     "tu": _sb(48, F32), "tv": _sb(24, F32), "tc": _sb(24, F32), "kt": _sb(72, F32), "t2": _sb(60, F32),
     "ta": _sb(24, F32), "tm": _sb(32, F32), "tp": _sb(32, F32), "tf": _sb(24, F32),
     "qs": _sb(72, F32), "sq": _sb(48, F32), "cs": _sb(48, F32), "kw": _sb(104, F32),
     "oh": _sb(160, F32), "ne": _sb(160, F32), "st": _sb(150, F32), "so": _sb(150, F32), "skb": _sb(18, F32), "yb": _sb(C, F32),
-    "ps": ("psum", [128, 4096], F32),
+    "ps": ("psum", [128, 4096], F32), "rb": ("sbuf", [128, 3, SEG], F32),
+    "rd": _sb(3 * SEG, F32), "ro": _sb(3 * SEG, F32), "gs": _sb(6, F32), "bh": _sb(48, F32), "mh": _sb(48, F32),
 }
-CYCLE, PE, SCALAR, SCATTER, WAKE, LOCAL, REMOTE = 0.87, 1.15, 15.0, 2.5, 180.0, 900.0, 1100.0
+CYCLE, PE, SCALAR, SCATTER, WAKE, LOCAL, REMOTE = 0.87, 1.15, 15.0, 2.5, 180.0, 900.0, 900.0
+BARS = 1200.0
+SKROW = 4000
+PULL, NEAR = 0.0, 150.0
+HINT, LASTC = 1, 0
+TWO = True
+FUSED = False
+FENCE = ("ta0",)
+CASES = ((1.0, 0.72, 1.0, 1.8), (1.0, 1.0, 1.0, 1.1), (1.25, 1.05, 1.7, 1.8), (1.05, 0.85, 1.2, 0.7))
+MOVES, GAIN = 8000, 1.0
 HOLD = {"local": 300.0, "remote": 300.0, "first": 2700.0}
-GRAIN, SLACK, LATE = 100.0, 20.0, 5000.0
+GRAIN, SLACK, LATE = 100.0, 20.0, 3500.0
 STORES = "ssaa"
-PASSES = 6
+PASSES, SHAKE = 3, 0.0
+BACK = "aavv"
 WHOLE = True
 POOL = {"v": 40, "a": 30, "p": 16, "g": 20}
 NDMA = 30
@@ -74,6 +91,8 @@ def bank(k, a=0, b=C):
 def bits(r):
     if r[0] == "ps":
         return 1 << (r[1] // 512)
+    if r[0] == "rb":
+        return sum(((1 << r[2]) - (1 << r[1])) << SEG * c for c in range(3) if r[3] in (0, c + 1))
     m = 0
     for c in range(r[1], r[2], r[3]):
         m |= 1 << c
@@ -104,6 +123,15 @@ def arrange(ops):
             e = ops[k]
             if e["sent"] and any(e["sent"] == name for name, _ in o["ext"]):
                 mine.append((k, e["lat"]))
+            elif o["dma"] and e["dma"] and o["q"] == e["q"] and any(wr for _, wr in o["use"].values()):
+                mine.append((k, (e["lat"] + WAKE if clash(o, e) else 0.0)))
+                continue
+            elif o["q"] == e["q"] == "g" and (o["sent"] == "uc" or e["sent"] in FENCE) and not clash(o, e):
+                mine.append((k, 0.0))
+                continue
+            elif o["q"] == e["q"] and o["stage"] > e["stage"] > 0 and not clash(o, e):
+                mine.append((k, 0.0))
+                continue
             elif o["acc"] and e["q"] == "p" and o["use"]["ps"][1] & e["use"]["ps"][1] and not have >> k & 1:
                 mine.append((k, 0.0))
             elif not have >> k & 1 and clash(o, e):
@@ -155,28 +183,113 @@ def arrange(ops):
             start[i] = t
         return start
 
-    best = (max(end[i] + ops[i]["lat"] for i in range(n)), order)
-    for _ in range(PASSES):
-        back = place(sorted(range(n), key=lambda i: (-end[i], -i)), succ, [o["lat"] for o in ops])
-        turn = sorted(range(n), key=lambda i: (-back[i] - ops[i]["cost"], i))
-        start = place(turn, pred, [0.0] * n)
+    def by(key):
+        key = list(key)
+        for i in range(n):
+            for k, _ in pred[i]:
+                key[i] = min(key[i], key[k] - 1e-3)
+        return sorted(range(n), key=lambda i: -key[i])
+
+    best = (max(end[i] + ops[i]["lat"] for i in range(n)), order, end)
+    seed = 1
+    for p in range(PASSES):
+        back = place(sorted(range(n), key=lambda i: (-best[2][i], -i)), succ, [o["lat"] for o in ops])
+        key, at = [], p * 1700.0 % best[0]
+        for i in range(n):
+            seed = seed * 48271 % 2147483647
+            key.append(back[i] + ops[i]["cost"] + (SHAKE * seed / 2147483647 if p and at <= best[2][i] < at + 2500.0 else 0.0))
+        start = place(by(key), pred, [0.0] * n)
         end = {i: start[i] + ops[i]["cost"] for i in range(n)}
         span = max(end[i] + ops[i]["lat"] for i in range(n))
-        if span < best[0]:
-            best = (span, sorted(range(n), key=lambda i: (start[i], i)))
-    return best[1]
+        if span <= best[0]:
+            best = (span, sorted(range(n), key=lambda i: (start[i], i)), end)
+    cases = []
+    for fast, pe, scatter, far in CASES:
+        cost = [o["cost"] * (1.0 if o["dma"] or o["sent"] else fast * (pe if o["q"] == "p" else scatter if o["scatter"] else 1.0)) for o in ops]
+        cases.append((cost, [[(k, gap * far if ops[k]["sent"] and gap > WAKE else gap) for k, gap in pred[i]] for i in range(n)]))
+    queue = ["vapgs".index(o["q"]) for o in ops]
+
+    def spans(order):
+        total = 0.0
+        for cost, before in cases:
+            free, end, last = [0.0] * 5, [0.0] * n, 0.0
+            for i in order:
+                t = free[queue[i]]
+                for k, gap in before[i]:
+                    if end[k] + gap > t:
+                        t = end[k] + gap
+                free[queue[i]] = end[i] = t = t + cost[i]
+                if ops[i]["dma"] and t + ops[i]["lat"] > last:
+                    last = t + ops[i]["lat"]
+            total += last + sum(end[i] * w for i, w in urgent)
+        return total
+
+    back = place(sorted(range(n), key=lambda i: (-best[2][i], -i)), succ, [o["lat"] for o in ops])
+    urgent = [(i, PULL) for i in range(n) if best[0] - back[i] - best[2][i] < NEAR]
+
+    def merged(lines):
+        order, done, at, moved = [], [False] * n, [0] * 5, True
+        while moved:
+            moved = False
+            for q in range(5):
+                while at[q] < len(lines[q]) and all(done[k] for k, _ in pred[lines[q][at[q]]]):
+                    done[lines[q][at[q]]] = moved = True
+                    order.append(lines[q][at[q]])
+                    at[q] += 1
+        return order if len(order) == n else None
+
+    def blocked(order):
+        found = []
+        for cost, before in cases:
+            free, ahead, end, why = [0.0] * 5, [None] * 5, [0.0] * n, [None] * n
+            for i in order:
+                t, why[i] = free[queue[i]], (ahead[queue[i]], True)
+                for k, gap in before[i]:
+                    if end[k] + gap > t:
+                        t, why[i] = end[k] + gap, (k, False)
+                free[queue[i]] = end[i] = t + cost[i]
+                ahead[queue[i]] = i
+            i = max(range(n), key=lambda k: end[k] + ops[k]["lat"] if ops[k]["dma"] else 0.0)
+            while i is not None:
+                if why[i][1] and why[i][0] is not None:
+                    found += [(i, -1), (why[i][0], 1), (why[i][0], -1)]
+                i = why[i][0]
+        return found
+
+    order, tight = best[1], []
+    lines = [[i for i in order if queue[i] == q] for q in range(5)]
+    now = spans(order)
+    for _ in range(MOVES):
+        seed = seed * 48271 % 2147483647
+        if not tight:
+            tight = blocked(order)
+        i, way = tight[seed % len(tight)] if seed % 3 else (seed % n, 1 - 2 * (seed // n % 2))
+        line = lines[queue[i]]
+        a = line.index(i)
+        e = a + way * (1, 1, 2, 3, 4, 6, 9, 14)[seed // (2 * n) % 8]
+        if not 0 <= e < len(line) or any(reach[max(i, k)] >> min(i, k) & 1 for k in line[min(a, e):max(a, e) + 1] if k != i):
+            continue
+        lines[queue[i]] = line[:a] + line[a + 1:]
+        lines[queue[i]].insert(e, i)
+        other = merged(lines)
+        span = spans(other) if other else now + 1.0
+        if span < now - GAIN:
+            order, now, tight = other, span, []
+        else:
+            lines[queue[i]] = line
+    return order
 
 
-PLAN = []
+PLAN = {}
 
 
-def emit(g, T, ops):
+def emit(g, T, ops, near):
     queue = {"v": g.vector, "a": g.scalar, "p": g.tensor, "g": g, "s": g.sync}
-    if not PLAN:
-        PLAN.append(arrange(ops))
-        PLAN.append(waits_of([ops[i] for i in PLAN[0]]))
-    ops = [ops[i] for i in PLAN[0]]
-    waits = PLAN[1]
+    if near not in PLAN:
+        order = arrange(ops)
+        PLAN[near] = (order, waits_of([ops[i] for i in order]))
+    ops = [ops[i] for i in PLAN[near][0]]
+    waits = PLAN[near][1]
     wanted, seen = {k for mine in waits for k in mine}, {q: set() for q in queue}
     sem, count, turn, ndma = {}, {}, {q: 0 for q in POOL}, 0
     for n, o in enumerate(ops):
@@ -227,6 +340,8 @@ def waits_of(ops):
 
 
 def size(r):
+    if r[0] == "rb":
+        return (r[2] - r[1]) * (1 if r[3] else 3)
     return 16 * (r[1][2] - r[1][1]) if len(r) == 2 else len(range(r[1], r[2], r[3]))
 
 
@@ -266,11 +381,17 @@ def rank_program(g, core, T, topo):
         common &= set(topo.engines(T.cores[k], T.cores[(k + 1) % n_ranks])) & set(topo.engines(T.cores[(k + 1) % n_ranks], T.cores[k]))
     common = sorted(common)
     use = {name: common for name in ("ta0", "ta1", "ta2", "fa0", "fa1", "uc")}
-    ops = []
+    coming = len(common)
+    near = True
+    ops, stage = [], [0]
 
     def ap(r):
         if len(r) == 2:
             return ap(r[0]).indirect(ap(r[1]))
+        if r[0] == "rb":
+            if r[3]:
+                return T.rb[:, r[3] - 1, r[1]:r[2]]
+            return T.rb[:, :, r[1]] if r[2] == r[1] + 1 else T.rb[:, :, r[1]:r[2]]
         if r[3] == 1:
             return T[r[0]][:, r[1]:r[2]]
         return T[r[0]][:, r[1]:r[2]:r[3]]
@@ -288,7 +409,8 @@ def rank_program(g, core, T, topo):
                 for p, side in parts:
                     u = use.setdefault(p[0], [0, 0])
                     u[side] |= bits(p)
-        ops.append({"q": q, "fn": fn, "use": use, "ext": ext, "dma": dma, "acc": acc, "lat": lat, "sent": sent,
+        ops.append({"q": q, "fn": fn, "use": use, "ext": ext, "dma": dma, "acc": acc, "lat": lat, "sent": sent, "stage": stage[0],
+                    "scatter": bool(writes) and len(writes[0]) == 2,
                     "cost": cost_of(q, kind, reads, writes)})
 
     def tt(o, a, b, f, ext=()):
@@ -364,12 +486,23 @@ def rank_program(g, core, T, topo):
         rid, pid, _ = topo.addr(to)
         mask = sum(1 << e for e in use[sem])
         kind = "remote" if any(e["sent"] for e in ops) else "first"
-        lat = LATE if sem == "uc" else REMOTE
+        lat = LATE if sem == "uc" else BARS if sem[0] == "f" else REMOTE
         if codes:
             op("g", lambda q: q.remote_dma(ap(o).bitcast(dt.uint8), ap(a).bitcast(dt.uint8), T.sem[sem], T.sem.left, pid, rid, mask), [a], [],
                kind=kind, lat=lat, sent=sem)
         else:
             op("g", lambda q: q.remote_dma(ap(o), ap(a), T.sem[sem], T.sem.left, pid, rid, mask), [a], [], kind=kind, lat=lat, sent=sem)
+
+    def send_tile(r, land):
+        rid, pid, _ = topo.addr(nxt)
+        sem = "ta%d" % r
+        share = len(use[sem]) // 4
+        sides = [(T.lq[:, land + 32 * k:land + 32 * k + 32].bitcast(dt.uint8), T.tq[:, 128 * r + 32 * k:128 * r + 32 * k + 32].bitcast(dt.uint8))
+                 for k in range(3)] + [(T.ls[:, land:land + 128], T.ts[:, 128 * r:128 * r + 128])]
+        parts = [RemoteDMATransfer(dst_ids=[DstId(rid=rid, pnc=pid)], dma_engine_mask=sum(1 << e for e in use[sem][share * k:share * k + share]),
+                                   remote_sem=T.sem[sem], src=a, dst=o) for k, (o, a) in enumerate(sides)]
+        op("g", lambda q: q.remote_dma_fused(parts, local_sem=T.sem.left), [R("tq", 128 * r, 128 * r + 96), R("ts", 128 * r, 128 * r + 128)], [],
+           kind="remote", lat=REMOTE + HOLD["remote"], sent=sem)
 
     def col(k):
         return R("col", k, k + 1)
@@ -386,7 +519,11 @@ def rank_program(g, core, T, topo):
     zw = ["zw0", "zw1", "zw2"]
 
     dma("a", lambda: T.ub[:], lambda: T.u[:], [], [R("ub", 0, 512)], 1024)
-    dma("s", lambda: T.zw0[:, 0:4 * C], lambda: T.x[:], [], [R("zw0", 0, 4 * C)], 3300)
+    if PARTS:
+        dma("s", lambda: T.zw0[:, 640:4 * C], lambda: T.x[:, 640:4 * C], [], [R("zw0", 640, 4 * C)], 1900)
+        dma("s", lambda: T.zw0[:, 0:640], lambda: T.x[:, 0:640], [], [R("zw0", 0, 640)], ROW2)
+    else:
+        dma("s", lambda: T.zw0[:, 0:4 * C], lambda: T.x[:], [], [R("zw0", 0, 4 * C)], 3300)
 
     iota(R("pi", 0, 1), [[0, 1]], 0, 1)
     iota(R("upi", 0, 16), [[1, 2], [16, 8]], 0)
@@ -404,7 +541,7 @@ def rank_program(g, core, T, topo):
         iota(R("rc", c, e), [[step, e - c]], rc[c])
         c = e
     iota(R("ij", 0, C), [[1, C]], 0)
-    dma("s", lambda: T.wq[:].bitcast(dt.uint8), lambda: T.wc[:], [R("zw0", 1151, 1152)], [R("wq", 0, 512)])
+    dma("s", lambda: T.wq[:].bitcast(dt.uint8), lambda: T.wc[:], [R("zw0", 0, 1)], [R("wq", 0, 512)])
     dma("s", lambda: T.wsc[:], lambda: T.ws[:], [], [R("wsc", 0, 512)])
     dma("s", lambda: T.vb[:], lambda: T.v[:], [], [R("vb", 0, 512)])
     fill(R("h0", 0, 160), BIG)
@@ -430,7 +567,7 @@ def rank_program(g, core, T, topo):
     act(R("m16", 0, 160), R("e16", 0, 160), scale=2 * BIG)
     act(col(2), col(0), scale=-K, bias=-3 * K)
     act(R("dk", 0, 160), R("e16", 0, 160), scale=18 * K, bias=8 * K)
-    fill(R("lf", 48, 128), 0.0)
+    fill(R("lf", 24, 128), 0.0)
     fill(R("tt", 384, 512), 0.0)
     fill(R("rs", 0, 1), 0.0)
     for t in range(4):
@@ -449,7 +586,9 @@ def rank_program(g, core, T, topo):
     def pick_u(k):
         pick(R("upq", 128 * k, 128 * k + 128), R("ups", 128 * k, 128 * k + 128), R("uq", 0, 128), R("us", 0, 128), R("upl", 8 * k, 8 * k + 8))
 
+    stage[0] = HINT
     pick_u(0)
+    stage[0] = 0
     u0, u1 = (R("upq", 0, 128), R("ups", 0, 128)), (R("upq", 128, 256), R("ups", 128, 256))
 
     def slot(n, t, w, low=0):
@@ -486,76 +625,93 @@ def rank_program(g, core, T, topo):
 
     def signs(blocks, k):
         for c in blocks:
-            act(slot(*where[c], 16 * c + 16), bank(k, 0, 16 * c + 16), scale=-1.0, bias=own_score(c))
+            if TWO:
+                act(slot(*where[c], 16 * c + 16, 160), bank(5, 0, 16 * c - 144), scale=-1.0, bias=own_score(c))
+                act(slot(*where[c], 160), bank(k, 0, 160), scale=-1.0, bias=own_score(c))
+            else:
+                act(slot(*where[c], 16 * c + 16), bank(k, 0, 16 * c + 16), scale=-1.0, bias=own_score(c))
         for c in blocks:
             n, t = where[c]
             act(slot(n, t, 16 * c), slot(n, t, 16 * c), scale=-1.0, bias=TINY, accum=R("rs", c, c + 1), f=F.Sign)
             act(slot(n, t, 16 * c + 16, 16 * c), slot(n, t, 16 * c + 16, 16 * c), scale=-1.0, bias=TINY, f=F.Sign)
 
+    for at in (0, 12):
+        iota(R("lf", at, at + 12), [[SEG, 3], [0, 2], [20, 2]], 16)
+    iota(R("lf", 32, 56), [[1, 4], [37, 2], [SEG, 3]], 16)
+    iota(R("lf", 64, 88), [[0, 4], [48, 2], [16, 3]], 15)
+    for at in (96, 108):
+        iota(R("lf", at, at + 12), [[1, 3], [0, 2], [3, 2]], 0)
+    iota(R("bc", 0, 36), [[1, 6], [0, 6]], 2048)
     pick(R("ucq", 0, 16), R("ucs", 0, 16), R("uq", 0, 128), R("us", 0, 128), R("upl", 24, 25))
     send(prv, R("unq", 0, 16), R("ucq", 0, 16), "uc", codes=True)
     send(prv, R("uns", 0, 16), R("ucs", 0, 16), "uc")
-    pick_u(1)
     act(R("dk", 15, 160, 16), R("dk", 15, 160, 16), bias=col(2))
     act(R("d16", 0, 160), R("dk", 0, 160))
     act(R("d16", 160, C), R("dk", 0, C - 160))
     act(R("ra", 0, 18), R("rc", 0, 18), bias=R("dk", 15, 16))
     low = C - 128
+    stage[0] = 2 * HINT
     quant(R("lq", low, C), R("ls", low, C), R("zw0", 4 * low, 4 * C))
     mm(bank(4, 0, 128), u0[0], u0[1], R("lq", low, C), R("ls", low, C))
+    stage[0] = 3 * HINT
+    if TWO:
+        mm(bank(5, 0, 128), u0[0], u0[1], R("lq", low, C), R("ls", low, C))
     quant(R("lq", 0, low), R("ls", 0, low), R("zw0", 0, 4 * low))
+    stage[0] = 4 * HINT
     mm(bank(0), u0[0], u0[1], R("lq", 0, C), R("ls", 0, C))
-    mm(bank(3), u0[0], u0[1], R("lq", 0, C), R("ls", 0, C))
+    if TWO:
+        mm(bank(3, 0, low), u0[0], u0[1], R("lq", 0, low), R("ls", 0, low))
+    else:
+        mm(bank(3), u0[0], u0[1], R("lq", 0, C), R("ls", 0, C))
+    stage[0] = 0
     tt(R("mm", low, C), bank(4, 0, 128), R("m16", 0, 128), A.min)
     scan(R("hh", low, C), R("h0", 0, 128), R("mm", low, C), -BIG, A.min, A.max)
+    tt(slot(0, 0, C, low), bank(4, 0, 128), R("hh", low, C), A.not_equal)
     signs(SIGNS, 3)
     tt(R("mm", 0, low), bank(0, 0, low), R("m16", 0, low), A.min)
     for c in range(17, -1, -1):
         if c not in SIGNS:
+            stage[0] = 5 * HINT * (c == LASTC)
             compare(c)
+            stage[0] = 0
             if c:
                 row_sum(c)
         if c == 15:
             scan(R("hh", 0, low), R("h0", 0, low), R("mm", 0, low), -BIG, A.min, A.max)
         if c == 14:
-            tt(slot(0, 0, C), bank(0), R("hh", 0, C), A.not_equal)
+            tt(slot(0, 0, low), bank(0, 0, low), R("hh", 0, low), A.not_equal)
         if c in (10, 6, 2):
             pack((10 - c) // 4)
             column_sums((10 - c) // 4)
     for n in (3, 4):
         pack(n)
         column_sums(n)
+    stage[0] = 6 * HINT
+    pick_u(1)
+    stage[0] = 0
     mm(bank(1), u1[0], u1[1], R("lq", 0, C), R("ls", 0, C))
     for c in SHORT:
         short_sum(c)
     act(R("ij", 0, C), R("ij", 0, C), scale=1.0 / 512)
-    iota(R("lf", 0, 24), [[0, 2], [32, 3], [0, 4]], 31)
-    iota(R("lf", 24, 48), [[0, 8], [32, 3]], 31)
-    iota(R("lf", 64, 88), [[0, 4], [48, 2], [16, 3]], 15)
-    for at in (96, 108):
-        iota(R("lf", at, at + 12), [[1, 3], [0, 2], [3, 2]], 0)
-    iota(R("bc", 0, 36), [[1, 6], [0, 6]], 2048)
-    iota(R("th", 0, 24), [[0, 6], [-1, 4]], 4)
-    iota(R("th", 24, 48), [[0, 4], [-1, 2], [0, 3]], 2)
-    const(R("lf", 128, 224), 3)
-    iota(R("lf", 128, 152), [[48, 2], [0, 4], [4, 3]], 3)
-    iota(R("lf", 160, 184), [[12, 2], [0, 4], [4, 3]], 3)
-    iota(R("lf", 192, 216), [[0, 2], [4, 3], [0, 4]], 15)
-    for at, n in ((224, 5), (416, 3)):
-        iota(R("lf", at, at + 24 * n), [[4, 4], [0, 6], [12, n]], 3)
-        iota(R("lf", at + 16 * n + 16, at + 40 * n + 16), [[16, 4], [48, 6], [0, n]], 15)
     act(R("d1", 0, 48), R("dk", 0, 48), scale=1.0 / K)
     for b in range(PLANES, 4):
         act(plane("x32", b), R("zw0", b, 1152, 4), scale=32.0)
     act(R("s1", 0, C), bank(1))
     tt(R("d16", 15, C, 16), R("ra", 0, 18), R("rs", 0, 18), A.subtract)
-    fill(R("dsc", 0, 96), 1.0)
-    pick_own(R("cx", 0, C), bank(2), R("d16", 0, C))
-    ts(R("dsc", 1, 96, 2), R("e16", 0, 48), 1.5, A.add)
-    ts(R("plu", 0, 18), R("cx", 15, C, 16), K, A.add, -0.5, A.mult)
-    fill(R("dsc", 0, 96, 32), 0.0)
-    cp((R("orep", 0, C), R("plu", 0, 18)), R("ij", 0, C))
+    stage[0] = 6
+    fill(R("rd", 0, 3 * SEG), 1.0)
+    fill(R("rd", 0, 3 * SEG, SEG), 0.0)
+    fill(R("rb", 0, SEG, 0), 0.0)
+    for at in (17, 54):
+        fill(R("rb", at, at + 3, 0), 1.0 / 2048)
     fill(R("tu", 0, 48), 0.0)
+    for b in range(4):
+        unpacker(b)
+    quant(R("vq", 0, 128), R("vs", 0, 128), R("vb", 0, 512))
+    stage[0] = 0
+    pick_own(R("cx", 0, C), bank(2), R("d16", 0, C))
+    ts(R("plu", 0, 18), R("cx", 15, C, 16), K, A.add, -0.5, A.mult)
+    cp((R("orep", 0, C), R("plu", 0, 18)), R("ij", 0, C))
     for k in range(2):
         pick_own(R("ow", 48 * k, 48 * k + 48), R("orep", k, C, 6), R("d1", 0, 48), 1.0)
     pick_own(R("ow", 96, 144), R("orep", 2, C, 6), R("d1", 0, 48), 1.0)
@@ -590,6 +746,10 @@ def rank_program(g, core, T, topo):
             tt(R("tg", 0, 32), (R("qs", 0, 64), R("lu", 8, 10)), R("bc", 36, 68), A.add)
             ts(R("xl", 0, 24), R("tg", 0, 24), 2048.0, A.mult)
             act(R("xc", 0, 384), (R(zw[r], 0, 1152), R("xl", 0, 24)), scale=0.5)
+        last, other = (9, 12) if r else (18, 3)
+        act(R("rb", 0, 1, 0), R("tg", 0, 3))
+        act(R("rb", 20, 21, 0), R("tg", last, last + 3), scale=-1.0)
+        act(R("rb", 37, 38, 0), R("tg", other, other + 3))
 
     def bars(r):
         scan(R("hb", 0, 96), R("h0", 0, 96), R("bm", 0, 96), -BIG, A.min, A.max)
@@ -635,7 +795,7 @@ def rank_program(g, core, T, topo):
     def arrivals(k, part):
         at, n = ((0, 5), (96, 3))[k]
         if part == 0:
-            tt(R("ne", at, at + 16 * n + 16), (R("kw", 64 * k, 64 * k + 12 * n + 4), R("lu", 14 + 12 * k, 15 + 12 * k + n)),
+            tt(R("ne", at, at + 16 * n + 16), (R("kw", 64 * k, 64 * k + 12 * n + 4), R("lu", 16 + 12 * k, 17 + 12 * k + n)),
                R("oh", at, at + 16 * n + 16), A.not_equal)
         else:
             horner(R("so", at, at + 18 * n), R("ne", at, at + 18 * n), R("st", at, at + 18 * n))
@@ -654,9 +814,13 @@ def rank_program(g, core, T, topo):
     for r in range(3):
         z = zw[r]
         quant(R("tq", 128 * r, 128 * r + 128), R("ts", 128 * r, 128 * r + 128), R("tt", 0, 512))
-        land = C + 96 * r
-        send(nxt, R("lq", land, land + 96), R("tq", 128 * r, 128 * r + 96), "ta%d" % r, codes=True)
-        send(nxt, R("ls", land, land + 96), R("ts", 128 * r, 128 * r + 96), "ta%d" % r)
+        own = (C + 128) * r
+        land = own + C
+        if FUSED:
+            send_tile(r, land)
+        else:
+            send(nxt, R("lq", land, land + 96), R("tq", 128 * r, 128 * r + 96), "ta%d" % r, codes=True)
+            send(nxt, R("ls", land, land + 96), R("ts", 128 * r, 128 * r + 96), "ta%d" % r)
         if r == 0:
             window = R("tl", 0, 6)
             act(R("bc", 0, 36), R("bc", 0, 36), scale=1.0 / 2048)
@@ -667,8 +831,6 @@ def rank_program(g, core, T, topo):
             offsets(0, 8)
             pick(R("upn", 0, 128), R("usn", 0, 128), R("unq", 0, 16), R("uns", 0, 16), R("upl", 16, 24), (("uc", 2 * len(use["uc"])),))
             targets(0)
-            for b in range(4):
-                unpacker(b)
             pick_own(R("ow", 240, C), R("orep", 5, C, 6), R("d1", 0, 48), 1.0)
             iota(R("tn", 0, 32), [[0, 8], [-1, 2], [0, 2]], 2)
             score_sent(0, 0)
@@ -677,8 +839,18 @@ def rank_program(g, core, T, topo):
             tt(entry("tu", 1, 0), ow(0), ow(1), A.subtract)
             tt(entry("tu", 0, 1, 3), ow(1, 3), ow(2, 3), A.subtract)
             tt(entry("tv", 1, 1), ow(2), ow(4), A.subtract)
-            lists(8, 34)
-            offsets(8, 34)
+            fill(R("lf", 128, 256), 3.0)
+            iota(R("lf", 128, 152), [[48, 2], [0, 4], [4, 3]], 3)
+            iota(R("lf", 160, 184), [[12, 2], [0, 4], [4, 3]], 3)
+            iota(R("lf", 192, 216), [[0, 2], [4, 3], [0, 4]], 15)
+            iota(R("lf", 224, 248), [[37, 2], [1, 4], [SEG, 3]], 16)
+            lists(8, 16)
+            offsets(8, 16)
+            for at, n in ((256, 5), (448, 3)):
+                iota(R("lf", at, at + 24 * n), [[4, 4], [0, 6], [12, n]], 3)
+                iota(R("lf", at + 16 * n + 16, at + 40 * n + 16), [[16, 4], [48, 6], [0, n]], 15)
+            lists(16, 36)
+            offsets(16, 36)
             act(entry("tu", 3, 0, 4), ow(2, 4))
             act(col(5), col(0), scale=2.0)
             act(col(6), col(0), scale=-2.0)
@@ -698,13 +870,16 @@ def rank_program(g, core, T, topo):
             copy(entry("tv", 1, 0), entry("tu", 2, 0))
         else:
             window = R("wl", 6 * r - 6, 6 * r)
-            for b in (3, 2, 1):
-                ts(R(z, b, 1152, 4), plane("x32", b), 2.0 ** -5, A.mult)
-            act(R(z, 0, 1152, 4), plane("x32", 0), scale=2.0 ** -5)
+            for b in range(4):
+                if BACK[b] == "v":
+                    ts(R(z, b, 1152, 4), plane("x32", b), 2.0 ** -5, A.mult)
+                else:
+                    act(R(z, b, 1152, 4), plane("x32", b), scale=2.0 ** -5)
             own_lists(r - 1, 1)
             for h in range(2):
-                quant(R("xq", H * h, H * h + H), R("xs", H * h, H * h + H), R(z, 4 * H * h, 4 * H * h + 4 * H))
-                mm(bank(h, 0, H), u1[0], u1[1], R("xq", H * h, H * h + H), R("xs", H * h, H * h + H))
+                a = own + H * h
+                quant(R("lq", a, a + H), R("ls", a, a + H), R(z, 4 * H * h, 4 * H * h + 4 * H))
+                mm(bank(h, 0, H), u1[0], u1[1], R("lq", a, a + H), R("ls", a, a + H))
                 act(R("s1", H * h, H * h + H), bank(h, 0, H))
             own_lists(r - 1, 2)
             columns(window, entry("qs", 3, 0, 2))
@@ -715,7 +890,10 @@ def rank_program(g, core, T, topo):
                 score_sent(r, 0)
                 bars(r)
                 score_sent(r, 1)
-            act(R("th", 24, 56), (R("cs", 0, 24), R("lu", 10, 12)))
+            ts(R("rd", 37, 3 * SEG, SEG), entry("cs", 3, 1), 1.0, A.is_le)
+            ts(R("gs", 0, 6, 2), entry("cs", 3, 1), 2.0, A.not_equal, -2 * BIG, A.mult)
+            tt(R("mh", 0, 48), (R("gs", 0, 6), R("upl", 16, 19)), R("m16", 0, 48), A.add)
+            tt(R("bh", 0, 48), (R("s1", 0, C), R("wl", 6 * r - 6, 6 * r - 3)), R("mh", 0, 48), A.min)
             tt(R("sf", 0, 16), (R("cs", 24, 48), R("lu", 10, 11)), R("sb", 0, 16), A.add)
             if r == 1:
                 horner(R("qs", 24, 48), flags(0), R("tu", 24, 48))
@@ -723,7 +901,11 @@ def rank_program(g, core, T, topo):
             else:
                 received(0)
                 received(1)
-            cp(R("sl", 0, 12), R("sf", 0, 12))
+            if SECOND[-1][0] == 3:
+                cp(R("sl", 0, 9), R("sf", 0, 9))
+                cp(R("sl", 10, 13), R("sf", 9, 12))
+            else:
+                cp(R("sl", 0, 12), R("sf", 0, 12))
         if r == 1:
             tables("sq", 2, 0)
             tables("sq", 2, 1)
@@ -736,9 +918,8 @@ def rank_program(g, core, T, topo):
             act(R("st", 0, 90, 5), R("st", 0, 90, 5), bias=col(6))
             act(R("st", 98, 150, 3), R("st", 98, 150, 3), bias=col(5))
             arrivals(0, 0)
-            quant(R("vq", 0, 128), R("vs", 0, 128), R("vb", 0, 512))
             arrivals(0, 1)
-        arrived = (("ta%d" % r, 2 * len(use["ta%d" % r])),)
+        arrived = (("ta%d" % r, (1 if FUSED else 2) * coming),)
         tq, tsc = R("lq", land - 32, land + 96), R("ls", land - 32, land + 96)
         mm(bank(3, 0, 128), u1[0], u1[1], tq, tsc, ext=arrived)
         for b in range(4):
@@ -748,27 +929,28 @@ def rank_program(g, core, T, topo):
             n = 48 if r else 96
             tt(R("val", n * b, n * b + n), bank(4 + b, 32, 32 + n), R("xc", n * b, n * b + n) if r else R("xc", b, 384, 4), A.add)
 
-        receipts = [lambda: horner(R("sc", 0, 96), R("dsc", 0, 96), R("ref", 0, 96)),
-                    lambda: tt(R("fl", 48 * r, 48 * r + 48), (R("sc", 0, 96), R("lu", 0, 3)), R("th", 0, 48), A.is_ge),
-                    lambda: tt(R("zo", 0, 24), R("fl", 48 * r + 24, 48 * r + 48), R("tg", 0, 24), A.add),
-                    lambda: ts(R("zl", 0, 24), R("zo", 0, 24), 2048.0, A.mult)]
         for i in range(2):
-            tt(R("ref", i, 96, 2), bank(3, 32 + 48 * i, 80 + 48 * i), R("bm", 48 * i, 48 * i + 48), A.is_lt)
-        for step in (BLEND if r else "f0 r0 f1 r1 f2 r2 f3 r3").split():
+            tt(R("rb", 1 + 20 * i, 17 + 20 * i, 0), bank(3, 32 + 48 * i, 80 + 48 * i), R("bm", 48 * i, 48 * i + 48), A.is_lt)
+        if r:
+            tt(R("rb", 38, 54, 0), bank(3, 32, 80), R("bh", 0, 48), A.is_lt)
+        for c in range(3):
+            horner(R("ro", SEG * c, SEG * c + SEG), R("rd", SEG * c, SEG * c + SEG), R("rb", 0, SEG, c + 1))
+        ts(R("zl", 0, 32), (R("ro", 0, 3 * SEG), R("lu", 14, 16) if r else R("lu", 2, 4)), 2048.0, A.mult)
+        tt(R("fl", 48 * r, 48 * r + 32), (R("ro", 0, 3 * SEG), R("lu", 0, 2)), R("tn", 0, 32), A.is_ge)
+        for step in (BLEND if r else "f0 f1 f2 f3").split():
             k = int(step[1])
             if step[0] == "f":
                 fresh(k)
             elif step[0] == "h":
                 hold(r, k)
-            elif step[0] == "v":
-                cp(R("dh", H * k + 48 * r, H * k + 48 * r + 48), bank(4 + k, 80, 128))
             else:
-                receipts[k]()
+                cp(R("dh", H * k + 48 * r, H * k + 48 * r + 48), bank(4 + k, 80, 128))
         if r:
-            tt(R("val", 192, 384), (R("dh", 0, 576), R("sl", 0, 12)), R("xc", 192, 384), A.add)
+            for a, e in SECOND:
+                tt(R("val", 192 + 48 * a, 192 + 48 * e), (R("dh", 0, H * e), R("sl", 3 * a + a % 2, 3 * e + a % 2)), R("xc", 192 + 48 * a, 192 + 48 * e), A.add)
         if r == 0:
             refused(0, 0)
-        cp((R(z, 0, 3200), R("zl", 0, 24)), R("val", 0, 384))
+        cp((R(z, 0, 5248), R("zl", 0, 24)), R("val", 0, 384))
         if r == 0:
             for b in range(4):
                 hold(0, b)
@@ -791,8 +973,8 @@ def rank_program(g, core, T, topo):
         if r == 1:
             tables("qs", 0, 1)
             copy(entry("t2", 3, 4), entry("qs", 3, 5))
-            act(R("oh", 0, 96), (R("ow", 0, C), R("lu", 20, 26)))
-            act(R("oh", 96, 160), (R("ow", 0, C), R("lu", 30, 34)))
+            act(R("oh", 0, 96), (R("ow", 0, C), R("lu", 22, 28)))
+            act(R("oh", 96, 160), (R("ow", 0, C), R("lu", 32, 36)))
             const(R("oh", 0, 90, 5), 0)
             const(R("oh", 96, 150, 3), 0)
             const(R("st", 0, 150), -1)
@@ -834,7 +1016,7 @@ def rank_program(g, core, T, topo):
                     arrivals(1, 1)
                     copy(R("skb", 0, 18), R("so", 98, 150, 3))
                     for c in range(3):
-                        dma("s", lambda c=c: T.sk[:, 96 * c:96 * c + 96], lambda c=c: T.skb[:, 6 * c:6 * c + 6], [R("skb", 0, 18)], [])
+                        dma("s", lambda c=c: T.sk[:, 96 * c:96 * c + 96], lambda c=c: T.skb[:, 6 * c:6 * c + 6], [R("skb", 0, 18)], [], SKROW)
                 elif kind == "ad":
                     add(b, h)
                 elif kind == "qx":
@@ -853,31 +1035,25 @@ def rank_program(g, core, T, topo):
                     if h or not WHOLE:
                         dma("a", lambda a=a, e=e: T.y[:, a:e], lambda a=a, e=e: T.yb[:, a:e], [R("yb", a, e)], [], 4 * (e - a))
             break
-        order = [(b, h) for b in range(4) for h in range(2)]
-        steps = list(range(1 - r, 5))
-        for a, e in half:
-            refused(r, steps.pop(0))
+        for step in range(1 - r, 5):
+            refused(r, step)
+        for a, e in ((0, CUTS[0]), (CUTS[0], C)):
             quant(R("zq", a, e), R("zs", a, e), R(z, 4 * a, 4 * e))
-        for b, h in order:
-            if h == 0 and b not in ZV:
-                scaled("a", plane("z32", b), R(z, b, 1152, 4), 32.0)
-            product(b, h)
-        refused(r, steps.pop(0))
-        for n, (b, h) in enumerate(order):
-            if h == 0 and b in ZV:
-                scaled("v", plane("z32", b), R(z, b, 1152, 4), 32.0)
-            add(b, h)
-            if steps:
-                refused(r, steps.pop(0))
-            if n in (1, 3, 5):
-                take("a", r + 1, n // 2)
-            if n == 7:
-                take("v", r + 1, 3, SPLIT, 6)
-                if SPLIT:
-                    take("a", r + 1, 3, 0, SPLIT)
+        for b in range(4):
+            scaled("v" if b in ZV else "a", plane("z32", b), R(z, b, 1152, 4), 32.0)
+            half = ((0, CUTS[b]), (CUTS[b], C)) if CUTS[b] else ((0, C),)
+            for h in range(len(half)):
+                product(b, h)
+                add(b, h)
+            if b < 3:
+                take("a", r + 1, b)
+        if SPLIT < 6:
+            take("v", r + 1, 3, SPLIT, 6)
+        if SPLIT:
+            take("a", r + 1, 3, 0, SPLIT)
 
     for k in range(4):
         dma(STORES[k], lambda k=k: T.osc[4 * k:4 * k + 4, :], lambda k=k: T.fs[32 * k:32 * k + 4, :], [R("fs", 0, C)], [])
 
-    emit(g, T, ops)
-    g.wait_ge(T.sem.left, sum(len(e) * (1 if name[0] == "f" else 2) for name, e in use.items()))
+    emit(g, T, ops, near)
+    g.wait_ge(T.sem.left, sum(len(e) * (1 if name[0] == "f" or FUSED and name[0] == "t" else 2) for name, e in use.items()))

from concourse.bass import DstId, RemoteDMATransfer
from concourse.mybir import dt, AluOpType as A, ActivationFunctionType as F, AxisListType as AX

C = 288
H = 144
SEG = 57
LOW = 128
SIGNS = (17, 16)
EARLY = 1
SHORT = (1, 2, 3)
BLEND = "h0 h1 h2 h3 f0 f1 f2 f3"
SECOND = ((0, 2), (2, 4))
LAST = ("qz0 rc qz1 az01 az02 az03 vz00 ne ad00 so ad01 ax00 ad02 ax01 ad03 ax02 vx03 az10 az11 qx0 az12 az13 "
        "ad10 ad11 ay0 vx10 ad12 ax11 ad13 vx12 vx13 qx1 vy1")
CUT = 160
PARTS = True
ROW2 = 2000
CUTS = (144, 144, 144, 144)
ZV = (0,)
SPLIT = 2
PLANES = 0
PACK0 = 14
BIG = 1.0e29
TINY = 2.0 ** -100
K = 1024.0
Q4, U8, BF, F32, U16, I32 = "float8_e4m3fn_x4", "uint8", "bfloat16", "float32", "uint16", "int32"


def _sb(n, d):
    return ("sbuf", [128, n], d)


SCRATCH = {
    "ub": _sb(512, BF), "vb": _sb(512, BF), "uq": _sb(128, Q4), "us": _sb(128, U8), "upq": _sb(256, Q4), "ups": _sb(256, U8),
    "vq": _sb(128, Q4), "vs": _sb(128, U8), "wq": _sb(512, Q4), "wsc": _sb(512, U8),
    "zw0": _sb(5248, BF), "zw1": _sb(5248, BF), "zw2": _sb(5248, BF), "xf": _sb(1152, BF),
    "x32": _sb(1152, BF), "z32": _sb(1152, BF), "lq": _sb(1248, Q4), "ls": _sb(1248, U8),
    "xq": _sb(C, Q4), "xs": _sb(C, U8), "zq": _sb(C, Q4), "zs": _sb(C, U8), "fq": _sb(C, Q4), "fs": _sb(C, U8),
    "tt": _sb(512, BF), "tq": _sb(384, Q4), "ts": _sb(384, U8),
    "zero": _sb(512, BF), "et": _sb(516, BF), "eq": _sb(512, Q4), "es": _sb(512, U8),
    "og": _sb(128, BF), "ot": _sb(512, BF), "oq": _sb(128, Q4), "osq": _sb(128, U8),
    "bt": _sb(3840, BF), "bq": _sb(960, Q4), "bs": _sb(960, U8), "junk": _sb(2448, BF),
    "pi": _sb(4, I32), "pb": _sb(4, I32), "col": _sb(16, F32), "upi": _sb(16, I32), "upl": _sb(26, U16),
    "ucq": _sb(16, Q4), "ucs": _sb(16, U8), "unq": _sb(16, Q4), "uns": _sb(16, U8), "upn": _sb(128, Q4), "usn": _sb(128, U8),
    "hb": _sb(96, F32), "bo": _sb(16, F32), "bn": _sb(16, F32), "rf": _sb(6, F32), "tn": _sb(32, F32), "sf": _sb(16, F32), "sb": _sb(18, F32), "dk": _sb(160, F32), "ms": _sb(6, F32), "d6": _sb(6, F32),
    "r16": _sb(C, F32), "e16": _sb(C, F32), "m16": _sb(C, F32), "d16": _sb(C, F32), "h0": _sb(C, BF), "d1": _sb(48, F32),
    "mm": _sb(C, F32), "hh": _sb(C, F32), "rs": _sb(18, F32), "rc": _sb(18, F32), "ra": _sb(18, F32), "cx": _sb(C, F32),
    "plu": _sb(18, U16), "ij": _sb(C, F32), "orep": _sb(C, F32), "ow": _sb(C, F32),
    "lf": _sb(584, F32), "lx": _sb(576, F32), "lu": _sb(36, U16),
    "tl": _sb(18, U16), "wl": _sb(12, U16), "xl": _sb(24, U16), "sl": _sb(14, U16),
    "bc": _sb(72, F32), "tg": _sb(32, F32), "zo": _sb(24, F32), "zl": _sb(32, U16),
    "s1": _sb(C, F32), "bm": _sb(96, F32), "ref": _sb(96, F32), "sc": _sb(96, F32), "dsc": _sb(96, F32),
    "th": _sb(56, F32), "fl": _sb(144, BF), "fa": _sb(32, BF), "xc": _sb(384, BF), "dh": _sb(576, BF), "val": _sb(384, BF),
    "tu": _sb(48, F32), "tv": _sb(24, F32), "tc": _sb(24, F32), "kt": _sb(72, F32), "t2": _sb(60, F32),
    "ta": _sb(24, F32), "tm": _sb(32, F32), "tp": _sb(32, F32), "tf": _sb(24, F32),
    "qs": _sb(72, F32), "sq": _sb(48, F32), "cs": _sb(48, F32), "kw": _sb(104, F32),
    "oh": _sb(160, F32), "ne": _sb(160, F32), "st": _sb(150, F32), "so": _sb(150, F32), "skb": _sb(18, F32), "yb": _sb(C, F32),
    "ps": ("psum", [128, 4096], F32), "rb": ("sbuf", [128, 3, SEG], F32),
    "rd": _sb(3 * SEG, F32), "ro": _sb(3 * SEG, F32), "gs": _sb(6, F32), "bh": _sb(48, F32), "mh": _sb(48, F32),
}
CYCLE, PE, SCALAR, SCATTER, WAKE, LOCAL, REMOTE = 0.87, 1.15, 15.0, 2.5, 180.0, 900.0, 900.0
BARS = 1200.0
SKROW = 4000
PULL, NEAR = 0.0, 150.0
HINT, LASTC = 1, 0
TWO = True
FUSED = False
FENCE = ("ta0",)
CASES = ((1.0, 0.72, 1.0, 1.8), (1.0, 1.0, 1.0, 1.1), (1.25, 1.05, 1.7, 1.8), (1.05, 0.85, 1.2, 0.7))
MOVES, GAIN = 8000, 1.0
HOLD = {"local": 300.0, "remote": 300.0, "first": 2700.0}
GRAIN, SLACK, LATE = 100.0, 20.0, 3500.0
STORES = "ssaa"
PASSES, SHAKE = 3, 0.0
BACK = "aavv"
WHOLE = True
POOL = {"v": 40, "a": 30, "p": 16, "g": 20}
NDMA = 30
SEMAPHORES = (["%s%d" % (q, k) for q in POOL for k in range(POOL[q])] + ["d%d" % k for k in range(NDMA)]
              + ["ta0", "ta1", "ta2", "fa0", "fa1", "uc", "left"])


def R(name, a, b, s=1):
    return (name, a, b, s)


def bank(k, a=0, b=C):
    return ("ps", 512 * k + a, 512 * k + b, 1)


def bits(r):
    if r[0] == "ps":
        return 1 << (r[1] // 512)
    if r[0] == "rb":
        return sum(((1 << r[2]) - (1 << r[1])) << SEG * c for c in range(3) if r[3] in (0, c + 1))
    m = 0
    for c in range(r[1], r[2], r[3]):
        m |= 1 << c
    return m


def clash(o, e):
    for name, (rd, wr) in o["use"].items():
        if name in e["use"]:
            erd, ewr = e["use"][name]
            if name == "ps" and e["q"] != o["q"]:
                if (rd | wr) & (erd | ewr):
                    return True
            elif name == "ps" and o["q"] == "p":
                if wr & ewr and not o["acc"]:
                    return True
            elif wr & (erd | ewr) or rd & ewr:
                return True
    return False


def arrange(ops):
    n = len(ops)
    pred, reach = [], []
    for i, o in enumerate(ops):
        mine, have = [], 0
        for k in range(i - 1, -1, -1):
            e = ops[k]
            if e["sent"] and any(e["sent"] == name for name, _ in o["ext"]):
                mine.append((k, e["lat"]))
            elif o["dma"] and e["dma"] and o["q"] == e["q"] and any(wr for _, wr in o["use"].values()):
                mine.append((k, (e["lat"] + WAKE if clash(o, e) else 0.0)))
                continue
            elif o["q"] == e["q"] == "g" and (o["sent"] == "uc" or e["sent"] in FENCE) and not clash(o, e):
                mine.append((k, 0.0))
                continue
            elif o["q"] == e["q"] and o["stage"] > e["stage"] > 0 and not clash(o, e):
                mine.append((k, 0.0))
                continue
            elif o["acc"] and e["q"] == "p" and o["use"]["ps"][1] & e["use"]["ps"][1] and not have >> k & 1:
                mine.append((k, 0.0))
            elif not have >> k & 1 and clash(o, e):
                mine.append((k, (e["lat"] if e["dma"] else 0.0) + WAKE))
            else:
                continue
            have |= reach[k] | 1 << k
        pred.append(mine)
        reach.append(have)
    rest = [o["cost"] + o["lat"] for o in ops]
    for i in range(n - 1, -1, -1):
        for k, gap in pred[i]:
            rest[k] = max(rest[k], ops[k]["cost"] + gap + rest[i])
    free, end, order, left = {}, {}, [], list(range(n))
    while left:
        soon = {}
        for i in left:
            t = free.get(ops[i]["q"], 0.0)
            for k, gap in pred[i]:
                t = max(t, (end[k] if k in end else soon[k] + ops[k]["cost"]) + gap)
            soon[i] = t
        bound = max(soon[i] + rest[i] for i in left)
        ready = sorted((i for i in left if all(k in end for k, _ in pred[i])), key=lambda i: (soon[i] // GRAIN, -rest[i]))
        best = None
        for i in ready:
            stop = soon[i] + ops[i]["cost"]
            harm = max([stop + rest[u] - bound for u in left if u != i and ops[u]["q"] == ops[i]["q"] and soon[u] < stop and rest[u] > rest[i]] + [0.0])
            if best is None or harm < best[0]:
                best = (harm, i)
            if harm <= SLACK:
                break
        i = best[1]
        end[i] = free[ops[i]["q"]] = soon[i] + ops[i]["cost"]
        order.append(i)
        left.remove(i)
    succ = [[] for _ in ops]
    for i in range(n):
        for k, gap in pred[i]:
            succ[k].append((i, gap))

    def place(turn, before, lead):
        start, busy = {}, {}
        for i in turn:
            t, c = max([start[k] + ops[k]["cost"] + gap for k, gap in before[i]] + [lead[i]]), ops[i]["cost"]
            for a, e in sorted(busy.setdefault(ops[i]["q"], [])):
                if e > t and a < t + c:
                    t = e
            busy[ops[i]["q"]].append((t, t + c))
            start[i] = t
        return start

    def by(key):
        key = list(key)
        for i in range(n):
            for k, _ in pred[i]:
                key[i] = min(key[i], key[k] - 1e-3)
        return sorted(range(n), key=lambda i: -key[i])

    best = (max(end[i] + ops[i]["lat"] for i in range(n)), order, end)
    seed = 1
    for p in range(PASSES):
        back = place(sorted(range(n), key=lambda i: (-best[2][i], -i)), succ, [o["lat"] for o in ops])
        key, at = [], p * 1700.0 % best[0]
        for i in range(n):
            seed = seed * 48271 % 2147483647
            key.append(back[i] + ops[i]["cost"] + (SHAKE * seed / 2147483647 if p and at <= best[2][i] < at + 2500.0 else 0.0))
        start = place(by(key), pred, [0.0] * n)
        end = {i: start[i] + ops[i]["cost"] for i in range(n)}
        span = max(end[i] + ops[i]["lat"] for i in range(n))
        if span <= best[0]:
            best = (span, sorted(range(n), key=lambda i: (start[i], i)), end)
    cases = []
    for fast, pe, scatter, far in CASES:
        cost = [o["cost"] * (1.0 if o["dma"] or o["sent"] else fast * (pe if o["q"] == "p" else scatter if o["scatter"] else 1.0)) for o in ops]
        cases.append((cost, [[(k, gap * far if ops[k]["sent"] and gap > WAKE else gap) for k, gap in pred[i]] for i in range(n)]))
    queue = ["vapgs".index(o["q"]) for o in ops]

    def spans(order):
        total = 0.0
        for cost, before in cases:
            free, end, last = [0.0] * 5, [0.0] * n, 0.0
            for i in order:
                t = free[queue[i]]
                for k, gap in before[i]:
                    if end[k] + gap > t:
                        t = end[k] + gap
                free[queue[i]] = end[i] = t = t + cost[i]
                if ops[i]["dma"] and t + ops[i]["lat"] > last:
                    last = t + ops[i]["lat"]
            total += last + sum(end[i] * w for i, w in urgent)
        return total

    back = place(sorted(range(n), key=lambda i: (-best[2][i], -i)), succ, [o["lat"] for o in ops])
    urgent = [(i, PULL) for i in range(n) if best[0] - back[i] - best[2][i] < NEAR]

    def merged(lines):
        order, done, at, moved = [], [False] * n, [0] * 5, True
        while moved:
            moved = False
            for q in range(5):
                while at[q] < len(lines[q]) and all(done[k] for k, _ in pred[lines[q][at[q]]]):
                    done[lines[q][at[q]]] = moved = True
                    order.append(lines[q][at[q]])
                    at[q] += 1
        return order if len(order) == n else None

    def blocked(order):
        found = []
        for cost, before in cases:
            free, ahead, end, why = [0.0] * 5, [None] * 5, [0.0] * n, [None] * n
            for i in order:
                t, why[i] = free[queue[i]], (ahead[queue[i]], True)
                for k, gap in before[i]:
                    if end[k] + gap > t:
                        t, why[i] = end[k] + gap, (k, False)
                free[queue[i]] = end[i] = t + cost[i]
                ahead[queue[i]] = i
            i = max(range(n), key=lambda k: end[k] + ops[k]["lat"] if ops[k]["dma"] else 0.0)
            while i is not None:
                if why[i][1] and why[i][0] is not None:
                    found += [(i, -1), (why[i][0], 1), (why[i][0], -1)]
                i = why[i][0]
        return found

    order, tight = best[1], []
    lines = [[i for i in order if queue[i] == q] for q in range(5)]
    now = spans(order)
    for _ in range(MOVES):
        seed = seed * 48271 % 2147483647
        if not tight:
            tight = blocked(order)
        i, way = tight[seed % len(tight)] if seed % 3 else (seed % n, 1 - 2 * (seed // n % 2))
        line = lines[queue[i]]
        a = line.index(i)
        e = a + way * (1, 1, 2, 3, 4, 6, 9, 14)[seed // (2 * n) % 8]
        if not 0 <= e < len(line) or any(reach[max(i, k)] >> min(i, k) & 1 for k in line[min(a, e):max(a, e) + 1] if k != i):
            continue
        lines[queue[i]] = line[:a] + line[a + 1:]
        lines[queue[i]].insert(e, i)
        other = merged(lines)
        span = spans(other) if other else now + 1.0
        if span < now - GAIN:
            order, now, tight = other, span, []
        else:
            lines[queue[i]] = line
    return order


PLAN = {}


def emit(g, T, ops, near):
    queue = {"v": g.vector, "a": g.scalar, "p": g.tensor, "g": g, "s": g.sync}
    if near not in PLAN:
        order = arrange(ops)
        PLAN[near] = (order, waits_of([ops[i] for i in order]))
    ops = [ops[i] for i in PLAN[near][0]]
    waits = PLAN[near][1]
    wanted, seen = {k for mine in waits for k in mine}, {q: set() for q in queue}
    sem, count, turn, ndma = {}, {}, {q: 0 for q in POOL}, 0
    for n, o in enumerate(ops):
        if o["dma"]:
            sem[n] = ("d%d" % ndma, 16, 16)
            ndma += 1
        elif n in wanted:
            name = "%s%d" % (o["q"], turn[o["q"]] % POOL[o["q"]])
            turn[o["q"]] += 1
            count[name] = count.get(name, 0) + 1
            sem[n] = (name, count[name], 1)
    for n, o in enumerate(ops):
        q = queue[o["q"]]
        for name, val in o["ext"]:
            if name not in seen[o["q"]]:
                seen[o["q"]].add(name)
                q.wait_ge(T.sem[name], val)
        for k in waits[n]:
            q.wait_ge(T.sem[sem[k][0]], sem[k][1])
        ins = o["fn"](q)
        if n in sem:
            ins.then_inc(T.sem[sem[n][0]], sem[n][2])
    for n, o in enumerate(ops):
        if o["dma"] and n not in wanted:
            queue[o["q"]].wait_ge(T.sem[sem[n][0]], 16)


def waits_of(ops):
    known_q = {q: 0 for q in "vapgs"}
    before, done = {q: 0 for q in "vapgs"}, []
    known, waits = [], []
    for n, o in enumerate(ops):
        deps = [k for k in range(n) if clash(o, ops[k])]
        have, mine = known_q[o["q"]], []
        for k in reversed(deps):
            if not have >> k & 1:
                mine.append(k)
                have |= known[k] | 1 << k
                if not ops[k]["dma"]:
                    have |= done[k]
        known_q[o["q"]] = have
        known.append(have)
        done.append(before[o["q"]])
        if not o["dma"]:
            before[o["q"]] |= 1 << n | have
        waits.append(mine)
    return waits


def size(r):
    if r[0] == "rb":
        return (r[2] - r[1]) * (1 if r[3] else 3)
    return 16 * (r[1][2] - r[1][1]) if len(r) == 2 else len(range(r[1], r[2], r[3]))


def cost_of(q, kind, reads, writes):
    if kind in HOLD:
        return HOLD[kind]
    out = writes[0]
    n = size(out)
    if kind == "quant":
        return 12 + 0.9 * n
    if q == "p":
        return (n + 16) * PE
    if q == "g":
        return 150 + 2 * CYCLE * n
    if len(out) == 2:
        return 50 + SCATTER * CYCLE * n
    if reads and len(reads[0]) == 2:
        return 60 + 1.56 * CYCLE * n
    if kind == "sum":
        n = size(reads[0])
    sides = [r[0] for r in [out] + list(reads) if isinstance(r, tuple) and size(r) == n]
    if kind == "pair" and "ps" not in sides:
        n *= 2
    if q == "v" and kind == "" and all(SCRATCH[s][2] in (BF, U16) for s in sides):
        n /= 2
    return max(64, n) * CYCLE + (SCALAR if q == "a" else 0)


def rank_program(g, core, T, topo):
    rank = T.rank_of(core)
    if rank is None:
        return
    n_ranks = len(T.cores)
    nxt, prv = T.cores[(rank + 1) % n_ranks], T.cores[(rank - 1) % n_ranks]
    common = set(topo.engines(T.cores[0], T.cores[1]))
    for k in range(n_ranks):
        common &= set(topo.engines(T.cores[k], T.cores[(k + 1) % n_ranks])) & set(topo.engines(T.cores[(k + 1) % n_ranks], T.cores[k]))
    common = sorted(common)
    use = {name: common for name in ("ta0", "ta1", "ta2", "fa0", "fa1", "uc")}
    coming = len(common)
    near = True
    ops, stage = [], [0]

    def ap(r):
        if len(r) == 2:
            return ap(r[0]).indirect(ap(r[1]))
        if r[0] == "rb":
            if r[3]:
                return T.rb[:, r[3] - 1, r[1]:r[2]]
            return T.rb[:, :, r[1]] if r[2] == r[1] + 1 else T.rb[:, :, r[1]:r[2]]
        if r[3] == 1:
            return T[r[0]][:, r[1]:r[2]]
        return T[r[0]][:, r[1]:r[2]:r[3]]

    def val(x):
        return ap(x) if isinstance(x, tuple) else x

    def op(q, fn, reads, writes, ext=(), dma=False, acc=False, kind="", lat=0.0, sent=None):
        use = {}
        for k, group in enumerate((reads, writes)):
            for r in group:
                if not isinstance(r, tuple):
                    continue
                parts = [(r, k)] if len(r) == 4 else [(r[0], k), (r[1], 0)]
                for p, side in parts:
                    u = use.setdefault(p[0], [0, 0])
                    u[side] |= bits(p)
        ops.append({"q": q, "fn": fn, "use": use, "ext": ext, "dma": dma, "acc": acc, "lat": lat, "sent": sent, "stage": stage[0],
                    "scatter": bool(writes) and len(writes[0]) == 2,
                    "cost": cost_of(q, kind, reads, writes)})

    def tt(o, a, b, f, ext=()):
        op("v", lambda q: q.tensor_tensor(ap(o), ap(a), ap(b), f), [a, b], [o], ext, kind="pair")

    def ts(o, a, s1, f1, s2=None, f2=None):
        if f2 is None:
            op("v", lambda q: q.tensor_scalar(ap(o), ap(a), val(s1), None, f1), [a, s1], [o])
        else:
            op("v", lambda q: q.tensor_scalar(ap(o), ap(a), val(s1), val(s2), f1, f2), [a, s1, s2], [o])

    def cp(o, a):
        op("v", lambda q: q.tensor_copy(ap(o), ap(a)), [a], [o])

    def fill(o, x):
        op("v", lambda q: q.memset(ap(o), x), [], [o])

    def scan(o, d0, d1, init, f0, f1, ext=()):
        op("v", lambda q: q.tensor_tensor_scan(ap(o), ap(d0), ap(d1), init, f0, f1), [d0, d1], [o], ext)

    def horner(o, flags, table, ext=()):
        scan(o, flags, table, 0.0, A.mult, A.add, ext)

    def pick_own(o, src, d, k=K):
        scan(o, src, d, -k, A.max, A.add)

    def columns(o, a):
        ts(o, a, 1.0, A.add, 512.0, A.mult)

    def quant(oq, osc, a):
        op("v", lambda q: q.quantize_mx(ap(oq), ap(osc), ap(a)), [a], [oq, osc], kind="quant")

    def act(o, a, scale=1.0, bias=None, accum=None, f=None):
        kw = {}
        if scale != 1.0:
            kw["scale"] = scale
        if f is None:
            f = F.Copy if bias is None else F.Identity

        def call(q):
            if bias is not None:
                kw["bias"] = val(bias)
            if accum is not None:
                kw["accum_out"] = ap(accum)
            return q.activation(ap(o), ap(a), f, **kw)
        op("a", call, [a, bias], [o, accum])

    def zeros(o):
        act(o, R("zero", 0, len(range(o[1], o[2], o[3]))))

    def mm(o, wq, wsc, xq, xsc, start=True, stop=True, ext=()):
        op("p", lambda q: q.matmul_mx(ap(o), ap(wq), ap(wsc), ap(xq), ap(xsc), start, stop), [wq, wsc, xq, xsc], [o], ext, acc=not start)

    def iota(o, pattern, base, cm=0):
        if SCRATCH[o[0]][2] == I32:
            op("g", lambda q: q.iota(ap(o), pattern, base, cm), [], [o])
        else:
            op("g", lambda q: q.iota(ap(o), pattern, base, cm, allow_small_or_imprecise_dtypes=True), [], [o])

    def const(o, x):
        iota(o, [[0, len(range(o[1], o[2], o[3]))]], x)

    def pair(name, y, x0, x1):
        iota(R(name, y, 24, 4), [[x1 - x0, 2], [0, 3]], x0)

    def sel(o, a, pattern, f, fill_with, base, cm):
        op("g", lambda q: q.affine_select(ap(o), ap(a), pattern, f, fill_with, base, cm), [a], [o])

    def dma(queue, o, a, reads, writes, row=512):
        op(queue, lambda q: q.dma_start(o(), a()), reads, writes, dma=True, kind="local", lat=LOCAL + row / 3.0)

    def send(to, o, a, sem, codes=False):
        rid, pid, _ = topo.addr(to)
        mask = sum(1 << e for e in use[sem])
        kind = "remote" if any(e["sent"] for e in ops) else "first"
        lat = LATE if sem == "uc" else BARS if sem[0] == "f" else REMOTE
        if codes:
            op("g", lambda q: q.remote_dma(ap(o).bitcast(dt.uint8), ap(a).bitcast(dt.uint8), T.sem[sem], T.sem.left, pid, rid, mask), [a], [],
               kind=kind, lat=lat, sent=sem)
        else:
            op("g", lambda q: q.remote_dma(ap(o), ap(a), T.sem[sem], T.sem.left, pid, rid, mask), [a], [], kind=kind, lat=lat, sent=sem)

    def send_tile(r, land):
        rid, pid, _ = topo.addr(nxt)
        sem = "ta%d" % r
        share = len(use[sem]) // 4
        sides = [(T.lq[:, land + 32 * k:land + 32 * k + 32].bitcast(dt.uint8), T.tq[:, 128 * r + 32 * k:128 * r + 32 * k + 32].bitcast(dt.uint8))
                 for k in range(3)] + [(T.ls[:, land:land + 128], T.ts[:, 128 * r:128 * r + 128])]
        parts = [RemoteDMATransfer(dst_ids=[DstId(rid=rid, pnc=pid)], dma_engine_mask=sum(1 << e for e in use[sem][share * k:share * k + share]),
                                   remote_sem=T.sem[sem], src=a, dst=o) for k, (o, a) in enumerate(sides)]
        op("g", lambda q: q.remote_dma_fused(parts, local_sem=T.sem.left), [R("tq", 128 * r, 128 * r + 96), R("ts", 128 * r, 128 * r + 128)], [],
           kind="remote", lat=REMOTE + HOLD["remote"], sent=sem)

    def col(k):
        return R("col", k, k + 1)

    def plane(name, b, a=0, e=C):
        return R(name, C * b + a, C * b + e)

    def entry(name, y, k, n=1):
        return R(name, 12 * k + y, 12 * (k + n), 4)

    def ow(k, n=1):
        return R("ow", 48 * k + 15, 48 * (k + n), 16)

    zw = ["zw0", "zw1", "zw2"]

    dma("a", lambda: T.ub[:], lambda: T.u[:], [], [R("ub", 0, 512)], 1024)
    if PARTS:
        dma("s", lambda: T.zw0[:, 640:4 * C], lambda: T.x[:, 640:4 * C], [], [R("zw0", 640, 4 * C)], 1900)
        dma("s", lambda: T.zw0[:, 0:640], lambda: T.x[:, 0:640], [], [R("zw0", 0, 640)], ROW2)
    else:
        dma("s", lambda: T.zw0[:, 0:4 * C], lambda: T.x[:], [], [R("zw0", 0, 4 * C)], 3300)

    iota(R("pi", 0, 1), [[0, 1]], 0, 1)
    iota(R("upi", 0, 16), [[1, 2], [16, 8]], 0)
    iota(R("r16", 0, 160), [[0, 10], [1, 16]], 0)
    iota(R("og", 0, 128), [[1, 8], [0, 16]], 0)
    fill(R("zero", 0, 512), 0.0)
    fill(R("et", 0, 516), 0.0)
    sel(R("et", 3, 515, 4), R("zero", 0, 128), [[-1, 128]], A.not_equal, 0.5, 0, 1)
    rc = [16 * sum(k >= c for k in SIGNS) - 16 * c * (c in SIGNS) - 32 * (18 - c) - 30 for c in range(18)]
    c = 0
    while c < 18:
        step, e = (0 if c in SIGNS else 32), c + 1
        while e < 18 and (e in SIGNS) == (c in SIGNS):
            e += 1
        iota(R("rc", c, e), [[step, e - c]], rc[c])
        c = e
    iota(R("ij", 0, C), [[1, C]], 0)
    dma("s", lambda: T.wq[:].bitcast(dt.uint8), lambda: T.wc[:], [R("zw0", 0, 1)], [R("wq", 0, 512)])
    dma("s", lambda: T.wsc[:], lambda: T.ws[:], [], [R("wsc", 0, 512)])
    dma("s", lambda: T.vb[:], lambda: T.v[:], [], [R("vb", 0, 512)])
    fill(R("h0", 0, 160), BIG)
    ts(R("pb", 0, 1), R("pi", 0, 1), 15, A.bitwise_and)
    ts(R("pb", 1, 2), R("pi", 0, 1), 4, A.arith_shift_right)
    ts(R("pb", 2, 3), R("pi", 0, 1), 14, A.bitwise_and)
    cp(R("upl", 0, 16), R("upi", 0, 16))
    fill(R("h0", 0, 160, 16), -BIG)
    cp(R("col", 0, 2), R("pb", 0, 2))
    ts(R("upl", 24, 25), R("pb", 2, 3), 8.0, A.mult, 1.0, A.add)
    ts(R("upl", 16, 24), R("upi", 0, 8), 0.125, A.mult)
    tiles, at = [], 0
    for blocks in ([None, 17, 16, 15], [14, 13, 12, 11], [10, 9, 8, 7], [6, 5, 4, 3], [0, 2, 1]):
        w = max(128, 16 * max(c for c in blocks if c is not None) + 16)
        low = 16 * min(c for c in blocks if c is not None) + 16 if len(blocks) == 4 else 0
        tiles.append((at, w, blocks))
        if len(tiles) < 5:
            zeros(R("bt", 4 * (at + low), 4 * (at + w)))
        else:
            fill(R("bt", 4 * (at + low), 4 * (at + w)), 0.0)
        at += w
    ts(R("e16", 0, 160), R("r16", 0, 160), col(0), A.is_equal, 0.5, A.subtract)
    act(R("m16", 0, 160), R("e16", 0, 160), scale=2 * BIG)
    act(col(2), col(0), scale=-K, bias=-3 * K)
    act(R("dk", 0, 160), R("e16", 0, 160), scale=18 * K, bias=8 * K)
    fill(R("lf", 24, 128), 0.0)
    fill(R("tt", 384, 512), 0.0)
    fill(R("rs", 0, 1), 0.0)
    for t in range(4):
        ts(R("ot", t, 512, 4), R("og", 0, 128), col(1), A.is_equal, 1.0 if t else 2.0, A.mult)

    def unpacker(b):
        quant(R("eq", 128 * b, 128 * b + 128), R("es", 128 * b, 128 * b + 128), R("et", 3 - b, 515 - b))

    quant(R("oq", 0, 128), R("osq", 0, 128), R("ot", 0, 512))
    quant(R("uq", 0, 128), R("us", 0, 128), R("ub", 0, 512))

    def pick(oq, osc, q_, sc_, by, ext=()):
        op("v", lambda q: q.tensor_copy(ap(oq).bitcast(dt.uint32), ap(q_).bitcast(dt.uint32).indirect(ap(by))), [q_, by], [oq], ext)
        op("a", lambda q: q.activation(ap(osc), ap((sc_, by)), F.Copy), [sc_, by], [osc], ext)

    def pick_u(k):
        pick(R("upq", 128 * k, 128 * k + 128), R("ups", 128 * k, 128 * k + 128), R("uq", 0, 128), R("us", 0, 128), R("upl", 8 * k, 8 * k + 8))

    stage[0] = HINT
    pick_u(0)
    stage[0] = 0
    u0, u1 = (R("upq", 0, 128), R("ups", 0, 128)), (R("upq", 128, 256), R("ups", 128, 256))

    def slot(n, t, w, low=0):
        return R("bt", 4 * (tiles[n][0] + low) + t, 4 * (tiles[n][0] + w), 4)

    def own_score(c):
        return R("hh", 16 * c + 15, 16 * c + 16)

    where = {c: (n, t) for n in range(5) for t, c in enumerate(tiles[n][2])}

    def compare(c):
        (n, t), scores = where[c], bank(0, 0, 16 * c + 16)
        if t:
            ts(slot(n, t, 16 * c + 16), scores, own_score(c), A.is_ge, 2.0, A.mult)
        else:
            ts(slot(n, t, 16 * c + 16), scores, own_score(c), A.is_ge)

    def row_sum(c):
        n, t = where[c]
        if c not in SHORT:
            act(R("junk", 8 * c * (c - 1), 8 * c * (c + 1)), slot(n, t, 16 * c), scale=1.0 if t else 2.0, accum=R("rs", c, c + 1))

    def short_sum(c):
        row = slot(*where[c], 16 * c)
        op("v", lambda q: q.tensor_reduce(ap(R("rs", c, c + 1)), ap(row), AX.X, A.add), [row], [R("rs", c, c + 1)], kind="sum")

    def pack(n):
        at, w = tiles[n][:2]
        quant(R("bq", at, at + w), R("bs", at, at + w), R("bt", 4 * at, 4 * (at + w)))

    def column_sums(n):
        at, w = tiles[n][:2]
        mm(bank(2, 0, w), R("oq", 0, 128), R("osq", 0, 128), R("bq", at, at + w), R("bs", at, at + w), n == 0, n == 4)

    def signs(blocks, k):
        for c in blocks:
            if TWO:
                act(slot(*where[c], 16 * c + 16, 160), bank(5, 0, 16 * c - 144), scale=-1.0, bias=own_score(c))
                act(slot(*where[c], 160), bank(k, 0, 160), scale=-1.0, bias=own_score(c))
            else:
                act(slot(*where[c], 16 * c + 16), bank(k, 0, 16 * c + 16), scale=-1.0, bias=own_score(c))
        for c in blocks:
            n, t = where[c]
            act(slot(n, t, 16 * c), slot(n, t, 16 * c), scale=-1.0, bias=TINY, accum=R("rs", c, c + 1), f=F.Sign)
            act(slot(n, t, 16 * c + 16, 16 * c), slot(n, t, 16 * c + 16, 16 * c), scale=-1.0, bias=TINY, f=F.Sign)

    for at in (0, 12):
        iota(R("lf", at, at + 12), [[SEG, 3], [0, 2], [20, 2]], 16)
    iota(R("lf", 32, 56), [[1, 4], [37, 2], [SEG, 3]], 16)
    iota(R("lf", 64, 88), [[0, 4], [48, 2], [16, 3]], 15)
    for at in (96, 108):
        iota(R("lf", at, at + 12), [[1, 3], [0, 2], [3, 2]], 0)
    iota(R("bc", 0, 36), [[1, 6], [0, 6]], 2048)
    pick(R("ucq", 0, 16), R("ucs", 0, 16), R("uq", 0, 128), R("us", 0, 128), R("upl", 24, 25))
    send(prv, R("unq", 0, 16), R("ucq", 0, 16), "uc", codes=True)
    send(prv, R("uns", 0, 16), R("ucs", 0, 16), "uc")
    act(R("dk", 15, 160, 16), R("dk", 15, 160, 16), bias=col(2))
    act(R("d16", 0, 160), R("dk", 0, 160))
    act(R("d16", 160, C), R("dk", 0, C - 160))
    act(R("ra", 0, 18), R("rc", 0, 18), bias=R("dk", 15, 16))
    low = C - 128
    stage[0] = 2 * HINT
    quant(R("lq", low, C), R("ls", low, C), R("zw0", 4 * low, 4 * C))
    mm(bank(4, 0, 128), u0[0], u0[1], R("lq", low, C), R("ls", low, C))
    stage[0] = 3 * HINT
    if TWO:
        mm(bank(5, 0, 128), u0[0], u0[1], R("lq", low, C), R("ls", low, C))
    quant(R("lq", 0, low), R("ls", 0, low), R("zw0", 0, 4 * low))
    stage[0] = 4 * HINT
    mm(bank(0), u0[0], u0[1], R("lq", 0, C), R("ls", 0, C))
    if TWO:
        mm(bank(3, 0, low), u0[0], u0[1], R("lq", 0, low), R("ls", 0, low))
    else:
        mm(bank(3), u0[0], u0[1], R("lq", 0, C), R("ls", 0, C))
    stage[0] = 0
    tt(R("mm", low, C), bank(4, 0, 128), R("m16", 0, 128), A.min)
    scan(R("hh", low, C), R("h0", 0, 128), R("mm", low, C), -BIG, A.min, A.max)
    tt(slot(0, 0, C, low), bank(4, 0, 128), R("hh", low, C), A.not_equal)
    signs(SIGNS, 3)
    tt(R("mm", 0, low), bank(0, 0, low), R("m16", 0, low), A.min)
    for c in range(17, -1, -1):
        if c not in SIGNS:
            stage[0] = 5 * HINT * (c == LASTC)
            compare(c)
            stage[0] = 0
            if c:
                row_sum(c)
        if c == 15:
            scan(R("hh", 0, low), R("h0", 0, low), R("mm", 0, low), -BIG, A.min, A.max)
        if c == 14:
            tt(slot(0, 0, low), bank(0, 0, low), R("hh", 0, low), A.not_equal)
        if c in (10, 6, 2):
            pack((10 - c) // 4)
            column_sums((10 - c) // 4)
    for n in (3, 4):
        pack(n)
        column_sums(n)
    stage[0] = 6 * HINT
    pick_u(1)
    stage[0] = 0
    mm(bank(1), u1[0], u1[1], R("lq", 0, C), R("ls", 0, C))
    for c in SHORT:
        short_sum(c)
    act(R("ij", 0, C), R("ij", 0, C), scale=1.0 / 512)
    act(R("d1", 0, 48), R("dk", 0, 48), scale=1.0 / K)
    for b in range(PLANES, 4):
        act(plane("x32", b), R("zw0", b, 1152, 4), scale=32.0)
    act(R("s1", 0, C), bank(1))
    tt(R("d16", 15, C, 16), R("ra", 0, 18), R("rs", 0, 18), A.subtract)
    stage[0] = 6
    fill(R("rd", 0, 3 * SEG), 1.0)
    fill(R("rd", 0, 3 * SEG, SEG), 0.0)
    fill(R("rb", 0, SEG, 0), 0.0)
    for at in (17, 54):
        fill(R("rb", at, at + 3, 0), 1.0 / 2048)
    fill(R("tu", 0, 48), 0.0)
    for b in range(4):
        unpacker(b)
    quant(R("vq", 0, 128), R("vs", 0, 128), R("vb", 0, 512))
    stage[0] = 0
    pick_own(R("cx", 0, C), bank(2), R("d16", 0, C))
    ts(R("plu", 0, 18), R("cx", 15, C, 16), K, A.add, -0.5, A.mult)
    cp((R("orep", 0, C), R("plu", 0, 18)), R("ij", 0, C))
    for k in range(2):
        pick_own(R("ow", 48 * k, 48 * k + 48), R("orep", k, C, 6), R("d1", 0, 48), 1.0)
    pick_own(R("ow", 96, 144), R("orep", 2, C, 6), R("d1", 0, 48), 1.0)
    columns(R("tl", 0, 6), ow(0, 2))
    pick_own(R("ow", 144, 192), R("orep", 3, C, 6), R("d1", 0, 48), 1.0)

    def copy(o, a):
        sel(o, a, [[0, len(range(o[1], o[2], o[3]))]], A.is_ge, 0.0, 0, 0)

    def take(q, r, b, c0=0, c1=6):
        o, a = R("tt", 64 * c0 + b, 64 * c1, 4), (plane("x32", b), R("tl", 6 * r + c0, 6 * r + c1))
        if q == "v":
            ts(o, a, 2.0 ** -5, A.mult)
        else:
            act(o, a, scale=2.0 ** -5)

    def flags(r):
        return R("fl", 48 * r, 48 * r + 24)

    def tables(name, k, part):
        if part == 0:
            tt(entry("t2", 2, k, 2), entry(name, 3, 1, 2), entry(name, 3, 2, 2), A.subtract)
            tt(entry("t2", 1, k), entry(name, 3, 0), entry(name, 3, 1), A.subtract)
        else:
            copy(entry("t2", 3, k, 2), entry(name, 3, 2, 2))
            copy(entry("t2", 0, k + 1), entry("t2", 2, k))

    def targets(r):
        if r == 0:
            tt(R("tg", 0, 32), (R("ow", 0, 96), R("lu", 4, 6)), R("bc", 0, 32), A.add)
        else:
            tt(R("tg", 0, 32), (R("qs", 0, 64), R("lu", 8, 10)), R("bc", 36, 68), A.add)
            ts(R("xl", 0, 24), R("tg", 0, 24), 2048.0, A.mult)
            act(R("xc", 0, 384), (R(zw[r], 0, 1152), R("xl", 0, 24)), scale=0.5)
        last, other = (9, 12) if r else (18, 3)
        act(R("rb", 0, 1, 0), R("tg", 0, 3))
        act(R("rb", 20, 21, 0), R("tg", last, last + 3), scale=-1.0)
        act(R("rb", 37, 38, 0), R("tg", other, other + 3))

    def bars(r):
        scan(R("hb", 0, 96), R("h0", 0, 96), R("bm", 0, 96), -BIG, A.min, A.max)
        copy(R("bo", 8 * r, 8 * r + 6), R("hb", 15, 96, 16))
        send(prv, R("bn", 8 * r, 8 * r + 6), R("bo", 8 * r, 8 * r + 6), "fa%d" % r)

    def refused(r, step):
        if step == 0:
            tt(R("rf", 0, 6), R("hh", 15, 96, 16), R("bn", 8 * r, 8 * r + 6), A.is_lt, (("fa%d" % r, len(use["fa%d" % r])),))
        elif step == 1:
            tt(R("rf", 3, 6), R("rf", 0, 3), R("rf", 3, 6), A.add)
        elif step == 2:
            tt(R("fa", 0, 32), (R("rf", 0, 6), R("lu", 6, 8)), R("tn", 0, 32), A.is_ge)
        elif step == 3:
            horner(R("sq", 0, 24), R("fa", 0, 24), R("tu", 0, 24) if r == 0 else R("t2", 24, 48))
        else:
            columns(R("tl", 6 * r + 6, 6 * r + 12), entry("sq", 3, 0, 2))

    def score_sent(r, step):
        if step == 0:
            mm(bank(2, 0, 128), R("upn", 0, 128), R("usn", 0, 128), R("tq", 128 * r, 128 * r + 128), R("ts", 128 * r, 128 * r + 128))
            tt(R("mm", 0, 96), bank(2, 0, 96), R("m16", 0, 96), A.min)
        else:
            scan(R("hh", 0, 96), R("h0", 0, 96), R("mm", 0, 96), -BIG, A.min, A.max)

    def own_lists(r, k):
        if k == 0:
            horner(R("cs", 12, 36), flags(r), R("tf" if r else "tc", 0, 24))
        elif k == 1:
            horner(R("qs", 0, 24), flags(r), R("t2" if r else "tu", 0, 24))
        elif r == 0:
            horner(R("qs", 48, 72), flags(0), R("tv", 0, 24))
        else:
            horner(R("qs", 48, 60), R("fl", 48, 60), R("t2", 48, 60))

    def hold(r, b):
        act(R("dh", H * b + 48 * r, H * b + 48 * r + 48), bank(4 + b, 80, 128))

    def received(r):
        at = (12, 36, 76)[r]
        horner(R("kw", at, at + 24), flags(r), R("kt", 24 * r, 24 * r + 24))

    def arrivals(k, part):
        at, n = ((0, 5), (96, 3))[k]
        if part == 0:
            tt(R("ne", at, at + 16 * n + 16), (R("kw", 64 * k, 64 * k + 12 * n + 4), R("lu", 16 + 12 * k, 17 + 12 * k + n)),
               R("oh", at, at + 16 * n + 16), A.not_equal)
        else:
            horner(R("so", at, at + 18 * n), R("ne", at, at + 18 * n), R("st", at, at + 18 * n))

    def lists(a, e):
        for at in range(16 * a, 16 * e, 160):
            n = min(160, 16 * e - at)
            pick_own(R("lx", at, at + n), R("lf", at, at + n), R("dk", 0, n))

    def offsets(a, e):
        ts(R("lu", a, e), R("lx", 16 * a + 15, 16 * e, 16), K, A.add)

    for b in range(4):
        take("va"[b // 2], 0, b)
    pick_own(R("ow", 192, 240), R("orep", 4, C, 6), R("d1", 0, 48), 1.0)
    for r in range(3):
        z = zw[r]
        quant(R("tq", 128 * r, 128 * r + 128), R("ts", 128 * r, 128 * r + 128), R("tt", 0, 512))
        own = (C + 128) * r
        land = own + C
        if FUSED:
            send_tile(r, land)
        else:
            send(nxt, R("lq", land, land + 96), R("tq", 128 * r, 128 * r + 96), "ta%d" % r, codes=True)
            send(nxt, R("ls", land, land + 96), R("ts", 128 * r, 128 * r + 96), "ta%d" % r)
        if r == 0:
            window = R("tl", 0, 6)
            act(R("bc", 0, 36), R("bc", 0, 36), scale=1.0 / 2048)
            act(R("xc", 0, 384), R("tt", 0, 384), scale=0.5)
            tt(R("bm", 0, 96), (R("s1", 0, C), window), R("m16", 0, 96), A.min)
            lists(0, 8)
            bars(0)
            offsets(0, 8)
            pick(R("upn", 0, 128), R("usn", 0, 128), R("unq", 0, 16), R("uns", 0, 16), R("upl", 16, 24), (("uc", 2 * len(use["uc"])),))
            targets(0)
            pick_own(R("ow", 240, C), R("orep", 5, C, 6), R("d1", 0, 48), 1.0)
            iota(R("tn", 0, 32), [[0, 8], [-1, 2], [0, 2]], 2)
            score_sent(0, 0)
            tt(entry("tu", 2, 0, 4), ow(1, 4), ow(2, 4), A.subtract)
            score_sent(0, 1)
            tt(entry("tu", 1, 0), ow(0), ow(1), A.subtract)
            tt(entry("tu", 0, 1, 3), ow(1, 3), ow(2, 3), A.subtract)
            tt(entry("tv", 1, 1), ow(2), ow(4), A.subtract)
            fill(R("lf", 128, 256), 3.0)
            iota(R("lf", 128, 152), [[48, 2], [0, 4], [4, 3]], 3)
            iota(R("lf", 160, 184), [[12, 2], [0, 4], [4, 3]], 3)
            iota(R("lf", 192, 216), [[0, 2], [4, 3], [0, 4]], 15)
            iota(R("lf", 224, 248), [[37, 2], [1, 4], [SEG, 3]], 16)
            lists(8, 16)
            offsets(8, 16)
            for at, n in ((256, 5), (448, 3)):
                iota(R("lf", at, at + 24 * n), [[4, 4], [0, 6], [12, n]], 3)
                iota(R("lf", at + 16 * n + 16, at + 40 * n + 16), [[16, 4], [48, 6], [0, n]], 15)
            lists(16, 36)
            offsets(16, 36)
            act(entry("tu", 3, 0, 4), ow(2, 4))
            act(col(5), col(0), scale=2.0)
            act(col(6), col(0), scale=-2.0)
            zeros(R("kw", 0, 104))
            zeros(R("t2", 0, 60))
            for y, (x0, x1) in enumerate(((-1, 48), (1, -48), (0, 0))):
                pair("tc", y, x0, x1)
            const(entry("tc", 3, 0), 1)
            iota(entry("tc", 3, 1), [[16, 3]], 48)
            const(R("cs", 0, 48), 2)
            iota(R("bc", 36, 72), [[0, 3], [1, 4], [0, 3]], 2048)
            iota(R("sb", 0, 18), [[H, 6], [0, 3]], 0)
            const(R("tv", 0, 12, 4), 0)
            for k in range(2):
                copy(entry("tv", 3, k), ow(3 + 2 * k))
                copy(entry("tv", 2, k), entry("tu", 2, 1 + 2 * k))
            copy(entry("tv", 1, 0), entry("tu", 2, 0))
        else:
            window = R("wl", 6 * r - 6, 6 * r)
            for b in range(4):
                if BACK[b] == "v":
                    ts(R(z, b, 1152, 4), plane("x32", b), 2.0 ** -5, A.mult)
                else:
                    act(R(z, b, 1152, 4), plane("x32", b), scale=2.0 ** -5)
            own_lists(r - 1, 1)
            for h in range(2):
                a = own + H * h
                quant(R("lq", a, a + H), R("ls", a, a + H), R(z, 4 * H * h, 4 * H * h + 4 * H))
                mm(bank(h, 0, H), u1[0], u1[1], R("lq", a, a + H), R("ls", a, a + H))
                act(R("s1", H * h, H * h + H), bank(h, 0, H))
            own_lists(r - 1, 2)
            columns(window, entry("qs", 3, 0, 2))
            own_lists(r - 1, 0)
            targets(r)
            tt(R("bm", 0, 96), (R("s1", 0, C), window), R("m16", 0, 96), A.min)
            if r < 2:
                score_sent(r, 0)
                bars(r)
                score_sent(r, 1)
            ts(R("rd", 37, 3 * SEG, SEG), entry("cs", 3, 1), 1.0, A.is_le)
            ts(R("gs", 0, 6, 2), entry("cs", 3, 1), 2.0, A.not_equal, -2 * BIG, A.mult)
            tt(R("mh", 0, 48), (R("gs", 0, 6), R("upl", 16, 19)), R("m16", 0, 48), A.add)
            tt(R("bh", 0, 48), (R("s1", 0, C), R("wl", 6 * r - 6, 6 * r - 3)), R("mh", 0, 48), A.min)
            tt(R("sf", 0, 16), (R("cs", 24, 48), R("lu", 10, 11)), R("sb", 0, 16), A.add)
            if r == 1:
                horner(R("qs", 24, 48), flags(0), R("tu", 24, 48))
                horner(R("sq", 24, 48), R("fa", 0, 24), R("tu", 24, 48))
            else:
                received(0)
                received(1)
            if SECOND[-1][0] == 3:
                cp(R("sl", 0, 9), R("sf", 0, 9))
                cp(R("sl", 10, 13), R("sf", 9, 12))
            else:
                cp(R("sl", 0, 12), R("sf", 0, 12))
        if r == 1:
            tables("sq", 2, 0)
            tables("sq", 2, 1)
            tables("qs", 0, 0)
            tt(R("tp", 0, 32), (R("cs", 0, 24), R("lu", 12, 14)), R("tm", 0, 32), A.mult)
            for k in range(2):
                tt(entry("t2", 2 - k, 4), entry("qs", 3, 2 + 2 * k), entry("qs", 3, 5 - 3 * k), A.subtract)
            tt(R("tf", 0, 24), R("tp", 0, 24), R("ta", 0, 24), A.add)
        if r == 2:
            act(R("st", 0, 90, 5), R("st", 0, 90, 5), bias=col(6))
            act(R("st", 98, 150, 3), R("st", 98, 150, 3), bias=col(5))
            arrivals(0, 0)
            arrivals(0, 1)
        arrived = (("ta%d" % r, (1 if FUSED else 2) * coming),)
        tq, tsc = R("lq", land - 32, land + 96), R("ls", land - 32, land + 96)
        mm(bank(3, 0, 128), u1[0], u1[1], tq, tsc, ext=arrived)
        for b in range(4):
            mm(bank(4 + b, 0, 128), R("eq", 128 * b, 128 * b + 128), R("es", 128 * b, 128 * b + 128), tq, tsc, ext=arrived)

        def fresh(b):
            n = 48 if r else 96
            tt(R("val", n * b, n * b + n), bank(4 + b, 32, 32 + n), R("xc", n * b, n * b + n) if r else R("xc", b, 384, 4), A.add)

        for i in range(2):
            tt(R("rb", 1 + 20 * i, 17 + 20 * i, 0), bank(3, 32 + 48 * i, 80 + 48 * i), R("bm", 48 * i, 48 * i + 48), A.is_lt)
        if r:
            tt(R("rb", 38, 54, 0), bank(3, 32, 80), R("bh", 0, 48), A.is_lt)
        for c in range(3):
            horner(R("ro", SEG * c, SEG * c + SEG), R("rd", SEG * c, SEG * c + SEG), R("rb", 0, SEG, c + 1))
        ts(R("zl", 0, 32), (R("ro", 0, 3 * SEG), R("lu", 14, 16) if r else R("lu", 2, 4)), 2048.0, A.mult)
        tt(R("fl", 48 * r, 48 * r + 32), (R("ro", 0, 3 * SEG), R("lu", 0, 2)), R("tn", 0, 32), A.is_ge)
        for step in (BLEND if r else "f0 f1 f2 f3").split():
            k = int(step[1])
            if step[0] == "f":
                fresh(k)
            elif step[0] == "h":
                hold(r, k)
            else:
                cp(R("dh", H * k + 48 * r, H * k + 48 * r + 48), bank(4 + k, 80, 128))
        if r:
            for a, e in SECOND:
                tt(R("val", 192 + 48 * a, 192 + 48 * e), (R("dh", 0, H * e), R("sl", 3 * a + a % 2, 3 * e + a % 2)), R("xc", 192 + 48 * a, 192 + 48 * e), A.add)
        if r == 0:
            refused(0, 0)
        cp((R(z, 0, 5248), R("zl", 0, 24)), R("val", 0, 384))
        if r == 0:
            for b in range(4):
                hold(0, b)
            act(R("bc", 36, 72), R("bc", 36, 72), scale=1.0 / 2048)
            act(entry("tc", 3, 1), entry("tc", 3, 1), bias=col(0))
            act(entry("ta", 3, 1), entry("tc", 3, 1), bias=96.0)
            act(entry("tv", 0, 1), entry("tu", 2, 1), scale=-1.0)
            for y, (m0, m1) in enumerate(((1, -48), (0, -48), (-3, 48), (3, -48))):
                pair("tm", y, m0, m1)
            const(R("tm", 24, 32), 0)
            for y, (a0, a1) in enumerate(((-2, 96), (1, 0), (3, -48))):
                pair("ta", y, a0, a1)
            const(entry("ta", 3, 0), -2)
        if r == 1:
            iota(R("kt", 0, 72, 2), [[0, 3], [8, 2], [0, 6]], 0)
            iota(R("kt", 1, 72, 4), [[0, 3], [-16, 2], [0, 3]], 8)
            copy(entry("kt", 3, 0, 2), ow(0, 2))
        if r:
            copy(entry("kt", 3, 2 * r, 2), entry("qs", 3, 0, 2))
        if r == 1:
            tables("qs", 0, 1)
            copy(entry("t2", 3, 4), entry("qs", 3, 5))
            act(R("oh", 0, 96), (R("ow", 0, C), R("lu", 22, 28)))
            act(R("oh", 96, 160), (R("ow", 0, C), R("lu", 32, 36)))
            const(R("oh", 0, 90, 5), 0)
            const(R("oh", 96, 150, 3), 0)
            const(R("st", 0, 150), -1)
            for y in (2, 4):
                const(R("st", y, 90, 5), -95)
            iota(R("st", 0, 90, 5), [[-32, 3], [0, 6]], -1)
            iota(R("st", 98, 150, 3), [[32, 3], [0, 6]], 193)
        if r == 2:
            copy(R("st", 96, 150, 3), R("so", 4, 90, 5))
        half = ((0, H), (H, C)) if r < 2 else ((0, CUT), (CUT, C))

        def product(b, h):
            a, e = half[h]
            mm(bank(4 - 4 * h + b, 0, e - a), R("wq", 128 * b, 128 * b + 128), R("wsc", 128 * b, 128 * b + 128), R("zq", a, e), R("zs", a, e))

        def add(b, h):
            a, e = half[h]
            tt(plane("x32", b, a, e), bank(4 - 4 * h + b, 0, e - a), plane("z32", b, a, e), A.add)

        def scaled(q, o, a, x):
            if q == "v":
                ts(o, a, x, A.mult)
            else:
                act(o, a, scale=x)

        if r == 2:
            for step in LAST.split():
                kind, h, b = step[:2], int(step[2:3] or 0), int(step[3:4] or 0)
                a, e = half[h] if h < 2 else (0, C)
                if kind == "qz":
                    quant(R("zq", a, e), R("zs", a, e), R(z, 4 * a, 4 * e))
                    for k in range(4):
                        product(k, h)
                elif kind == "rc":
                    received(2)
                elif kind == "ne":
                    arrivals(1, 0)
                elif kind == "so":
                    arrivals(1, 1)
                    copy(R("skb", 0, 18), R("so", 98, 150, 3))
                    for c in range(3):
                        dma("s", lambda c=c: T.sk[:, 96 * c:96 * c + 96], lambda c=c: T.skb[:, 6 * c:6 * c + 6], [R("skb", 0, 18)], [], SKROW)
                elif kind == "ad":
                    add(b, h)
                elif kind == "qx":
                    quant(R("fq", a, e), R("fs", a, e), R("xf", 4 * a, 4 * e))
                    mm(bank(4 - 4 * h, 0, e - a), R("vq", 0, 128), R("vs", 0, 128), R("fq", a, e), R("fs", a, e))
                    a = 0 if WHOLE else a
                    if h or not WHOLE:
                        dma("s", lambda a=a, e=e: T.oc[:, 4 * a:4 * e], lambda a=a, e=e: T.fq[:, a:e].bitcast(dt.uint8), [R("fq", a, e)], [], 4 * (e - a))
                elif kind[1] == "z":
                    scaled(kind[0], plane("z32", b, a, e), R(z, 4 * a + b, 4 * e, 4), 32.0)
                elif kind[1] == "x":
                    scaled(kind[0], R("xf", 4 * a + b, 4 * e, 4), plane("x32", b, a, e), 2.0 ** -5)
                else:
                    scaled(kind[0], R("yb", a, e), bank(4 - 4 * h, 0, e - a), 1.0)
                    a = 0 if WHOLE else a
                    if h or not WHOLE:
                        dma("a", lambda a=a, e=e: T.y[:, a:e], lambda a=a, e=e: T.yb[:, a:e], [R("yb", a, e)], [], 4 * (e - a))
            break
        for step in range(1 - r, 5):
            refused(r, step)
        for a, e in ((0, CUTS[0]), (CUTS[0], C)):
            quant(R("zq", a, e), R("zs", a, e), R(z, 4 * a, 4 * e))
        for b in range(4):
            scaled("v" if b in ZV else "a", plane("z32", b), R(z, b, 1152, 4), 32.0)
            half = ((0, CUTS[b]), (CUTS[b], C)) if CUTS[b] else ((0, C),)
            for h in range(len(half)):
                product(b, h)
                add(b, h)
            if b < 3:
                take("a", r + 1, b)
        if SPLIT < 6:
            take("v", r + 1, 3, SPLIT, 6)
        if SPLIT:
            take("a", r + 1, 3, 0, SPLIT)

    for k in range(4):
        dma(STORES[k], lambda k=k: T.osc[4 * k:4 * k + 4, :], lambda k=k: T.fs[32 * k:32 * k + 4, :], [R("fs", 0, C)], [])

    emit(g, T, ops, near)
    g.wait_ge(T.sem.left, sum(len(e) * (1 if name[0] == "f" or FUSED and name[0] == "t" else 2) for name, e in use.items()))
